import numpy as np, ml_dtypes
CORES = [23,119,17,113]
N = 4
import mx_ref
BF = ml_dtypes.bfloat16
def gcols(t, e):
    v = np.concatenate([t.reshape(8, 16, -1, 4), np.zeros((8, 16, 1, 4), BF)], axis=2)
    return np.ascontiguousarray(np.stack([v[g][:, e[g]] for g in range(8)])).reshape(128, -1)
def tile(rs):
    return np.stack(rs, axis=2).reshape(128, -1).astype(BF)
def cut(t, i, w=512):
    return t[:, w * i:w * i + w]
def pick(q, e):
    c = np.concatenate([q[0].reshape(128, -1, 4), np.zeros((128, 1, 4), np.uint8)], axis=1); s = np.concatenate([q[1], np.ones((16, 1), np.uint8)], axis=1)
    return (np.ascontiguousarray(c[:, e].reshape(128, -1)), np.ascontiguousarray(s[:, e]))
def join(*qs):
    return (np.concatenate([q[0] for q in qs], axis=1), np.concatenate([q[1] for q in qs], axis=1))
def put(q, e, v):
    c, s = q[0].reshape(128, -1, 4).copy(), q[1].copy(); c[:, e] = v[0].reshape(128, -1, 4); s[:, e] = v[1]
    return (c.reshape(128, -1), s)
def pk(c, s):
    return (np.ascontiguousarray(c), mx_ref.live(s))
def emit(q):
    return q[0], q[1]
def packed(v, rng):
    q = [mx_ref.quantize(np.ascontiguousarray(v[r])) for r in range(N)]
    return np.stack([a for a, b in q]), np.stack([mx_ref.plane(b, rng) for a, b in q])
def values_of_codes():
    e, c = np.zeros((128, 128, 4), np.float32), np.zeros((128, 2, 4), np.uint8)
    e[np.arange(128), np.arange(128), 0] = 1
    c[:127, :, 0] = np.arange(256).reshape(2, 128).T[:127]
    return mx_ref.matmul(mx_ref.quantize(e.reshape(128, 512).astype(BF)), (c.reshape(128, 8), np.full((16, 2), 127, np.uint8))).T.reshape(-1).astype(np.float64)
CODE_VALUE, SCALE_VALUE = values_of_codes(), 2.0 ** (np.arange(256) - 127.0)
def decode(q):
    return (CODE_VALUE[q[0]].reshape(16, 8, -1, 4) * SCALE_VALUE[q[1]][:, None, :, None] + 0.0).reshape(128, -1).astype(np.float32)
def f(rng, *shape):
    return mx_ref.flush((rng.standard_normal(shape, dtype=np.float32) * np.exp2(rng.integers(-2, 3, shape[:-1] + (1,)))).astype(BF))
def wide(rng, *shape, cols=0):
    v = rng.standard_normal(shape, dtype=np.float32) * np.exp2(rng.integers(-12, 13, shape)).astype(np.float32)
    if cols: v *= np.repeat(np.exp2(rng.integers(-cols, cols + 1, shape[:-2] + (1, shape[-1] // 4))) * (rng.random(shape[:-2] + (1, shape[-1] // 4)) > 0.0625), 4, axis=-1).astype(np.float32)
    return mx_ref.flush(v.astype(BF))
C, K, R = 192, 64, 3
STEP = [1, 2, 1]
PAIRS = np.array([(i, j) for i in range(K) for j in range(K) if (i + 1) * (j + 1) <= K])
PI, PJ = PAIRS[:, 0], PAIRS[:, 1]
def partner(r, t):
    return r ^ STEP[t]
def best(s, n):
    return np.argsort(-s, axis=1, kind="stable")[:, :n]
def big(v):
    v = v.astype(np.float32)
    v[np.abs(v) < np.float32(2.0 ** -16)] = 0
    return v.astype(BF)
def numbers_of(rng):
    return {"x": big(f(rng, N, 128, 4 * C)), "u": np.array(f(rng, N, 128, 512)), "v": np.array(f(rng, N, 128, 512))}
def weights(rng, w):
    c, p = packed(w, rng)
    return {"wc": c, "ws": p}
def signs(rng):
    return np.stack([rng.permutation(8) % 2 * 2.0 - 1.0 for r in range(N)])
def half(rng):
    return (np.arange(N) >> int(rng.integers(1, N.bit_length() - 1))) & 1 == int(rng.integers(2))
def setup_inputs(rng):
    return {**numbers_of(rng), **weights(rng, big(f(rng, N, 128, 2048)))}
def setup_inputs_ties(rng):
    d = numbers_of(rng)
    e = rng.permutation(N)
    x = d["x"].reshape(N, 8, 16, C, 4)
    for r in range(N):
        k = np.zeros(C, int) if r == e[0] else rng.permutation(C) % 3
        a = x[r][:, :8, :3].copy()
        a[:, :, 2] = 0
        x[r][:, :8] = a[:, :, k]
    x[e[1]] = 0
    u = d["u"].reshape(N, 8, 16, 128, 4)
    u[:, :, 8:, ::16] = 0
    w = big(f(rng, N, 128, 2048)).reshape(N, 8, 16, 4, 8, 16, 4)
    w[:, :, 8:, :, :, :8] = 0
    return {"x": x.reshape(N, 128, 4 * C), "u": u.reshape(N, 128, 512), "v": d["v"], **weights(rng, w.reshape(N, 128, 2048))}
def setup_inputs_near(rng):
    d = numbers_of(rng)
    x = d["x"].astype(np.float32).reshape(N, 8, 16, C, 4)
    a, low = signs(rng), half(rng)
    m = low[:, None] & (a < 0)
    s = np.arange(C) // 2
    s = np.where(m[:, :, None], C // 2 - 1 - s, s)
    g = ((s[:, :, :, None] >> np.arange(8)) & 1) * np.exp2(np.arange(8) - 23.0) * np.where(m, -1.0, 1.0)[:, :, None, None] + 0.0
    x[:, :, 0] = 0
    x[:, :, 0, :, 0] = np.where(low[:, None], 0.0, a)[:, :, None]
    x[:, :, 8] = g[:, :, :, :4]
    x[:, :, 9] = g[:, :, :, 4:]
    x[:, :, 10:] = rng.integers(4, 8, (N, 8, 6, C, 4)) * rng.choice([-1.0, 1.0], (N, 8, 6, C, 4)) * 2.0 ** -20
    x[low, :, 8:] *= np.float32(2.0 ** -4)
    u = d["u"].reshape(N, 128, 128, 4)
    k = np.where(low, 2.0 ** -30, 1.0).astype(np.float32).astype(BF)
    u[:, :, ::16] = 0
    for h in range(0, 128, 16):
        u[:, h, h, 0] = k
        u[:, h + 8:h + 10, h] = k[:, None, None]
    w = big(f(rng, N, 128, 2048)).reshape(N, 128, 4, 8, 16, 4)
    w[:, :, :, :, 0] = 0
    w[:, :, :, :, 8:] = 0
    return {"x": x.reshape(N, 128, 4 * C).astype(BF), "u": u.reshape(N, 128, 512), "v": d["v"], **weights(rng, w.reshape(N, 128, 2048))}
def setup_inputs_huge(rng):
    d = numbers_of(rng)
    x = 2.0 ** 30 * (0.9 + 0.1 * rng.random((N, 128, C, 4)))
    c = np.stack([np.where(rng.permutation(C) % 4 == 0, 1.0, -1.0) for r in range(N)])
    c[half(rng)] = 1
    x *= c[:, None, :, None]
    u = d["u"].reshape(N, 128, 128, 4)
    a = 2.0 ** 30 * (0.9 + 0.1 * rng.random((N, 128, 8, 4))) * signs(rng)[np.arange(N) // 2][:, None, :, None]
    u[:, :, ::16] = a.astype(np.float32).astype(BF)
    w = np.zeros((N, 128, 4, 128, 4), np.float32)
    i = np.arange(128)
    for b in range(4): w[:, i, b, i, b] = -4
    return {"x": x.astype(np.float32).reshape(N, 128, 4 * C).astype(BF), "u": u.reshape(N, 128, 512), "v": d["v"], **weights(rng, w.reshape(N, 128, 2048).astype(BF))}
def setup_inputs_steep(rng):
    d = numbers_of(rng)
    x = d["x"].astype(np.float32).reshape(N, 8, 16, C, 4)
    k = np.argsort(rng.random((N, 8, C)), axis=2)
    x[:, :, 0] = 0
    x[:, :, 0, :, 0] = k // 16 * 16
    x[:, :, 0, :, 1] = k % 16
    x[:, :, 0, :, 2] = 256
    flat = np.arange(N) % 2 == int(rng.integers(2))
    x[flat, :, :8] *= np.float32(2.0 ** -10)
    for r in range(N):
        for g in rng.permutation(8)[:4]: x[r, g, 0, int(rng.integers(C)), 0] = 2.0 ** 30
    u = d["u"].reshape(N, 128, 128, 4)
    u[:, :, ::16] = 0
    for h in range(0, 128, 16): u[:, h, h, :2] = 1
    w = big(f(rng, N, 128, 2048))
    w[:, ::16] = 0
    return {"x": x.reshape(N, 128, 4 * C).astype(BF), "u": u.reshape(N, 128, 512), "v": d["v"], **weights(rng, w)}
def setup_inputs_spread(rng):
    d = setup_inputs(rng)
    d["x"] = big(wide(rng, N, 128, 4 * C, cols=6))
    return d
def check_inputs(d):
    b = []
    for k in ("x", "u", "v"):
        a = np.abs(d[k].astype(np.float32))
        if not (np.isfinite(a).all() and ((a == 0) | (a >= 2.0 ** -30) & (a <= 2.0 ** 30)).all()): b.append("a value of " + k)
    return b
def reference(x, u, v, wc, ws):
    qu = [mx_ref.quantize(u[r]) for r in range(N)]
    lay = [pk(wc[r], ws[r]) for r in range(N)]
    now = [x[r] for r in range(N)]
    taken = [None] * N
    for t in range(R):
        first, score, sent = [], [], []
        for r in range(N):
            s = mx_ref.matmul(qu[r], mx_ref.quantize(now[r]))[::16] + np.float32(0.0)
            o = best(s, K)
            first.append(o)
            score.append(np.take_along_axis(s, o, axis=1))
            sent.append(mx_ref.quantize(gcols(now[r], o)))
        came = decode(join(*sent)).astype(BF)
        for r in range(N):
            e = partner(r, t)
            n = best(score[r][:, PI] + score[e][:, PJ], C)
            taken[r] = n
            one = gcols(now[r], np.take_along_axis(first[r], PI[n], axis=1))
            two = gcols(cut(came, e, 4 * K), PJ[n])
            z = ((one.astype(np.float32) + two.astype(np.float32)) * np.float32(0.5)).astype(BF)
            q, zf = mx_ref.quantize(z), z.astype(np.float32)
            now[r] = tile([np.maximum(mx_ref.matmul(pick(lay[r], np.arange(128 * b, 128 * b + 128)), q), np.float32(0.0)) * np.float32(0.03125) + zf[:, b::4] for b in range(4)])
    y, ol = np.zeros((N, 128, C), np.float32), np.zeros((N, 8, C), np.float32)
    oc, osc = np.zeros((N, 128, 4 * C), np.uint8), np.zeros((N, 16, C), np.uint8)
    for r in range(N):
        q = mx_ref.quantize(now[r])
        y[r] = mx_ref.matmul(mx_ref.quantize(v[r]), q)
        ol[r] = taken[r]
        oc[r], osc[r] = emit(q)
    return {"y": y, "ol": ol, "oc": oc, "osc": osc}

@@ -1,0 +1,416 @@
+from concourse.bass import DstId, RemoteDMATransfer
+from concourse.mybir import dt, AluOpType, ActivationFunctionType
+
+C, K, ROUNDS = 192, 64, 3
+STEP = [1, 2, 1]
+LENS = [K // (i + 1) for i in range(K)]
+NP = 288
+FILL0, FILL1 = 248, 256
+LOW = -9.0e29
+DROP = float(2 ** 19)
+
+FROM1 = [16 * k for k in range(12)]
+SUM1 = [16 * k + 16 for k in range(12)]
+BASE1 = [0, 64, 64]
+FROM2 = [64] * 4 + [96] * 2 + [112] + [16 * k for k in range(7, 16)]
+SUM2 = FROM2[:7] + [16 * k + 16 for k in range(7, 16)]
+BASE2 = [64, 64, 64, 160]
+ON_SCALAR1 = [0]
+ON_SCALAR2 = [0, 1]
+TILES1 = {4: [0], 8: [1], 11: [2]}
+TILES2 = {8: [1], 9: [0], 12: [2], 15: [3]}
+
+Q4, U8, BF, F32, I32, U16 = "float8_e4m3fn_x4", "uint8", "bfloat16", "float32", "int32", "uint16"
+SCRATCH = {}
+
+
+def _sb(name, n, kind):
+    SCRATCH[name] = ("sbuf", [128, n], kind)
+
+
+def _mx(name, n):
+    _sb(name + "q", n, Q4)
+    _sb(name + "s", n, U8)
+
+
+MOFF1 = [0, 4 * 192, 4 * 320]
+MOFF2 = [0, 4 * 224, 4 * 448, 4 * 672]
+for _n, _w, _k in [
+        ("xb", 4 * C, BF), ("ub", 512, BF), ("vb", 512, BF),
+        ("pbit", 8, I32), ("pcol", 8, F32), ("crow", NP, F32), ("cm16", NP, BF), ("dcol", 8, F32),
+        ("m16", NP, BF), ("nm16", NP, BF), ("d16", NP, BF), ("d4", C, BF), ("ocol", 8, F32),
+        ("orow", C, F32), ("nrow", NP, F32), ("val0", NP, F32), ("valr", NP, F32),
+        ("lrep", 16, U16), ("lrp", 16, U16), ("lcmp", 16, U16), ("lpi", 32, U16), ("lpj", 32, U16),
+        ("tint", 48, I32), ("tand", 48, I32), ("gidx", 128, BF), ("gtile", 512, BF), ("etile", 520, BF),
+        ("sc", C, F32), ("sp", C, F32), ("sm", NP, F32), ("hold", NP, F32), ("eq", C, BF), ("cor", C, BF),
+        ("ma", 4 * 448, BF), ("mb", 4 * 800, BF), ("junk", 16 * 224, BF), ("sg", 4 * 224, BF), ("hh", NP, F32),
+        ("acc", 32, F32), ("bas", 32, F32), ("pre", 32, F32), ("cnt", 32, F32), ("rkp", 32, U16),
+        ("ss", C + 8, F32), ("so", C, F32), ("es", C, F32), ("spi", NP, F32), ("vv", NP, F32), ("xs", NP, F32),
+        ("h4", C, F32), ("offa", 48, U16), ("offe", 48, U16), ("nout", NP, F32), ("ysb", C, F32),
+        ("eg", 4 * C, BF), ("rr", 4 * C, F32)]:
+    _sb(_n, _w, _k)
+for _n, _w in [("u", 128), ("urep", 128), ("ucmp", 32), ("lu0", 32), ("lu1", 32), ("urp0", 128), ("urp1", 128),
+               ("v", 128), ("w", 512), ("e", 512), ("g", 128), ("ma", 448), ("mb", 800)]:
+    _mx("c" + _n, _w)
+for _t in range(ROUNDS + 1):
+    _mx("ct%d" % _t, C)
+_mx("cz", C)
+for _n, _w, _k in [("zz", 4 * C, BF), ("dd", 4 * C, BF), ("aa", 4 * K, BF), ("ee", 4 * K, BF), ("tt", 4 * C, BF)]:
+    _sb(_n, _w, _k)
+for _t in range(ROUNDS):
+    _mx("cl%d" % _t, C)
+    for _n, _w, _k in [("rk", 16, U16), ("lrk", 16, U16), ("ol", 16, U16), ("lol", 16, U16)]:
+        _sb("%s%d" % (_n, _t), _w, _k)
+for _n in ["pa", "pb", "pp", "py", "pw0", "pw1", "pw2", "pw3"]:
+    SCRATCH[_n] = ("psum", [128, 512], F32)
+
+SEMAPHORES = (["vec", "act", "pe", "pool", "sent", "ldx", "ldu", "ldw", "ldv", "stored", "gotu0", "gotu1"]
+              + ["%s%d" % (n, t) for n in ("gott", "gotr", "goto") for t in range(ROUNDS)])
+
+
+def rank_program(g, core, T, topo):
+    rank = T.rank_of(core)
+    if rank is None:
+        return
+    A, F = AluOpType, ActivationFunctionType
+    V, S, P, Y = g.vector, g.scalar, g.tensor, g.sync
+    queue = {"vec": V, "act": S, "pe": P, "pool": g, "sync": Y}
+    count = {}
+    seen = {q: {} for q in queue}
+
+    def need(q, *toks):
+        for sem, val in toks:
+            if seen[q].get(sem, 0) < val:
+                queue[q].wait_ge(T.sem[sem], val)
+                seen[q][sem] = val
+
+    def done(sem, inst, n=1):
+        inst.then_inc(T.sem[sem], n)
+        count[sem] = count.get(sem, 0) + n
+        return (sem, count[sem])
+
+    def vts(out, in0, s1, s2, op0, op1=None, after=()):
+        need("vec", *after)
+        if op1 is None:
+            return done("vec", V.tensor_scalar(out, in0, s1, None, op0))
+        return done("vec", V.tensor_scalar(out, in0, s1, s2, op0, op1))
+
+    def vtt(out, in0, in1, op, after=()):
+        need("vec", *after)
+        return done("vec", V.tensor_tensor(out, in0, in1, op))
+
+    def vcp(out, in_, after=()):
+        need("vec", *after)
+        return done("vec", V.tensor_copy(out, in_))
+
+    def vset(out, value, after=()):
+        need("vec", *after)
+        return done("vec", V.memset(out, value))
+
+    def vsum(out, d0, d1, after=()):
+        need("vec", *after)
+        return done("vec", V.tensor_tensor_scan(out, d0, d1, 0.0, A.mult, A.add))
+
+    def vhold(out, d0, d1, after=()):
+        need("vec", *after)
+        return done("vec", V.tensor_tensor_scan(out, d0, d1, 0.0, A.add, A.min))
+
+    def vq(name, a, n, in_, after=()):
+        need("vec", *after)
+        return done("vec", V.quantize_mx(T[name + "q"][:, a:a + n], T[name + "s"][:, a:a + n], in_))
+
+    def act(out, in_, func, after=(), **kw):
+        need("act", *after)
+        return done("act", S.activation(out, in_, func, **kw))
+
+    def mm(out, lhs, a, rhs, b, n, after=(), start=True, stop=True):
+        need("pe", *after)
+        return done("pe", P.matmul_mx(T[out][:, 0:n], T[lhs + "q"][:, a:a + 128], T[lhs + "s"][:, a:a + 128],
+                                      T[rhs + "q"][:, b:b + n], T[rhs + "s"][:, b:b + n], start, stop))
+
+    def iota(out, pattern, base, cm):
+        return done("pool", g.iota(out, pattern, base, cm, allow_small_or_imprecise_dtypes=True))
+
+    def pick_codes(dst, src, n, m, off, after=()):
+        return vcp(T[dst + "q"][:, 0:n].bitcast(dt.uint32), T[src + "q"][:, 0:m].bitcast(dt.uint32).indirect(off), after)
+
+    def pick_scales(dst, src, n, m, off, after=()):
+        return act(T[dst + "s"][:, 0:n], T[src + "s"][:, 0:m].indirect(off), F.Copy, after)
+
+    def fill(buf, a, n, value, after=()):
+        return [act(buf[:, b:min(b + NP, a + n)], T.cm16[:, 0:min(b + NP, a + n) - b], F.Identity, after, scale=0.0, bias=value)
+                for b in range(a, a + n, NP)]
+
+    peer = [T.cores[rank ^ s] for s in STEP]
+    kind = [0, 1, 0]
+    nen = [len(topo.engines(core, c)) for c in peer]
+    nin = [len(topo.engines(c, core)) for c in peer]
+
+    def send(out, in_, sem, t, after):
+        need("pool", *after)
+        rid, pid = topo.addr(peer[t])[0:2]
+        g.remote_dma(out, in_, T.sem[sem], T.sem["sent"], pid, rid, topo.mask(core, peer[t]))
+        count["sent"] = count.get("sent", 0) + nen[t]
+
+    def send_u(h, after):
+        need("pool", *after)
+        rid, pid = topo.addr(peer[h])[0:2]
+        eng = topo.engines(core, peer[h])
+        half = len(eng) // 2
+        g.remote_dma_fused(
+            [RemoteDMATransfer(dst_ids=[DstId(rid=rid, pnc=pid)], dma_engine_mask=sum(1 << x for x in e),
+                               remote_sem=T.sem["gotu%d" % h], src=src, dst=dst)
+             for src, dst, e in ((T.cucmpq[:, 0:8].bitcast(dt.uint8), T["clu%dq" % h][:, 0:8].bitcast(dt.uint8), eng[:half]),
+                                 (T.cucmps[:], T["clu%ds" % h][:], eng[half:]))], local_sem=T.sem["sent"])
+        count["sent"] = count.get("sent", 0) + len(eng)
+        return ("gotu%d" % h, nin[h])
+
+    ldx = done("ldx", Y.dma_start(T.xb[:], T.x[:]), 16)
+    ldu = done("ldu", S.dma_start(T.ub[:], T.u[:]), 16)
+
+    k_p = done("pool", g.iota(T.pbit[:, 3:4], [[0, 1]], 0, 1))
+    k_cm16 = iota(T.cm16[:], [[0, NP // 16], [1, 16]], 0, 0)
+    k_crow = iota(T.crow[:], [[1, NP]], 0, 0)
+    k_gi = iota(T.gidx[:], [[16, 8], [0, 16]], 0, 0)
+    place, singles, i = 0, [], 0
+    k_val = []
+    while i < K:
+        n = 1
+        while i + n < K and LENS[i + n] == LENS[i]:
+            n += 1
+        if place == FILL0:
+            place = FILL1
+        if n == 1:
+            singles.append((i, place))
+        else:
+            k_val.append(iota(T.val0[:, place:place + n * LENS[i]], [[4, n], [4096, LENS[i]]], 4 * i, 0))
+        place += n * LENS[i]
+        i += n
+
+    z1 = [vset(T.ma[:, MOFF1[n]:MOFF1[n] + 4 * (FROM1[4 * n + 3] - BASE1[n])], 0.0) for n in range(3)]
+    k_et0 = fill(T.etile, 0, 520, 0.0, [k_cm16])
+    z2 = []
+    for n in range(1, 4):
+        z2 += fill(T.mb, MOFF2[n], 4 * (FROM2[4 * n + 3] - BASE2[n]), 0.0)
+    pint = T.pbit[:, 3:4]
+    bits = [vts(T.pbit[:, 0:1], pint, 15, None, A.bitwise_and, after=[k_p]),
+            vts(T.pbit[:, 1:2], pint, 3, None, A.bitwise_and),
+            vts(T.pbit[:, 2:3], pint, 2, 3, A.logical_shift_right, A.bitwise_and)]
+    k_col = vcp(T.pcol[:, 0:4], T.pbit[:, 0:4], bits)
+    qcol, rcol, ccol, ncol = [T.pcol[:, n:n + 1] for n in range(4)]
+    lrep, lrp, lcmp = T.lrep[:, 0:8], T.lrp[:, 0:8], T.lcmp[:, 0:2]
+    k_m16 = vts(T.m16[:], T.cm16[:], qcol, None, A.is_equal, after=[k_col, k_cm16])
+    k_nm16 = vts(T.nm16[:], T.cm16[:], qcol, None, A.not_equal)
+    k_lcmp = vts(lcmp, T.pcol[:, 0:2], 7.0, 16.0, A.min, A.mult)
+    k_lrep = vts(lrep, T.cm16[:, 0:8], 16.0, None, A.mult)
+    k_lrp = vcp(lrp, T.cm16[:, 0:8])
+    k_dc = vts(T.dcol[:, 0:4], T.cm16[:, 0:4], ccol, 5 * DROP, A.is_equal, A.mult)
+    k_et = vts(T.etile[:, 3:512:4], T.crow[:, 0:128], ncol, None, A.is_equal, after=k_et0 + [k_crow])
+    qe = [vq("ce", 128 * b, 128, T.etile[:, 3 - b:515 - b], [k_et]) for b in range(4)]
+
+    qu = vq("cu", 0, 128, T.ub[:], [ldu])
+    uc_c = pick_codes("cucmp", "cu", 32, 128, lcmp, [qu, k_lcmp])
+    uc_s = pick_scales("cucmp", "cu", 32, 128, lcmp, [qu, k_lcmp])
+    qt = vq("ct0", 0, C, T.xb[:], [ldx])
+    ur_c = pick_codes("curep", "cu", 128, 128, lrep, [k_lrep])
+    ur_s = pick_scales("curep", "cu", 128, 128, lrep, [k_lrep])
+    gotu = [send_u(kind[0], [uc_c, uc_s])]
+
+    def compare(row, n, own, frm, summ, base, moff, mt, a0, scalar_blocks, ready, tile_done, extra):
+        def slot(k, a, b):
+            o = moff[k // 4] + k % 4 - 4 * base[k // 4]
+            return mt[:, o + 4 * a:o + 4 * b - 3:4]
+        wrote = {}
+        sums = []
+        turn = [job for k in sorted(extra) for job in extra[k]]
+        sign = [act(T.sg[:, 224 * j:224 * j + n - frm[k]], row[:, frm[k]:n], F.Sign, ready, scale=-1.0, bias=own(k))
+                for j, k in enumerate(scalar_blocks)]
+        for j, k in enumerate(scalar_blocks):
+            d = summ[k] - frm[k]
+            if d:
+                act(slot(k, frm[k], summ[k]), T.sg[:, 224 * j:224 * j + d], F.Relu, [sign[j]], scale=-1.0)
+            wrote[k] = act(slot(k, summ[k], n), T.sg[:, 224 * j + d:224 * j + n - frm[k]], F.Relu, [sign[j]], scale=-1.0,
+                           accum_out=T.acc[:, a0 + k:a0 + k + 1])
+            sums.append(wrote[k])
+        for k in range(len(frm)):
+            if k not in wrote:
+                wrote[k] = vts(slot(k, frm[k], n), row[:, frm[k]:n], own(k), None, A.is_gt, after=ready)
+                if summ[k] < n:
+                    sums.append(act(T.junk[:, 224 * k:224 * k + n - summ[k]], slot(k, summ[k], n), F.Identity, [wrote[k]],
+                                    accum_out=T.acc[:, a0 + k:a0 + k + 1]))
+            for job in extra.get(k, ()):
+                tile_done(job, [wrote[j] for j in range(4 * job, 4 * job + 4)], turn)
+        return sums[-1]
+
+    state = T.xb
+    keep = {}
+    for t in range(ROUNDS):
+        R = lambda n: T["%s%d" % (n, t)]
+        ct, cl = "ct%d" % t, "cl%d" % t
+        send(T[cl + "q"][:].bitcast(dt.uint8), T[ct + "q"][:].bitcast(dt.uint8), "gott%d" % t, t, [qt])
+        send(T[cl + "s"][:], T[ct + "s"][:], "gott%d" % t, t, [qt])
+        gott = ("gott%d" % t, 2 * nin[t])
+        if t == 0:
+            gotu.append(send_u(kind[1], []))
+
+        sa = mm("pa", "curep", 0, ct, 0, C, [qt, ur_c, ur_s])
+        sb = mm("pb", "curep", 0, ct, 0, C)
+        if t == 0:
+            k_gt = [vts(T.gtile[:, b:512:4], T.gidx[:], qcol, ncol, A.add, A.is_equal, after=[k_gi]) for b in range(4)]
+            k_o16 = act(T.ocol[:, 0:1], qcol, F.Identity, [k_col], scale=DROP, bias=-15 * DROP)
+            k_acc = fill(T.acc, 0, 32, 0.0)
+            k_d16 = act(T.d16[:], T.nm16[:], F.Identity, [k_nm16], scale=-17 * DROP, bias=16 * DROP)
+            k_b1 = act(T.bas[:, 0:12], T.crow[:, 16:193:16], F.Identity, [k_o16, k_crow], bias=T.ocol[:, 0:1])
+        cp = act(T.sc[:], T.pb[:, 0:C], F.Copy, [sb])
+        a0 = vtt(T.sm[:, 0:C], T.pa[:, 0:C], T.m16[:, 0:C], A.mult, [sa, k_m16])
+        if t == 0:
+            qg = vq("cg", 0, 128, T.gtile[:], k_gt)
+        a1 = vsum(T.hold[:, 0:C], T.nm16[:, 0:C], T.sm[:, 0:C], [a0])
+        got = {}
+
+        def tile1(n, toks, turn):
+            w = C - BASE1[n]
+            if n == turn[-1]:
+                got["eq"] = vtt(T.eq[:], T.pa[:, 0:C], T.hold[:, 0:C], A.is_equal)
+            q = vq("cma", MOFF1[n] // 4, w, T.ma[:, MOFF1[n]:MOFF1[n] + 4 * w], toks + z1)
+            got["y"] = mm("pp", "cg", 0, "cma", MOFF1[n] // 4 + 64 - BASE1[n], 128, [q, qg], n == turn[0], n == turn[-1])
+            if n == 0:
+                got["x"] = mm("py", "cg", 0, "cma", 0, 128, [q])
+
+        sums = compare(T.sc, C, lambda k: T.hold[:, 16 * k + 15:16 * k + 16], FROM1, SUM1, BASE1, MOFF1, T.ma, 0,
+                       ON_SCALAR1, [a1, cp] + k_acc + z1, tile1, TILES1)
+        a3 = vsum(T.cor[:], T.nm16[:, 0:C], T.eq[:], [got["eq"]])
+        a4 = vhold(T.hh[:, 0:64], T.d16[:, 0:64], T.py[:, 0:64], [got["x"], k_d16])
+        a5 = vtt(T.pre[:, 0:12], T.bas[:, 0:12], T.cor[:, 15:C:16], A.subtract, [a3, k_b1])
+        a6 = vhold(T.hh[:, 64:C], T.d16[:, 0:128], T.pp[:, 0:128], [got["y"]])
+        a7 = vtt(T.cnt[:, 0:12], T.pre[:, 0:12], T.acc[:, 0:12], A.add, [a5, sums])
+        a8 = vtt(T.cnt[:, 0:12], T.cnt[:, 0:12], T.hh[:, 15:C:16], A.subtract, [a4, a6, a7])
+        a9 = vcp(R("rk")[:, 0:12], T.cnt[:, 0:12], [a8])
+        send(R("lrk")[:, 0:12], R("rk")[:, 0:12], "gotr%d" % t, t, [a9])
+        gotr = ("gotr%d" % t, nin[t])
+
+        h = kind[t]
+
+        def scores():
+            pp = mm("pp", "curp%d" % h, 0, cl, 0, C, [gott, a6, keep["c%d" % h], keep["s%d" % h]])
+            return act(T.sp[:], T.pp[:, 0:C], F.Copy, [pp])
+
+        if t == 0:
+            k_val += [act(T.val0[:, place:place + LENS[i]], T.crow[:, 0:LENS[i]], F.Identity, scale=4096.0, bias=4.0 * i)
+                      for i, place in singles]
+            k_val += fill(T.val0, FILL0, FILL1 - FILL0, 4.0 * C)
+            k_orow = act(T.orow[:], T.crow[:, 0:C], F.Identity, scale=4.0, bias=rcol)
+            k_dd = act(T.dcol[:, 4:8], T.dcol[:, 0:4], F.Identity, [k_dc], bias=-DROP)
+            k_low = fill(T.ss, C, 8, LOW)
+            k_o4 = act(T.ocol[:, 1:2], ccol, F.Identity, scale=-DROP, bias=3 * DROP)
+            k_d4 = [act(T.d4[:, b:C:4], T.crow[:, 0:C // 4], F.Identity, [k_dd], scale=0.0, bias=T.dcol[:, 4 + b:5 + b])
+                    for b in range(4)]
+        else:
+            c5 = scores()
+        c1 = vcp(T.ss[:, 0:C].indirect(R("rk")[:, 0:12]), T.sc[:], [a9])
+        if t == 0:
+            t1 = vhold(T.hold[:], T.d16[:], T.val0[:], k_val)
+            t2 = vts(T.tint[:, 0:18], T.hold[:, 15:NP:16], T.ocol[:, 0:1], None, A.subtract, after=[t1])
+            k_lpj = vts(T.lpj[:, 0:18], T.hold[:, 15:NP:16], T.ocol[:, 0:1], 1.0 / 4096.0, A.subtract, A.mult)
+            t3 = vts(T.tand[:, 0:18], T.tint[:, 0:18], 2, 1023, A.logical_shift_right, A.bitwise_and, after=[t2])
+            k_lpi = vcp(T.lpi[:, 0:18], T.tand[:, 0:18], [t3])
+        c4 = act(T.spi[:], T.ss[:, 0:C + 8].indirect(T.lpi[:, 0:18]), F.Copy, [c1, k_lpi] + k_low)
+        c0 = vcp(T.so[:, 0:C].indirect(R("rk")[:, 0:12]), T.orow[:], [k_orow])
+        if t == 0:
+            keep["s0"] = pick_scales("curp0", "clu0", 128, 8, lrp, [gotu[0], k_lrp])
+            keep["c0"] = pick_codes("curp0", "clu0", 128, 8, lrp, [gotu[0], k_lrp])
+            c5 = scores()
+        c2 = vhold(T.h4[:, 0:K], T.d4[:, 0:K], T.so[:, 0:K], [c0] + k_d4)
+        c3 = vts(R("ol")[:, 0:16], T.h4[:, 3:K:4], T.ocol[:, 1:2], None, A.add, after=[c2, k_o4])
+        send(R("lol")[:, 0:16], R("ol")[:, 0:16], "goto%d" % t, t, [c3])
+        goto = ("goto%d" % t, nin[t])
+        pd = [mm("pw%d" % b, "ce", 128 * b, cl, 0, C, qe) for b in range(4)]
+        c6 = act(T.aa[:], state[:, 0:4 * C].indirect(R("ol")[:, 0:16]), F.Copy, [c3], scale=0.5)
+        c7 = [act(T.dd[:, b:4 * C:4], T["pw%d" % b][:, 0:C], F.Copy, [pd[b]], scale=0.5) for b in range(4)]
+        if t == 0:
+            need("sync", gotr)
+            done("ldw", Y.dma_start(T.cwq[:].bitcast(dt.uint8), T.wc[:]), 16)
+            ldw = done("ldw", Y.dma_start(T.cws[:], T.ws[:]), 16)
+            ldv = done("ldv", Y.dma_start(T.vb[:], T.v[:]), 16)
+            k_c3 = act(T.ocol[:, 3:4], qcol, F.Identity, bias=T.ocol[:, 0:1])
+            k_c2 = act(T.ocol[:, 2:3], rcol, F.Identity, scale=1025.0)
+            k_pre = [act(T.pre[:, 12:16], T.crow[:, 0:64:16], F.Identity, bias=qcol),
+                     act(T.bas[:, 12:21], T.crow[:, 128:257:16], F.Identity, bias=T.ocol[:, 0:1]),
+                     act(T.pre[:, 16:30], T.crow[:, 64:NP:16], F.Identity, [k_c3], bias=T.ocol[:, 3:4])]
+
+        d0 = vcp(T.es[:, 0:C].indirect(R("lrk")[:, 0:12]), T.sp[:], [gotr, c5])
+        d1 = vtt(T.vv[:], T.es[:, 0:C].indirect(T.lpj[:, 0:18]), T.spi[:], A.add, [d0, c4, k_lpj])
+        d2 = vtt(T.sm[:, 0:FILL1], T.vv[:, 0:FILL1], T.m16[:, 0:FILL1], A.mult, [d1])
+        d3 = vsum(T.hold[:, 0:FILL1], T.nm16[:, 0:FILL1], T.sm[:, 0:FILL1], [d2])
+        lo, hi = 16 * 7, 16 * 16
+
+        def tile2(n, toks, turn):
+            skip = 0 if t == 0 or n == 3 else FROM2[4 * n] - BASE2[n]
+            w = NP - BASE2[n] - skip
+            o = MOFF2[n] + 4 * skip
+            if n == 3:
+                got["eq"] = vtt(T.eq[:, 0:hi - lo], T.vv[:, lo:hi], T.hold[:, lo:hi], A.is_equal)
+            q = vq("cmb", o // 4, w, T.mb[:, o:o + 4 * w], toks + z2)
+            got["y"] = mm("pb", "cg", 0, "cmb", MOFF2[n] // 4 + 160 - BASE2[n], 128, [q], n == turn[0], n == turn[-1])
+            if n < 3:
+                got["x"] = mm("pa", "cg", 0, "cmb", MOFF2[n] // 4, 128, [q], n == turn[0], n == turn[-2])
+
+        sums = compare(T.vv, NP, lambda k: T.hold[:, 16 * k + 15:16 * k + 16], FROM2, SUM2, BASE2, MOFF2, T.mb, 12,
+                       ON_SCALAR2, [d3] + z2, tile2, TILES2)
+        d5 = vsum(T.cor[:, 0:hi - lo], T.nm16[:, lo:hi], T.eq[:, 0:hi - lo], [got["eq"]])
+        d6 = vhold(T.hh[:, 64:192], T.d16[:, 0:128], T.pa[:, 0:128], [got["x"]])
+        d7 = vtt(T.pre[:, 19:28], T.bas[:, 12:21], T.cor[:, 15:hi - lo:16], A.subtract, [d5] + k_pre)
+        d8 = vhold(T.hh[:, 192:NP], T.d16[:, 0:96], T.pb[:, 32:128], [got["y"]])
+        d9 = vtt(T.cnt[:, 12:30], T.pre[:, 12:30], T.acc[:, 12:30], A.add, [d7, sums])
+        d10 = vtt(T.cnt[:, 16:30], T.cnt[:, 16:30], T.hh[:, 79:NP:16], A.subtract, [d6, d8, d9])
+        if t == 0:
+            k_valr = act(T.valr[:], T.val0[:], F.Identity, [k_c2], bias=T.ocol[:, 2:3])
+        d11 = vcp(T.rkp[:, 0:18], T.cnt[:, 12:30], [d10])
+        e0 = act(T.ee[:], T.dd[:, 0:4 * C].indirect(R("lol")[:, 0:16]), F.Copy, [goto, c7[-1]])
+        if t == 0:
+            keep["s1"] = pick_scales("curp1", "clu1", 128, 8, lrp, [gotu[1]])
+        if t == ROUNDS - 1:
+            act(T.nrow[:, 0:FILL1], T.crow[:, 0:FILL1], F.Copy)
+            k_nrow = act(T.nrow[:, FILL1:NP], T.crow[:, FILL0:NP - 8], F.Copy)
+
+        e1 = vcp(T.xs[:, 0:NP].indirect(T.rkp[:, 0:18]), T.valr[:], [d11, k_valr])
+        e2 = vhold(T.h4[:], T.d4[:], T.xs[:, 0:C], [e1])
+        e4 = vts(T.tint[:], T.h4[:, 3:C:4], T.ocol[:, 1:2], None, A.add, after=[e2])
+        e3 = vts(T.offe[:], T.h4[:, 3:C:4], T.ocol[:, 1:2], 1.0 / 1024.0, A.add, A.mult)
+        e5 = vts(T.tand[:], T.tint[:], 1023, None, A.bitwise_and, after=[e4])
+        e6 = vcp(T.offa[:], T.tand[:], [e5])
+        zs = []
+        for a, b in ((0, 8), (8, 20), (20, 34), (34, 48)):
+            f0 = act(T.eg[:, 16 * a:16 * b], T.ee[:, 0:4 * K].indirect(T.offe[:, a:b]), F.Copy, [e3, e0])
+            zs.append(vtt(T.zz[:, 16 * a:16 * b], T.aa[:, 0:4 * K].indirect(T.offa[:, a:b]), T.eg[:, 16 * a:16 * b], A.add,
+                          [e6, f0, c6]))
+        qz = vq("cz", 0, C, T.zz[:], zs)
+
+        pw = [mm("pw%d" % b, "cw", 128 * b, "cz", 0, C, [qz, ldw]) for b in range(4)]
+        if t == 0:
+            keep["c1"] = pick_codes("curp1", "clu1", 128, 8, lrp, [gotu[1]])
+        if t == 1:
+            qv = vq("cv", 0, 128, T.vb[:], [ldv])
+        if t == ROUNDS - 1:
+            n0 = vcp(T.nout[:, 0:NP].indirect(T.rkp[:, 0:18]), T.nrow[:], [k_nrow])
+            need("sync", n0)
+            done("stored", Y.dma_start(T.ol[:], T.nout[0:128:16, 0:C]), 16)
+        ts = []
+        for b in range(4):
+            r0 = act(T.rr[:, C * b:C * b + C], T["pw%d" % b][:, 0:C], F.Relu, [pw[b]], scale=0.03125)
+            ts.append(vtt(T.tt[:, b:4 * C:4], T.rr[:, C * b:C * b + C], T.zz[:, b:4 * C:4], A.add, [r0]))
+        state = T.tt
+        qt = vq("ct%d" % (t + 1), 0, C, state[:], ts)
+
+    ct = "ct%d" % ROUNDS
+    py = mm("py", "cv", 0, ct, 0, C, [qt, qv])
+    need("sync", qt)
+    done("stored", Y.dma_start(T.oc[:], T[ct + "q"][:].bitcast(dt.uint8)), 16)
+    need("act", qt)
+    for k in range(4):
+        done("stored", S.dma_start(T.osc[4 * k:4 * k + 4, :], T[ct + "s"][32 * k:32 * k + 4, 0:C]), 16)
+    yc = vcp(T.ysb[:], T.py[:, 0:C], [py])
+    need("sync", yc)
+    done("stored", Y.dma_start(T.y[:], T.ysb[:]), 16)
+    need("pool", ("sent", count["sent"]), ("pool", count["pool"]))
+    need("sync", ("act", count["act"]), ("pe", count["pe"]), ("stored", count["stored"]))

@@ -54,7 +54,7 @@ for _n, _w in [("u", 128), ("urep", 128), ("ucmp", 32), ("lu0", 32), ("lu1", 32)
     _mx("c" + _n, _w)
 for _t in range(ROUNDS + 1):
     _mx("ct%d" % _t, C)
-_mx("cz", C)
+_mx("cz", 256)
 for _n, _w, _k in [("zz", 4 * C, BF), ("dd", 4 * C, BF), ("aa", 4 * K, BF), ("ee", 4 * K, BF), ("tt", 4 * C, BF)]:
     _sb(_n, _w, _k)
 for _t in range(ROUNDS):
@@ -216,7 +216,7 @@ def rank_program(g, core, T, topo):
     ur_s = pick_scales("curep", "cu", 128, 128, lrep, [k_lrep])
     gotu = [send_u(kind[0], [uc_c, uc_s])]
 
-    def compare(row, n, own, frm, summ, base, moff, mt, a0, scalar_blocks, ready, tile_done, extra):
+    def compare(row, n, own, frm, summ, base, moff, mt, a0, scalar_blocks, ready, between, tile_done, extra):
         def slot(k, a, b):
             o = moff[k // 4] + k % 4 - 4 * base[k // 4]
             return mt[:, o + 4 * a:o + 4 * b - 3:4]
@@ -234,13 +234,19 @@ def rank_program(g, core, T, topo):
             sums.append(wrote[k])
         for k in range(len(frm)):
             if k not in wrote:
-                wrote[k] = vts(slot(k, frm[k], n), row[:, frm[k]:n], own(k), None, A.is_gt, after=ready)
+                wrote[k] = vts(slot(k, frm[k], n), row[:, frm[k]:n], own(k), None, A.is_gt, after=ready + between(k))
                 if summ[k] < n:
                     sums.append(act(T.junk[:, 224 * k:224 * k + n - summ[k]], slot(k, summ[k], n), F.Identity, [wrote[k]],
                                     accum_out=T.acc[:, a0 + k:a0 + k + 1]))
             for job in extra.get(k, ()):
                 tile_done(job, [wrote[j] for j in range(4 * job, 4 * job + 4)], turn)
         return sums[-1]
+
+    def first_scores(ct, after):
+        return mm("pw0", "curep", 0, ct, 0, 128, after), mm("pw1", "curep", 0, ct, 0, 128)
+
+    def first_mask(early):
+        return vtt(T.sm[:, 0:128], T.pw0[:, 0:128], T.m16[:, 0:128], A.mult, [early[0], k_m16])
 
     state = T.xb
     keep = {}
@@ -253,32 +259,43 @@ def rank_program(g, core, T, topo):
         if t == 0:
             gotu.append(send_u(kind[1], []))
 
-        sa = mm("pa", "curep", 0, ct, 0, C, [qt, ur_c, ur_s])
-        sb = mm("pb", "curep", 0, ct, 0, C)
+        if t == 0:
+            early = first_scores(ct, [qt, ur_c, ur_s])
+        sb2 = mm("pw3", "curep", 0, ct, 64, 128, [qt])
+        sb = mm("pw2", "curep", 0, ct, 64, 128)
         if t == 0:
             k_gt = [vts(T.gtile[:, b:512:4], T.gidx[:], qcol, ncol, A.add, A.is_equal, after=[k_gi]) for b in range(4)]
             k_o16 = act(T.ocol[:, 0:1], qcol, F.Identity, [k_col], scale=DROP, bias=-15 * DROP)
             k_acc = fill(T.acc, 0, 32, 0.0)
             k_d16 = act(T.d16[:], T.nm16[:], F.Identity, [k_nm16], scale=-17 * DROP, bias=16 * DROP)
-            k_b1 = act(T.bas[:, 0:12], T.crow[:, 16:193:16], F.Identity, [k_o16, k_crow], bias=T.ocol[:, 0:1])
-        cp = act(T.sc[:], T.pb[:, 0:C], F.Copy, [sb])
-        a0 = vtt(T.sm[:, 0:C], T.pa[:, 0:C], T.m16[:, 0:C], A.mult, [sa, k_m16])
-        if t == 0:
+            act(T.sc[:, 0:128], T.pw1[:, 0:128], F.Copy, [early[1]])
+            a0 = first_mask(early)
             qg = vq("cg", 0, 128, T.gtile[:], k_gt)
-        a1 = vsum(T.hold[:, 0:C], T.nm16[:, 0:C], T.sm[:, 0:C], [a0])
+        cp = act(T.sc[:, 128:C], T.pw3[:, 64:128], F.Copy, [sb2])
+        a1 = vsum(T.hold[:, 0:128], T.nm16[:, 0:128], T.sm[:, 0:128], [a0])
+        vtt(T.eq[:, 0:128], T.pw0[:, 0:128], T.hold[:, 0:128], A.is_equal, [a1])
         got = {}
+
+        def between1(k):
+            if k == 2:
+                got["m"] = vtt(T.sm[:, 128:C], T.pw2[:, 64:128], T.m16[:, 128:C], A.mult, [sb])
+            if k == 3:
+                got["h"] = vsum(T.hold[:, 128:C], T.nm16[:, 128:C], T.sm[:, 128:C], [got["m"]])
+            return [got["h"]] if k >= 8 else []
 
         def tile1(n, toks, turn):
             w = C - BASE1[n]
             if n == turn[-1]:
-                got["eq"] = vtt(T.eq[:], T.pa[:, 0:C], T.hold[:, 0:C], A.is_equal)
+                got["eq"] = vtt(T.eq[:, 128:C], T.pw2[:, 64:128], T.hold[:, 128:C], A.is_equal)
             q = vq("cma", MOFF1[n] // 4, w, T.ma[:, MOFF1[n]:MOFF1[n] + 4 * w], toks + z1)
             got["y"] = mm("pp", "cg", 0, "cma", MOFF1[n] // 4 + 64 - BASE1[n], 128, [q, qg], n == turn[0], n == turn[-1])
             if n == 0:
                 got["x"] = mm("py", "cg", 0, "cma", 0, 128, [q])
 
         sums = compare(T.sc, C, lambda k: T.hold[:, 16 * k + 15:16 * k + 16], FROM1, SUM1, BASE1, MOFF1, T.ma, 0,
-                       ON_SCALAR1, [a1, cp] + k_acc + z1, tile1, TILES1)
+                       ON_SCALAR1, [a1, cp] + k_acc + z1, between1, tile1, TILES1)
+        if t == 0:
+            k_b1 = act(T.bas[:, 0:12], T.crow[:, 16:193:16], F.Identity, [k_o16, k_crow], bias=T.ocol[:, 0:1])
         a3 = vsum(T.cor[:], T.nm16[:, 0:C], T.eq[:], [got["eq"]])
         a4 = vhold(T.hh[:, 0:64], T.d16[:, 0:64], T.py[:, 0:64], [got["x"], k_d16])
         a5 = vtt(T.pre[:, 0:12], T.bas[:, 0:12], T.cor[:, 15:C:16], A.subtract, [a3, k_b1])
@@ -299,6 +316,7 @@ def rank_program(g, core, T, topo):
             k_val += [act(T.val0[:, place:place + LENS[i]], T.crow[:, 0:LENS[i]], F.Identity, scale=4096.0, bias=4.0 * i)
                       for i, place in singles]
             k_val += fill(T.val0, FILL0, FILL1 - FILL0, 4.0 * C)
+            keep["s0"] = pick_scales("curp0", "clu0", 128, 8, lrp, [gotu[0], k_lrp])
             k_orow = act(T.orow[:], T.crow[:, 0:C], F.Identity, scale=4.0, bias=rcol)
             k_dd = act(T.dcol[:, 4:8], T.dcol[:, 0:4], F.Identity, [k_dc], bias=-DROP)
             k_low = fill(T.ss, C, 8, LOW)
@@ -309,6 +327,8 @@ def rank_program(g, core, T, topo):
             c5 = scores()
         c1 = vcp(T.ss[:, 0:C].indirect(R("rk")[:, 0:12]), T.sc[:], [a9])
         if t == 0:
+            keep["c0"] = pick_codes("curp0", "clu0", 128, 8, lrp, [gotu[0], k_lrp])
+            c5 = scores()
             t1 = vhold(T.hold[:], T.d16[:], T.val0[:], k_val)
             t2 = vts(T.tint[:, 0:18], T.hold[:, 15:NP:16], T.ocol[:, 0:1], None, A.subtract, after=[t1])
             k_lpj = vts(T.lpj[:, 0:18], T.hold[:, 15:NP:16], T.ocol[:, 0:1], 1.0 / 4096.0, A.subtract, A.mult)
@@ -317,9 +337,9 @@ def rank_program(g, core, T, topo):
         c4 = act(T.spi[:], T.ss[:, 0:C + 8].indirect(T.lpi[:, 0:18]), F.Copy, [c1, k_lpi] + k_low)
         c0 = vcp(T.so[:, 0:C].indirect(R("rk")[:, 0:12]), T.orow[:], [k_orow])
         if t == 0:
-            keep["s0"] = pick_scales("curp0", "clu0", 128, 8, lrp, [gotu[0], k_lrp])
-            keep["c0"] = pick_codes("curp0", "clu0", 128, 8, lrp, [gotu[0], k_lrp])
-            c5 = scores()
+            keep["c1"] = pick_codes("curp1", "clu1", 128, 8, lrp, [gotu[1]])
+        if t == 1:
+            qv = vq("cv", 0, 128, T.vb[:], [ldv])
         c2 = vhold(T.h4[:, 0:K], T.d4[:, 0:K], T.so[:, 0:K], [c0] + k_d4)
         c3 = vts(R("ol")[:, 0:16], T.h4[:, 3:K:4], T.ocol[:, 1:2], None, A.add, after=[c2, k_o4])
         send(R("lol")[:, 0:16], R("ol")[:, 0:16], "goto%d" % t, t, [c3])
@@ -339,9 +359,10 @@ def rank_program(g, core, T, topo):
                      act(T.pre[:, 16:30], T.crow[:, 64:NP:16], F.Identity, [k_c3], bias=T.ocol[:, 3:4])]
 
         d0 = vcp(T.es[:, 0:C].indirect(R("lrk")[:, 0:12]), T.sp[:], [gotr, c5])
-        d1 = vtt(T.vv[:], T.es[:, 0:C].indirect(T.lpj[:, 0:18]), T.spi[:], A.add, [d0, c4, k_lpj])
-        d2 = vtt(T.sm[:, 0:FILL1], T.vv[:, 0:FILL1], T.m16[:, 0:FILL1], A.mult, [d1])
-        d3 = vsum(T.hold[:, 0:FILL1], T.nm16[:, 0:FILL1], T.sm[:, 0:FILL1], [d2])
+        d1 = [vtt(T.vv[:, 16 * a:16 * b], T.es[:, 0:C].indirect(T.lpj[:, a:b]), T.spi[:, 16 * a:16 * b], A.add, [d0, c4, k_lpj])
+              for a, b in ((0, 8), (8, 18))]
+        d2 = [vtt(T.sm[:, a:a + 128], T.vv[:, a:a + 128], T.m16[:, a:a + 128], A.mult, [d1[a // 128]]) for a in (0, 128)]
+        d3 = [vsum(T.hold[:, a:a + 128], T.nm16[:, a:a + 128], T.sm[:, a:a + 128], [d2[a // 128]]) for a in (0, 128)]
         lo, hi = 16 * 7, 16 * 16
 
         def tile2(n, toks, turn):
@@ -356,7 +377,7 @@ def rank_program(g, core, T, topo):
                 got["x"] = mm("pa", "cg", 0, "cmb", MOFF2[n] // 4, 128, [q], n == turn[0], n == turn[-2])
 
         sums = compare(T.vv, NP, lambda k: T.hold[:, 16 * k + 15:16 * k + 16], FROM2, SUM2, BASE2, MOFF2, T.mb, 12,
-                       ON_SCALAR2, [d3] + z2, tile2, TILES2)
+                       ON_SCALAR2, [d3[0], d1[1]] + z2, lambda k: [d3[1]] if k >= 8 else [], tile2, TILES2)
         d5 = vsum(T.cor[:, 0:hi - lo], T.nm16[:, lo:hi], T.eq[:, 0:hi - lo], [got["eq"]])
         d6 = vhold(T.hh[:, 64:192], T.d16[:, 0:128], T.pa[:, 0:128], [got["x"]])
         d7 = vtt(T.pre[:, 19:28], T.bas[:, 12:21], T.cor[:, 15:hi - lo:16], A.subtract, [d5] + k_pre)
@@ -380,37 +401,46 @@ def rank_program(g, core, T, topo):
         e5 = vts(T.tand[:], T.tint[:], 1023, None, A.bitwise_and, after=[e4])
         e6 = vcp(T.offa[:], T.tand[:], [e5])
         zs = []
-        for a, b in ((0, 8), (8, 20), (20, 34), (34, 48)):
+        for a, b in ((0, 8), (8, 20), (20, 32), (32, 48)):
             f0 = act(T.eg[:, 16 * a:16 * b], T.ee[:, 0:4 * K].indirect(T.offe[:, a:b]), F.Copy, [e3, e0])
             zs.append(vtt(T.zz[:, 16 * a:16 * b], T.aa[:, 0:4 * K].indirect(T.offa[:, a:b]), T.eg[:, 16 * a:16 * b], A.add,
                           [e6, f0, c6]))
-        qz = vq("cz", 0, C, T.zz[:], zs)
+            if b == 32:
+                qz = vq("cz", 0, 128, T.zz[:, 0:512], zs)
+                pw = [mm("pw%d" % n, "cw", 128 * n, "cz", 0, 128, [qz, ldw]) for n in range(4)]
 
-        pw = [mm("pw%d" % b, "cw", 128 * b, "cz", 0, C, [qz, ldw]) for b in range(4)]
-        if t == 0:
-            keep["c1"] = pick_codes("curp1", "clu1", 128, 8, lrp, [gotu[1]])
-        if t == 1:
-            qv = vq("cv", 0, 128, T.vb[:], [ldv])
-        if t == ROUNDS - 1:
-            n0 = vcp(T.nout[:, 0:NP].indirect(T.rkp[:, 0:18]), T.nrow[:], [k_nrow])
-            need("sync", n0)
-            done("stored", Y.dma_start(T.ol[:], T.nout[0:128:16, 0:C]), 16)
+        qz = vq("cz", 128, 128, T.zz[:, 256:768], zs)
+        banks = ["pa", "pb", "pp", "py"]
+        pw += [mm(banks[n], "cw", 128 * n, "cz", 128, 128, [qz]) for n in range(4)]
+        nxt = "ct%d" % (t + 1)
         ts = []
         for b in range(4):
-            r0 = act(T.rr[:, C * b:C * b + C], T["pw%d" % b][:, 0:C], F.Relu, [pw[b]], scale=0.03125)
-            ts.append(vtt(T.tt[:, b:4 * C:4], T.rr[:, C * b:C * b + C], T.zz[:, b:4 * C:4], A.add, [r0]))
+            r0 = act(T.rr[:, C * b:C * b + 128], T["pw%d" % b][:, 0:128], F.Relu, [pw[b]], scale=0.03125)
+            ts.append(vtt(T.tt[:, b:512:4], T.rr[:, C * b:C * b + 128], T.zz[:, b:512:4], A.add, [r0]))
+        for b in range(4):
+            r0 = act(T.rr[:, C * b + 128:C * b + C], T[banks[b]][:, 64:128], F.Relu, [pw[4 + b]], scale=0.03125)
+            ts.append(vtt(T.tt[:, 512 + b:768:4], T.rr[:, C * b + 128:C * b + C], T.zz[:, 512 + b:768:4], A.add, [r0]))
+            if b == 0 and t < ROUNDS - 1:
+                early = first_scores(nxt, [vq(nxt, 0, 128, T.tt[:, 0:512], ts[:4])])
         state = T.tt
-        qt = vq("ct%d" % (t + 1), 0, C, state[:], ts)
+        if t < ROUNDS - 1:
+            act(T.sc[:, 0:128], T.pw1[:, 0:128], F.Copy, [early[1]])
+            a0 = first_mask(early)
+            qt = vq(nxt, 64, 128, T.tt[:, 256:768], ts + [early[1]])
+        else:
+            qt = vq(nxt, 0, C, T.tt[:], ts)
 
     ct = "ct%d" % ROUNDS
-    py = mm("py", "cv", 0, ct, 0, C, [qt, qv])
+    py = mm("pw0", "cv", 0, ct, 0, C, [qt, qv])
+    n0 = vcp(T.nout[:, 0:NP].indirect(T.rkp[:, 0:18]), T.nrow[:], [k_nrow])
     need("sync", qt)
     done("stored", Y.dma_start(T.oc[:], T[ct + "q"][:].bitcast(dt.uint8)), 16)
-    need("act", qt)
     for k in range(4):
-        done("stored", S.dma_start(T.osc[4 * k:4 * k + 4, :], T[ct + "s"][32 * k:32 * k + 4, 0:C]), 16)
-    yc = vcp(T.ysb[:], T.py[:, 0:C], [py])
-    need("sync", yc)
-    done("stored", Y.dma_start(T.y[:], T.ysb[:]), 16)
+        done("stored", Y.dma_start(T.osc[4 * k:4 * k + 4, :], T[ct + "s"][32 * k:32 * k + 4, 0:C]), 16)
+    yc = act(T.ysb[:], T.pw0[:, 0:C], F.Copy, [py])
+    need("act", yc)
+    done("stored", S.dma_start(T.y[:], T.ysb[:]), 16)
+    need("sync", n0)
+    done("stored", Y.dma_start(T.ol[:], T.nout[0:128:16, 0:C]), 16)
     need("pool", ("sent", count["sent"]), ("pool", count["pool"]))
     need("sync", ("act", count["act"]), ("pe", count["pe"]), ("stored", count["stored"]))

@@ -17,8 +17,8 @@ SUM2 = FROM2[:7] + [16 * k + 16 for k in range(7, 16)]
 BASE2 = [64, 64, 64, 160]
 ON_SCALAR1 = [0]
 ON_SCALAR2 = [0, 1]
-TILES1 = {4: [0], 8: [1], 11: [2]}
-TILES2 = {8: [1], 9: [0], 12: [2], 15: [3]}
+TILES1 = {6: [0], 11: [1, 2]}
+TILES2 = {9: [1], 11: [0], 15: [2, 3]}
 
 Q4, U8, BF, F32, I32, U16 = "float8_e4m3fn_x4", "uint8", "bfloat16", "float32", "int32", "uint16"
 SCRATCH = {}
@@ -209,14 +209,14 @@ def rank_program(g, core, T, topo):
     qe = [vq("ce", 128 * b, 128, T.etile[:, 3 - b:515 - b], [k_et]) for b in range(4)]
 
     qu = vq("cu", 0, 128, T.ub[:], [ldu])
+    qt = vq("ct0", 0, C, T.xb[:], [ldx])
     uc_c = pick_codes("cucmp", "cu", 32, 128, lcmp, [qu, k_lcmp])
     uc_s = pick_scales("cucmp", "cu", 32, 128, lcmp, [qu, k_lcmp])
-    qt = vq("ct0", 0, C, T.xb[:], [ldx])
     ur_c = pick_codes("curep", "cu", 128, 128, lrep, [k_lrep])
     ur_s = pick_scales("curep", "cu", 128, 128, lrep, [k_lrep])
     gotu = [send_u(kind[0], [uc_c, uc_s])]
 
-    def compare(row, n, own, frm, summ, base, moff, mt, a0, scalar_blocks, ready, between, tile_done, extra):
+    def compare(row, n, own, frm, summ, base, moff, mt, a0, scalar_blocks, ready, between, tile_done, extra, head=None):
         def slot(k, a, b):
             o = moff[k // 4] + k % 4 - 4 * base[k // 4]
             return mt[:, o + 4 * a:o + 4 * b - 3:4]
@@ -232,9 +232,16 @@ def rank_program(g, core, T, topo):
             wrote[k] = act(slot(k, summ[k], n), T.sg[:, 224 * j + d:224 * j + n - frm[k]], F.Relu, [sign[j]], scale=-1.0,
                            accum_out=T.acc[:, a0 + k:a0 + k + 1])
             sums.append(wrote[k])
+        start = list(frm)
+        if head:
+            blocks, upto, soon = head
+            for k in blocks:
+                vts(slot(k, frm[k], upto), row[:, frm[k]:upto], own(k), None, A.is_gt, after=soon)
+                start[k] = upto
         for k in range(len(frm)):
             if k not in wrote:
-                wrote[k] = vts(slot(k, frm[k], n), row[:, frm[k]:n], own(k), None, A.is_gt, after=ready + between(k))
+                between(k)
+                wrote[k] = vts(slot(k, start[k], n), row[:, start[k]:n], own(k), None, A.is_gt, after=ready)
                 if summ[k] < n:
                     sums.append(act(T.junk[:, 224 * k:224 * k + n - summ[k]], slot(k, summ[k], n), F.Identity, [wrote[k]],
                                     accum_out=T.acc[:, a0 + k:a0 + k + 1]))
@@ -268,39 +275,39 @@ def rank_program(g, core, T, topo):
             k_o16 = act(T.ocol[:, 0:1], qcol, F.Identity, [k_col], scale=DROP, bias=-15 * DROP)
             k_acc = fill(T.acc, 0, 32, 0.0)
             k_d16 = act(T.d16[:], T.nm16[:], F.Identity, [k_nm16], scale=-17 * DROP, bias=16 * DROP)
-            act(T.sc[:, 0:128], T.pw1[:, 0:128], F.Copy, [early[1]])
+            cp0 = act(T.sc[:, 0:128], T.pw1[:, 0:128], F.Copy, [early[1]])
+            k_b1 = act(T.bas[:, 0:12], T.crow[:, 16:193:16], F.Identity, [k_o16, k_crow], bias=T.ocol[:, 0:1])
             a0 = first_mask(early)
             qg = vq("cg", 0, 128, T.gtile[:], k_gt)
         cp = act(T.sc[:, 128:C], T.pw3[:, 64:128], F.Copy, [sb2])
         a1 = vsum(T.hold[:, 0:128], T.nm16[:, 0:128], T.sm[:, 0:128], [a0])
-        vtt(T.eq[:, 0:128], T.pw0[:, 0:128], T.hold[:, 0:128], A.is_equal, [a1])
         got = {}
 
         def between1(k):
-            if k == 2:
+            if k == 1:
+                vtt(T.eq[:, 0:128], T.pw0[:, 0:128], T.hold[:, 0:128], A.is_equal, [a1])
                 got["m"] = vtt(T.sm[:, 128:C], T.pw2[:, 64:128], T.m16[:, 128:C], A.mult, [sb])
             if k == 3:
                 got["h"] = vsum(T.hold[:, 128:C], T.nm16[:, 128:C], T.sm[:, 128:C], [got["m"]])
-            return [got["h"]] if k >= 8 else []
+            if k == 5:
+                got["eq"] = vtt(T.eq[:, 128:C], T.pw2[:, 64:128], T.hold[:, 128:C], A.is_equal, [got["h"]])
+            if k == 7:
+                got["cor"] = vsum(T.cor[:], T.nm16[:, 0:C], T.eq[:], [got["eq"]])
+            if k == 10:
+                got["pre"] = vtt(T.pre[:, 0:12], T.bas[:, 0:12], T.cor[:, 15:C:16], A.subtract, [got["cor"], k_b1])
 
         def tile1(n, toks, turn):
             w = C - BASE1[n]
-            if n == turn[-1]:
-                got["eq"] = vtt(T.eq[:, 128:C], T.pw2[:, 64:128], T.hold[:, 128:C], A.is_equal)
             q = vq("cma", MOFF1[n] // 4, w, T.ma[:, MOFF1[n]:MOFF1[n] + 4 * w], toks + z1)
             got["y"] = mm("pp", "cg", 0, "cma", MOFF1[n] // 4 + 64 - BASE1[n], 128, [q, qg], n == turn[0], n == turn[-1])
             if n == 0:
                 got["x"] = mm("py", "cg", 0, "cma", 0, 128, [q])
 
         sums = compare(T.sc, C, lambda k: T.hold[:, 16 * k + 15:16 * k + 16], FROM1, SUM1, BASE1, MOFF1, T.ma, 0,
-                       ON_SCALAR1, [a1, cp] + k_acc + z1, between1, tile1, TILES1)
-        if t == 0:
-            k_b1 = act(T.bas[:, 0:12], T.crow[:, 16:193:16], F.Identity, [k_o16, k_crow], bias=T.ocol[:, 0:1])
-        a3 = vsum(T.cor[:], T.nm16[:, 0:C], T.eq[:], [got["eq"]])
+                       ON_SCALAR1, [a1, cp] + k_acc + z1, between1, tile1, TILES1, ([1, 2, 3], 128, [a1, cp0] + z1))
         a4 = vhold(T.hh[:, 0:64], T.d16[:, 0:64], T.py[:, 0:64], [got["x"], k_d16])
-        a5 = vtt(T.pre[:, 0:12], T.bas[:, 0:12], T.cor[:, 15:C:16], A.subtract, [a3, k_b1])
+        a7 = vtt(T.cnt[:, 0:12], T.pre[:, 0:12], T.acc[:, 0:12], A.add, [got["pre"], sums])
         a6 = vhold(T.hh[:, 64:C], T.d16[:, 0:128], T.pp[:, 0:128], [got["y"]])
-        a7 = vtt(T.cnt[:, 0:12], T.pre[:, 0:12], T.acc[:, 0:12], A.add, [a5, sums])
         a8 = vtt(T.cnt[:, 0:12], T.cnt[:, 0:12], T.hh[:, 15:C:16], A.subtract, [a4, a6, a7])
         a9 = vcp(R("rk")[:, 0:12], T.cnt[:, 0:12], [a8])
         send(R("lrk")[:, 0:12], R("rk")[:, 0:12], "gotr%d" % t, t, [a9])
@@ -327,25 +334,16 @@ def rank_program(g, core, T, topo):
             c5 = scores()
         c1 = vcp(T.ss[:, 0:C].indirect(R("rk")[:, 0:12]), T.sc[:], [a9])
         if t == 0:
+            t1 = vhold(T.hold[:], T.d16[:], T.val0[:], k_val)
             keep["c0"] = pick_codes("curp0", "clu0", 128, 8, lrp, [gotu[0], k_lrp])
             c5 = scores()
-            t1 = vhold(T.hold[:], T.d16[:], T.val0[:], k_val)
             t2 = vts(T.tint[:, 0:18], T.hold[:, 15:NP:16], T.ocol[:, 0:1], None, A.subtract, after=[t1])
             k_lpj = vts(T.lpj[:, 0:18], T.hold[:, 15:NP:16], T.ocol[:, 0:1], 1.0 / 4096.0, A.subtract, A.mult)
             t3 = vts(T.tand[:, 0:18], T.tint[:, 0:18], 2, 1023, A.logical_shift_right, A.bitwise_and, after=[t2])
             k_lpi = vcp(T.lpi[:, 0:18], T.tand[:, 0:18], [t3])
         c4 = act(T.spi[:], T.ss[:, 0:C + 8].indirect(T.lpi[:, 0:18]), F.Copy, [c1, k_lpi] + k_low)
         c0 = vcp(T.so[:, 0:C].indirect(R("rk")[:, 0:12]), T.orow[:], [k_orow])
-        if t == 0:
-            keep["c1"] = pick_codes("curp1", "clu1", 128, 8, lrp, [gotu[1]])
-        if t == 1:
-            qv = vq("cv", 0, 128, T.vb[:], [ldv])
-        c2 = vhold(T.h4[:, 0:K], T.d4[:, 0:K], T.so[:, 0:K], [c0] + k_d4)
-        c3 = vts(R("ol")[:, 0:16], T.h4[:, 3:K:4], T.ocol[:, 1:2], None, A.add, after=[c2, k_o4])
-        send(R("lol")[:, 0:16], R("ol")[:, 0:16], "goto%d" % t, t, [c3])
-        goto = ("goto%d" % t, nin[t])
         pd = [mm("pw%d" % b, "ce", 128 * b, cl, 0, C, qe) for b in range(4)]
-        c6 = act(T.aa[:], state[:, 0:4 * C].indirect(R("ol")[:, 0:16]), F.Copy, [c3], scale=0.5)
         c7 = [act(T.dd[:, b:4 * C:4], T["pw%d" % b][:, 0:C], F.Copy, [pd[b]], scale=0.5) for b in range(4)]
         if t == 0:
             need("sync", gotr)
@@ -359,34 +357,44 @@ def rank_program(g, core, T, topo):
                      act(T.pre[:, 16:30], T.crow[:, 64:NP:16], F.Identity, [k_c3], bias=T.ocol[:, 3:4])]
 
         d0 = vcp(T.es[:, 0:C].indirect(R("lrk")[:, 0:12]), T.sp[:], [gotr, c5])
+        c2 = vhold(T.h4[:, 0:K], T.d4[:, 0:K], T.so[:, 0:K], [c0] + k_d4)
         d1 = [vtt(T.vv[:, 16 * a:16 * b], T.es[:, 0:C].indirect(T.lpj[:, a:b]), T.spi[:, 16 * a:16 * b], A.add, [d0, c4, k_lpj])
               for a, b in ((0, 8), (8, 18))]
         d2 = [vtt(T.sm[:, a:a + 128], T.vv[:, a:a + 128], T.m16[:, a:a + 128], A.mult, [d1[a // 128]]) for a in (0, 128)]
-        d3 = [vsum(T.hold[:, a:a + 128], T.nm16[:, a:a + 128], T.sm[:, a:a + 128], [d2[a // 128]]) for a in (0, 128)]
+        d3 = [vsum(T.hold[:, 0:128], T.nm16[:, 0:128], T.sm[:, 0:128], [d2[0]])]
+        c3 = vts(R("ol")[:, 0:16], T.h4[:, 3:K:4], T.ocol[:, 1:2], None, A.add, after=[c2, k_o4])
+        d3.append(vsum(T.hold[:, 128:256], T.nm16[:, 128:256], T.sm[:, 128:256], [d2[1]]))
+        send(R("lol")[:, 0:16], R("ol")[:, 0:16], "goto%d" % t, t, [c3])
+        goto = ("goto%d" % t, nin[t])
         lo, hi = 16 * 7, 16 * 16
+
+        def between2(k):
+            if k == 5:
+                got["eq"] = vtt(T.eq[:, 0:hi - lo], T.vv[:, lo:hi], T.hold[:, lo:hi], A.is_equal, [d3[1]])
+            if k == 7:
+                got["cor"] = vsum(T.cor[:, 0:hi - lo], T.nm16[:, lo:hi], T.eq[:, 0:hi - lo], [got["eq"]])
+            if k == 9:
+                got["pre"] = vtt(T.pre[:, 19:28], T.bas[:, 12:21], T.cor[:, 15:hi - lo:16], A.subtract, [got["cor"]] + k_pre)
 
         def tile2(n, toks, turn):
             skip = 0 if t == 0 or n == 3 else FROM2[4 * n] - BASE2[n]
             w = NP - BASE2[n] - skip
             o = MOFF2[n] + 4 * skip
-            if n == 3:
-                got["eq"] = vtt(T.eq[:, 0:hi - lo], T.vv[:, lo:hi], T.hold[:, lo:hi], A.is_equal)
             q = vq("cmb", o // 4, w, T.mb[:, o:o + 4 * w], toks + z2)
-            got["y"] = mm("pb", "cg", 0, "cmb", MOFF2[n] // 4 + 160 - BASE2[n], 128, [q], n == turn[0], n == turn[-1])
             if n < 3:
                 got["x"] = mm("pa", "cg", 0, "cmb", MOFF2[n] // 4, 128, [q], n == turn[0], n == turn[-2])
+            got["y"] = mm("pb", "cg", 0, "cmb", MOFF2[n] // 4 + 160 - BASE2[n], 128, [q], n == turn[0], n == turn[-1])
 
         sums = compare(T.vv, NP, lambda k: T.hold[:, 16 * k + 15:16 * k + 16], FROM2, SUM2, BASE2, MOFF2, T.mb, 12,
-                       ON_SCALAR2, [d3[0], d1[1]] + z2, lambda k: [d3[1]] if k >= 8 else [], tile2, TILES2)
-        d5 = vsum(T.cor[:, 0:hi - lo], T.nm16[:, lo:hi], T.eq[:, 0:hi - lo], [got["eq"]])
+                       ON_SCALAR2, [d3[0], d1[1]] + z2, between2, tile2, TILES2)
         d6 = vhold(T.hh[:, 64:192], T.d16[:, 0:128], T.pa[:, 0:128], [got["x"]])
-        d7 = vtt(T.pre[:, 19:28], T.bas[:, 12:21], T.cor[:, 15:hi - lo:16], A.subtract, [d5] + k_pre)
+        d9 = vtt(T.cnt[:, 12:30], T.pre[:, 12:30], T.acc[:, 12:30], A.add, [got["pre"], sums])
         d8 = vhold(T.hh[:, 192:NP], T.d16[:, 0:96], T.pb[:, 32:128], [got["y"]])
-        d9 = vtt(T.cnt[:, 12:30], T.pre[:, 12:30], T.acc[:, 12:30], A.add, [d7, sums])
         d10 = vtt(T.cnt[:, 16:30], T.cnt[:, 16:30], T.hh[:, 79:NP:16], A.subtract, [d6, d8, d9])
         if t == 0:
             k_valr = act(T.valr[:], T.val0[:], F.Identity, [k_c2], bias=T.ocol[:, 2:3])
         d11 = vcp(T.rkp[:, 0:18], T.cnt[:, 12:30], [d10])
+        c6 = act(T.aa[:], state[:, 0:4 * C].indirect(R("ol")[:, 0:16]), F.Copy, [c3], scale=0.5)
         e0 = act(T.ee[:], T.dd[:, 0:4 * C].indirect(R("lol")[:, 0:16]), F.Copy, [goto, c7[-1]])
         if t == 0:
             keep["s1"] = pick_scales("curp1", "clu1", 128, 8, lrp, [gotu[1]])
@@ -395,6 +403,10 @@ def rank_program(g, core, T, topo):
             k_nrow = act(T.nrow[:, FILL1:NP], T.crow[:, FILL0:NP - 8], F.Copy)
 
         e1 = vcp(T.xs[:, 0:NP].indirect(T.rkp[:, 0:18]), T.valr[:], [d11, k_valr])
+        if t == 0:
+            keep["c1"] = pick_codes("curp1", "clu1", 128, 8, lrp, [gotu[1]])
+        if t == 1:
+            qv = vq("cv", 0, 128, T.vb[:], [ldv])
         e2 = vhold(T.h4[:], T.d4[:], T.xs[:, 0:C], [e1])
         e4 = vts(T.tint[:], T.h4[:, 3:C:4], T.ocol[:, 1:2], None, A.add, after=[e2])
         e3 = vts(T.offe[:], T.h4[:, 3:C:4], T.ocol[:, 1:2], 1.0 / 1024.0, A.add, A.mult)
@@ -424,7 +436,7 @@ def rank_program(g, core, T, topo):
                 early = first_scores(nxt, [vq(nxt, 0, 128, T.tt[:, 0:512], ts[:4])])
         state = T.tt
         if t < ROUNDS - 1:
-            act(T.sc[:, 0:128], T.pw1[:, 0:128], F.Copy, [early[1]])
+            cp0 = act(T.sc[:, 0:128], T.pw1[:, 0:128], F.Copy, [early[1]])
             a0 = first_mask(early)
             qt = vq(nxt, 64, 128, T.tt[:, 256:768], ts + [early[1]])
         else:

@@ -1,24 +1,30 @@
 from concourse.bass import DstId, RemoteDMATransfer
-from concourse.mybir import dt, AluOpType, ActivationFunctionType
+from concourse.mybir import dt, AluOpType, ActivationFunctionType, AxisListType
 
 C, K, ROUNDS = 192, 64, 3
 STEP = [1, 2, 1]
 LENS = [K // (i + 1) for i in range(K)]
 NP = 288
 FILL0, FILL1 = 248, 256
-LOW = -9.0e29
+LOW = -2.0 ** 83
+HIGH = 2.0 ** 90
+RESET = 2.0 ** 96
 DROP = float(2 ** 19)
+SLOPE, LIFT = 2048.0, float(2 ** 18)
 
-FROM1 = [16 * k for k in range(12)]
-SUM1 = [16 * k + 16 for k in range(12)]
+FROM1 = [16 * k + 16 for k in range(11)]
 BASE1 = [0, 64, 64]
+MOFF1 = [0, 4 * 320, 4 * 192]
 FROM2 = [64] * 4 + [96] * 2 + [112] + [16 * k for k in range(7, 16)]
 SUM2 = FROM2[:7] + [16 * k + 16 for k in range(7, 16)]
 BASE2 = [64, 64, 64, 160]
-ON_SCALAR1 = [0]
-ON_SCALAR2 = [0, 1]
-TILES1 = {6: [0], 11: [1, 2]}
-TILES2 = {9: [1], 11: [0], 15: [2, 3]}
+MOFF2 = [0, 4 * 224, 4 * 448, 4 * 672]
+ORDER1 = [5, "copy", 6, "mask", 7, 10, "in1", "hold", "a0", 9, 8, 4, "b0", "in2", 3, 1, 2, "q12", "r4", "cor", "r10", "q0", "pre",
+          "x", "s1", "s0"]
+ORDER2 = ["a0", "a1", "b0", "mask", "b1", 2, "hold", 3, 10, 9, 4, 5, 7, 6, "eq", "q1", 11, 8, "q0", 14, "cor", "q2",
+          15, 13, "pre", 12, "x0", "x1", "q3", "s1", "x2", "n1", "s2", "put1", "n2", "put2"]
+
+ZRUNS = [(16, 22), (22, 36), (36, 48), (0, 8), (8, 16)]
 
 Q4, U8, BF, F32, I32, U16 = "float8_e4m3fn_x4", "uint8", "bfloat16", "float32", "int32", "uint16"
 SCRATCH = {}
@@ -33,27 +39,25 @@ def _mx(name, n):
     _sb(name + "s", n, U8)
 
 
-MOFF1 = [0, 4 * 192, 4 * 320]
-MOFF2 = [0, 4 * 224, 4 * 448, 4 * 672]
 for _n, _w, _k in [
         ("xb", 4 * C, BF), ("ub", 512, BF), ("vb", 512, BF),
-        ("pbit", 8, I32), ("pcol", 8, F32), ("crow", NP, F32), ("cm16", NP, BF), ("dcol", 8, F32),
-        ("m16", NP, BF), ("nm16", NP, BF), ("d16", NP, BF), ("d4", C, BF), ("ocol", 8, F32),
-        ("orow", C, F32), ("nrow", NP, F32), ("val0", NP, F32), ("valr", NP, F32),
-        ("lrep", 16, U16), ("lrp", 16, U16), ("lcmp", 16, U16), ("lpi", 32, U16), ("lpj", 32, U16),
+        ("pbit", 8, I32), ("pcol", 8, F32), ("crow", C, F32), ("cm16", NP, BF), ("c16", 24, F32), ("dcol", 8, F32),
+        ("off16", 224, BF), ("new16", C, BF), ("d16", 224, BF), ("d4", C, BF), ("ocol", 16, F32),
+        ("pat", NP, F32), ("pats", K, F32), ("nrow", NP, F32), ("val0", NP, F32),
+        ("lrep", 16, U16), ("lrp", 16, U16), ("lcmp", 16, U16), ("lpi", 16, U16), ("lpj", 16, U16),
         ("tint", 48, I32), ("tand", 48, I32), ("gidx", 128, BF), ("gtile", 512, BF), ("etile", 520, BF),
         ("sc", C, F32), ("sp", C, F32), ("sm", NP, F32), ("hold", NP, F32), ("eq", C, BF), ("cor", C, BF),
         ("ma", 4 * 448, BF), ("mb", 4 * 800, BF), ("junk", 16 * 224, BF), ("sg", 4 * 224, BF), ("hh", NP, F32),
-        ("acc", 32, F32), ("bas", 32, F32), ("pre", 32, F32), ("cnt", 32, F32), ("rkp", 32, U16),
-        ("ss", C + 8, F32), ("so", C, F32), ("es", C, F32), ("spi", NP, F32), ("vv", NP, F32), ("xs", NP, F32),
-        ("h4", C, F32), ("offa", 48, U16), ("offe", 48, U16), ("nout", NP, F32), ("ysb", C, F32),
+        ("acc1", 16, F32), ("acc2", 24, F32), ("bas", 40, F32), ("pre1", 16, F32), ("pre2", 24, F32), ("rkp", 32, U16),
+        ("ss", K + 8, F32), ("so", C, F32), ("es", C, F32), ("spi", NP, F32), ("vv", NP, F32), ("xs", NP, F32),
+        ("h4", K, F32), ("hi", C, I32), ("offa", 48, U16), ("offe", 48, U16), ("nout", NP, F32), ("ysb", C, F32),
         ("eg", 4 * C, BF), ("rr", 4 * C, F32)]:
     _sb(_n, _w, _k)
 for _n, _w in [("u", 128), ("urep", 128), ("ucmp", 32), ("lu0", 32), ("lu1", 32), ("urp0", 128), ("urp1", 128),
                ("v", 128), ("w", 512), ("e", 512), ("g", 128), ("ma", 448), ("mb", 800)]:
     _mx("c" + _n, _w)
 for _t in range(ROUNDS + 1):
-    _mx("ct%d" % _t, C)
+    _mx("ct%d" % _t, C + 128)
 _mx("cz", 256)
 for _n, _w, _k in [("zz", 4 * C, BF), ("dd", 4 * C, BF), ("aa", 4 * K, BF), ("ee", 4 * K, BF), ("tt", 4 * C, BF)]:
     _sb(_n, _w, _k)
@@ -107,13 +111,17 @@ def rank_program(g, core, T, topo):
         need("vec", *after)
         return done("vec", V.memset(out, value))
 
-    def vsum(out, d0, d1, after=()):
+    def vred(out, in_, after=()):
         need("vec", *after)
-        return done("vec", V.tensor_tensor_scan(out, d0, d1, 0.0, A.mult, A.add))
+        return done("vec", V.tensor_reduce(out, in_, AxisListType.X, A.add))
 
     def vhold(out, d0, d1, after=()):
         need("vec", *after)
         return done("vec", V.tensor_tensor_scan(out, d0, d1, 0.0, A.add, A.min))
+
+    def vcount(out, d0, d1, start, after=()):
+        need("vec", *after)
+        return done("vec", V.tensor_tensor_scan(out, d0, d1, start, A.min, A.add))
 
     def vq(name, a, n, in_, after=()):
         need("vec", *after)
@@ -137,10 +145,6 @@ def rank_program(g, core, T, topo):
     def pick_scales(dst, src, n, m, off, after=()):
         return act(T[dst + "s"][:, 0:n], T[src + "s"][:, 0:m].indirect(off), F.Copy, after)
 
-    def fill(buf, a, n, value, after=()):
-        return [act(buf[:, b:min(b + NP, a + n)], T.cm16[:, 0:min(b + NP, a + n) - b], F.Identity, after, scale=0.0, bias=value)
-                for b in range(a, a + n, NP)]
-
     peer = [T.cores[rank ^ s] for s in STEP]
     kind = [0, 1, 0]
     nen = [len(topo.engines(core, c)) for c in peer]
@@ -151,6 +155,11 @@ def rank_program(g, core, T, topo):
         rid, pid = topo.addr(peer[t])[0:2]
         g.remote_dma(out, in_, T.sem[sem], T.sem["sent"], pid, rid, topo.mask(core, peer[t]))
         count["sent"] = count.get("sent", 0) + nen[t]
+
+    def send_state(t, a, b, n, after):
+        src, dst = "ct%d" % t, "cl%d" % t
+        send(T[dst + "q"][:, b:b + n].bitcast(dt.uint8), T[src + "q"][:, a:a + n].bitcast(dt.uint8), "gott%d" % t, t, after)
+        send(T[dst + "s"][:, b:b + n], T[src + "s"][:, a:a + n], "gott%d" % t, t, after)
 
     def send_u(h, after):
         need("pool", *after)
@@ -165,294 +174,325 @@ def rank_program(g, core, T, topo):
         count["sent"] = count.get("sent", 0) + len(eng)
         return ("gotu%d" % h, nin[h])
 
-    ldx = done("ldx", Y.dma_start(T.xb[:], T.x[:]), 16)
-    ldu = done("ldu", S.dma_start(T.ub[:], T.u[:]), 16)
+    ldu = done("ldu", Y.dma_start(T.ub[:], T.u[:]), 16)
+    ldx = done("ldx", S.dma_start(T.xb[:], T.x[:]), 16)
 
     k_p = done("pool", g.iota(T.pbit[:, 3:4], [[0, 1]], 0, 1))
     k_cm16 = iota(T.cm16[:], [[0, NP // 16], [1, 16]], 0, 0)
-    k_crow = iota(T.crow[:], [[1, NP]], 0, 0)
+    k_crow = iota(T.crow[:], [[1, C]], 0, 0)
     k_gi = iota(T.gidx[:], [[16, 8], [0, 16]], 0, 0)
-    place, singles, i = 0, [], 0
-    k_val = []
+    k_c16 = iota(T.c16[:], [[16, 24]], 0, 0)
+
+    runs, place, i = [], 0, 0
     while i < K:
-        n = 1
-        while i + n < K and LENS[i + n] == LENS[i]:
-            n += 1
+        n = LENS.count(LENS[i])
         if place == FILL0:
+            runs.append((FILL0, FILL1, [[0, FILL1 - FILL0]], 4 * K))
             place = FILL1
-        if n == 1:
-            singles.append((i, place))
-        else:
-            k_val.append(iota(T.val0[:, place:place + n * LENS[i]], [[4, n], [4096, LENS[i]]], 4 * i, 0))
+        runs.append((place, place + n * LENS[i], [[4, n], [4096, LENS[i]]], 4 * i))
         place += n * LENS[i]
         i += n
 
-    z1 = [vset(T.ma[:, MOFF1[n]:MOFF1[n] + 4 * (FROM1[4 * n + 3] - BASE1[n])], 0.0) for n in range(3)]
-    k_et0 = fill(T.etile, 0, 520, 0.0, [k_cm16])
-    z2 = []
-    for n in range(1, 4):
-        z2 += fill(T.mb, MOFF2[n], 4 * (FROM2[4 * n + 3] - BASE2[n]), 0.0)
+    def pair_rows(n):
+        return [iota(T.val0[:, a:b], pattern, base, 0) for a, b, pattern, base in [runs.pop() for _ in range(n)]][-1]
+
+    pair_rows(6)
+
     pint = T.pbit[:, 3:4]
+    z1 = [vset(T.ma[:, MOFF1[n]:MOFF1[n] + 4 * (FROM1[4 * n + 2] - BASE1[n])], 0.0) for n in range(3)]
     bits = [vts(T.pbit[:, 0:1], pint, 15, None, A.bitwise_and, after=[k_p]),
             vts(T.pbit[:, 1:2], pint, 3, None, A.bitwise_and),
             vts(T.pbit[:, 2:3], pint, 2, 3, A.logical_shift_right, A.bitwise_and)]
+    k_et0 = vset(T.etile[:], 0.0)
     k_col = vcp(T.pcol[:, 0:4], T.pbit[:, 0:4], bits)
     qcol, rcol, ccol, ncol = [T.pcol[:, n:n + 1] for n in range(4)]
     lrep, lrp, lcmp = T.lrep[:, 0:8], T.lrp[:, 0:8], T.lcmp[:, 0:2]
-    k_m16 = vts(T.m16[:], T.cm16[:], qcol, None, A.is_equal, after=[k_col, k_cm16])
-    k_nm16 = vts(T.nm16[:], T.cm16[:], qcol, None, A.not_equal)
+    col = lambda n: T.ocol[:, n:n + 1]
+    k_acc = [vset(T.acc1[:], 0.0), vset(T.acc2[:], 0.0), vset(T.ss[:, K:K + 8], LOW)]
+    k_lrep = vts(lrep, T.cm16[:, 0:8], 16.0, None, A.mult, after=[k_cm16])
+    k_off = vts(T.off16[:], T.cm16[:, 0:224], qcol, HIGH, A.not_equal, A.mult, after=[k_col])
+    k_new = vts(T.new16[:], T.cm16[:, 0:C], 0.0, RESET, A.is_equal, A.mult)
     k_lcmp = vts(lcmp, T.pcol[:, 0:2], 7.0, 16.0, A.min, A.mult)
-    k_lrep = vts(lrep, T.cm16[:, 0:8], 16.0, None, A.mult)
     k_lrp = vcp(lrp, T.cm16[:, 0:8])
     k_dc = vts(T.dcol[:, 0:4], T.cm16[:, 0:4], ccol, 5 * DROP, A.is_equal, A.mult)
-    k_et = vts(T.etile[:, 3:512:4], T.crow[:, 0:128], ncol, None, A.is_equal, after=k_et0 + [k_crow])
-    qe = [vq("ce", 128 * b, 128, T.etile[:, 3 - b:515 - b], [k_et]) for b in range(4)]
+    k_et = vts(T.etile[:, 3:512:4], T.crow[:, 0:128], ncol, None, A.is_equal, after=[k_et0, k_crow])
+    unpack = lambda b: vq("ce", 128 * b, 128, T.etile[:, 3 - b:515 - b], [k_et])
+    qe = [unpack(0)]
+
+    k_s0 = act(col(0), qcol, F.Square, [k_col], scale=-32.0, bias=480.0)
+    k_s2 = act(col(2), qcol, F.Identity, scale=SLOPE, bias=-SLOPE / 2)
+    k_s3 = act(col(3), qcol, F.Identity, scale=-1.0, bias=LIFT)
+    k_o16 = act(col(4), qcol, F.Identity, scale=DROP, bias=-15 * DROP)
+    k_s1 = act(col(1), col(0), F.Identity, [k_s0], bias=-LIFT)
+    k_pat = act(T.pat[:], T.cm16[:], F.Identity, [k_s2, k_cm16], scale=-SLOPE, bias=col(2))
+    k_d16 = act(T.d16[:], T.off16[:], F.Identity, [k_off], scale=-17 * DROP / HIGH, bias=16 * DROP)
 
     qu = vq("cu", 0, 128, T.ub[:], [ldu])
+    k_gt = vts(T.gtile[:, 0:512:4], T.gidx[:], qcol, ncol, A.add, A.is_equal, after=[k_gi])
+    ur_c = pick_codes("curep", "cu", 128, 128, lrep, [qu, k_lrep])
+    ur_s = pick_scales("curep", "cu", 128, 128, lrep, [qu, k_lrep])
     qt = vq("ct0", 0, C, T.xb[:], [ldx])
-    uc_c = pick_codes("cucmp", "cu", 32, 128, lcmp, [qu, k_lcmp])
-    uc_s = pick_scales("cucmp", "cu", 32, 128, lcmp, [qu, k_lcmp])
-    ur_c = pick_codes("curep", "cu", 128, 128, lrep, [k_lrep])
-    ur_s = pick_scales("curep", "cu", 128, 128, lrep, [k_lrep])
-    gotu = [send_u(kind[0], [uc_c, uc_s])]
+    uc_c = pick_codes("cucmp", "cu", 32, 128, lcmp, [k_lcmp])
+    uc_s = pick_scales("cucmp", "cu", 32, 128, lcmp, [k_lcmp])
+    qe.append(unpack(1))
+    k_gt = [act(T.gtile[:, b:512:4], T.gtile[:, 0:512:4], F.Copy, [k_gt]) for b in range(1, 4)]
 
-    def compare(row, n, own, frm, summ, base, moff, mt, a0, scalar_blocks, ready, between, tile_done, extra, head=None):
-        def slot(k, a, b):
-            o = moff[k // 4] + k % 4 - 4 * base[k // 4]
-            return mt[:, o + 4 * a:o + 4 * b - 3:4]
-        wrote = {}
-        sums = []
-        turn = [job for k in sorted(extra) for job in extra[k]]
-        sign = [act(T.sg[:, 224 * j:224 * j + n - frm[k]], row[:, frm[k]:n], F.Sign, ready, scale=-1.0, bias=own(k))
-                for j, k in enumerate(scalar_blocks)]
-        for j, k in enumerate(scalar_blocks):
-            d = summ[k] - frm[k]
-            if d:
-                act(slot(k, frm[k], summ[k]), T.sg[:, 224 * j:224 * j + d], F.Relu, [sign[j]], scale=-1.0)
-            wrote[k] = act(slot(k, summ[k], n), T.sg[:, 224 * j + d:224 * j + n - frm[k]], F.Relu, [sign[j]], scale=-1.0,
-                           accum_out=T.acc[:, a0 + k:a0 + k + 1])
-            sums.append(wrote[k])
-        start = list(frm)
-        if head:
-            blocks, upto, soon = head
-            for k in blocks:
-                vts(slot(k, frm[k], upto), row[:, frm[k]:upto], own(k), None, A.is_gt, after=soon)
-                start[k] = upto
-        for k in range(len(frm)):
-            if k not in wrote:
-                between(k)
-                wrote[k] = vts(slot(k, start[k], n), row[:, start[k]:n], own(k), None, A.is_gt, after=ready)
-                if summ[k] < n:
-                    sums.append(act(T.junk[:, 224 * k:224 * k + n - summ[k]], slot(k, summ[k], n), F.Identity, [wrote[k]],
-                                    accum_out=T.acc[:, a0 + k:a0 + k + 1]))
-            for job in extra.get(k, ()):
-                tile_done(job, [wrote[j] for j in range(4 * job, 4 * job + 4)], turn)
-        return sums[-1]
+    def counting(order, row, n, own, ready, frm, summ, slot, acc, named):
+        got = {}
+        for s in order:
+            k = s if s in range(len(frm)) else int(s[1:]) if s[0] in "abr" and s[1:].isdigit() else None
+            if k is None:
+                got[s] = named[s](got)
+            elif k == s:
+                got[k] = vts(slot(k, frm[k], n), row[:, frm[k]:n], own(k), None, A.is_gt, after=ready(k, got))
+                if "r%d" % k not in order:
+                    got["r%d" % k] = act(T.junk[:, 224 * k:224 * k + n - summ[k]], slot(k, summ[k], n), F.Identity, [got[k]],
+                                         accum_out=acc[:, k:k + 1])
+            elif s[0] == "r":
+                got[s] = vred(acc[:, k:k + 1], slot(k, summ[k], n), [got[k]] + k_acc)
+            elif s[0] == "a":
+                got[s] = act(T.sg[:, 224 * k:224 * k + n - frm[k]], row[:, frm[k]:n], F.Sign, ready(k, got), scale=-1.0, bias=own(k))
+            else:
+                got[k] = got["r%d" % k] = act(slot(k, frm[k], n), T.sg[:, 224 * k:224 * k + n - frm[k]], F.Relu, [got["a%d" % k]],
+                                              scale=-1.0, accum_out=acc[:, k:k + 1])
+        return got
 
-    def first_scores(ct, after):
-        return mm("pw0", "curep", 0, ct, 0, 128, after), mm("pw1", "curep", 0, ct, 0, 128)
+    def sums(got, a, b):
+        return [got["r%d" % k] for k in range(a, b)]
+
+    def slot1(k, a, b):
+        n = (k + 1) // 4
+        o = MOFF1[n] + (k + 1) % 4 - 4 * BASE1[n]
+        return T.ma[:, o + 4 * a:o + 4 * b - 3:4]
+
+    def slot2(k, a, b):
+        o = MOFF2[k // 4] + k % 4 - 4 * BASE2[k // 4]
+        return T.mb[:, o + 4 * a:o + 4 * b - 3:4]
+
+    def zeros(n):
+        w = 4 * (FROM2[4 * n + 3] - BASE2[n])
+        return act(T.mb[:, MOFF2[n]:MOFF2[n] + w], T.etile[:, 0:w], F.Identity, [k_et], scale=0.0)
+
+    def first_scores(ct, at, after):
+        return mm("pw0", "curep", 0, ct, at, 128, after), mm("pw1", "curep", 0, ct, at, 128)
 
     def first_mask(early):
-        return vtt(T.sm[:, 0:128], T.pw0[:, 0:128], T.m16[:, 0:128], A.mult, [early[0], k_m16])
+        return vtt(T.sm[:, 64:C], T.pw0[:, 0:128], T.off16[:, 0:128], A.add, [early[0], k_off])
 
     state = T.xb
     keep = {}
     for t in range(ROUNDS):
         R = lambda n: T["%s%d" % (n, t)]
         ct, cl = "ct%d" % t, "cl%d" % t
-        send(T[cl + "q"][:].bitcast(dt.uint8), T[ct + "q"][:].bitcast(dt.uint8), "gott%d" % t, t, [qt])
-        send(T[cl + "s"][:], T[ct + "s"][:], "gott%d" % t, t, [qt])
-        gott = ("gott%d" % t, 2 * nin[t])
+        if t == 0:
+            gotu = [send_u(kind[0], [uc_c, uc_s])]
+        send_state(t, 0, 0, 64 if t else C, [qt])
+        gott = ("gott%d" % t, (4 if t else 2) * nin[t])
         if t == 0:
             gotu.append(send_u(kind[1], []))
+            k_val = pair_rows(len(runs) - 1)
+            k_row0 = pair_rows(1)
+        if t == 1:
+            iota(T.nrow[:, 0:FILL1], [[1, FILL1]], 0, 0)
+            k_nrow = iota(T.nrow[:, FILL1:NP], [[1, NP - FILL1]], FILL0, 0)
 
         if t == 0:
-            early = first_scores(ct, [qt, ur_c, ur_s])
-        sb2 = mm("pw3", "curep", 0, ct, 64, 128, [qt])
-        sb = mm("pw2", "curep", 0, ct, 64, 128)
+            early = first_scores(ct, 64, [qt, ur_c, ur_s])
+        sb = mm("pw2", "curep", 0, ct, 0, 128, [qt])
+        sb2 = mm("pw3", "curep", 0, ct, 0, 128)
         if t == 0:
-            k_gt = [vts(T.gtile[:, b:512:4], T.gidx[:], qcol, ncol, A.add, A.is_equal, after=[k_gi]) for b in range(4)]
-            k_o16 = act(T.ocol[:, 0:1], qcol, F.Identity, [k_col], scale=DROP, bias=-15 * DROP)
-            k_acc = fill(T.acc, 0, 32, 0.0)
-            k_d16 = act(T.d16[:], T.nm16[:], F.Identity, [k_nm16], scale=-17 * DROP, bias=16 * DROP)
-            cp0 = act(T.sc[:, 0:128], T.pw1[:, 0:128], F.Copy, [early[1]])
-            k_b1 = act(T.bas[:, 0:12], T.crow[:, 16:193:16], F.Identity, [k_o16, k_crow], bias=T.ocol[:, 0:1])
+            cp0 = act(T.sc[:, 64:C], T.pw1[:, 0:128], F.Copy, [early[1]])
             a0 = first_mask(early)
+            qe.append(unpack(2))
+            k_bas = act(T.bas[:, 0:18], T.c16[:, 0:18], F.Identity, [k_s3, k_c16], scale=-1.0, bias=col(3))
+            k_pats = act(T.pats[:], T.cm16[:, 0:K], F.Identity, scale=-SLOPE, bias=col(2))
+            k_dd = act(T.dcol[:, 4:8], T.dcol[:, 0:4], F.Identity, [k_dc], bias=-DROP)
+            k_pats = act(T.pats[:, 15:K:16], T.c16[:, 0:4], F.Identity, [k_pats], scale=0.0, bias=LIFT)
+        a1 = vhold(T.hold[:, 64:C], T.new16[:, 0:128], T.sm[:, 64:C], [a0, k_new])
+        if t == 0:
             qg = vq("cg", 0, 128, T.gtile[:], k_gt)
-        cp = act(T.sc[:, 128:C], T.pw3[:, 64:128], F.Copy, [sb2])
-        a1 = vsum(T.hold[:, 0:128], T.nm16[:, 0:128], T.sm[:, 0:128], [a0])
-        got = {}
 
-        def between1(k):
-            if k == 1:
-                vtt(T.eq[:, 0:128], T.pw0[:, 0:128], T.hold[:, 0:128], A.is_equal, [a1])
-                got["m"] = vtt(T.sm[:, 128:C], T.pw2[:, 64:128], T.m16[:, 128:C], A.mult, [sb])
-            if k == 3:
-                got["h"] = vsum(T.hold[:, 128:C], T.nm16[:, 128:C], T.sm[:, 128:C], [got["m"]])
-            if k == 5:
-                got["eq"] = vtt(T.eq[:, 128:C], T.pw2[:, 64:128], T.hold[:, 128:C], A.is_equal, [got["h"]])
-            if k == 7:
-                got["cor"] = vsum(T.cor[:], T.nm16[:, 0:C], T.eq[:], [got["eq"]])
-            if k == 10:
-                got["pre"] = vtt(T.pre[:, 0:12], T.bas[:, 0:12], T.cor[:, 15:C:16], A.subtract, [got["cor"], k_b1])
+        def tiles12(got):
+            a = MOFF1[2] // 4 + (64 if t else 0)
+            q = vq("cma", a, 448 - a, T.ma[:, 4 * a:4 * 448], [got[j] for j in range(3, 11)] + z1)
+            return [mm("pa", "cg", 0, "cma", MOFF1[n] // 4, 128, [q, qg], n == 2, False) for n in (2, 1)]
 
-        def tile1(n, toks, turn):
-            w = C - BASE1[n]
-            q = vq("cma", MOFF1[n] // 4, w, T.ma[:, MOFF1[n]:MOFF1[n] + 4 * w], toks + z1)
-            got["y"] = mm("pp", "cg", 0, "cma", MOFF1[n] // 4 + 64 - BASE1[n], 128, [q, qg], n == turn[0], n == turn[-1])
-            if n == 0:
-                got["x"] = mm("py", "cg", 0, "cma", 0, 128, [q])
+        def tile0(got):
+            q = vq("cma", 0, C, T.ma[:, 0:4 * C], [got[j] for j in (0, 1, 2, "in1", "in2")] + z1)
+            got["pa"] = mm("pa", "cg", 0, "cma", 64, 128, [q], False, True)
+            got["py"] = mm("py", "cg", 0, "cma", 0, 128)
 
-        sums = compare(T.sc, C, lambda k: T.hold[:, 16 * k + 15:16 * k + 16], FROM1, SUM1, BASE1, MOFF1, T.ma, 0,
-                       ON_SCALAR1, [a1, cp] + k_acc + z1, between1, tile1, TILES1, ([1, 2, 3], 128, [a1, cp0] + z1))
-        a4 = vhold(T.hh[:, 0:64], T.d16[:, 0:64], T.py[:, 0:64], [got["x"], k_d16])
-        a7 = vtt(T.cnt[:, 0:12], T.pre[:, 0:12], T.acc[:, 0:12], A.add, [got["pre"], sums])
-        a6 = vhold(T.hh[:, 64:C], T.d16[:, 0:128], T.pp[:, 0:128], [got["y"]])
-        a8 = vtt(T.cnt[:, 0:12], T.cnt[:, 0:12], T.hh[:, 15:C:16], A.subtract, [a4, a6, a7])
-        a9 = vcp(R("rk")[:, 0:12], T.cnt[:, 0:12], [a8])
+        got = counting(ORDER1, T.sc, C, lambda k: T.hold[:, 16 * k + 15:16 * k + 16],
+                       lambda k, got: [a1, cp0] + z1 + ([got["hold"]] if k < 4 else []) + ([got["copy"]] if k < 3 else []),
+                       FROM1, FROM1, slot1, T.acc1, {
+            "copy": lambda got: act(T.sc[:, 0:64], T.pw3[:, 0:64], F.Copy, [sb2]),
+            "mask": lambda got: vtt(T.sm[:, 0:64], T.pw2[:, 0:64], T.off16[:, 0:64], A.add, [sb]),
+            "hold": lambda got: vhold(T.hold[:, 0:64], T.new16[:, 0:64], T.sm[:, 0:64], [got["mask"]]),
+            "in1": lambda got: vtt(slot1(-1, 64, C), T.pw0[:, 0:128], T.hold[:, 64:C], A.is_gt, [a1]),
+            "in2": lambda got: vtt(slot1(-1, 0, 64), T.pw2[:, 0:64], T.hold[:, 0:64], A.is_gt, [got["hold"]]),
+            "cor": lambda got: vcount(T.cor[:], T.off16[:, 0:C], slot1(-1, 0, C), 0.0, [got["in1"], got["in2"]]),
+            "pre": lambda got: vtt(T.pre1[:, 0:12], T.bas[:, 0:12], T.cor[:, 15:C:16], A.subtract, [got["cor"], k_bas]),
+            "q0": tile0, "q12": tiles12,
+            "x": lambda got: vtt(T.pat[:, 15:C:16], T.pre1[:, 0:12], T.acc1[:, 0:12], A.subtract, [got["pre"], k_pat] + sums(got, 0, 11)),
+            "s0": lambda got: vcount(T.hh[:, 0:64], T.py[:, 0:64], T.pat[:, 0:64], LIFT, [got["py"], got["x"]]),
+            "s1": lambda got: vcount(T.hh[:, 64:C], T.pa[:, 0:128], T.pat[:, 64:C], LIFT, [got["pa"], got["x"]])})
+        a7 = max(got["s0"], got["s1"])
+        read = [got["in1"], got["in2"], got["copy"]]
+        h = kind[t]
+        if t == 0:
+            keep["s0"] = pick_scales("curp0", "clu0", 128, 8, lrp, [gotu[0], k_lrp])
+            keep["c0"] = pick_codes("curp0", "clu0", 128, 8, lrp, [gotu[0], k_lrp])
+        a9 = vts(R("rk")[:, 0:12], T.hh[:, 15:C:16], col(1), -1.0, A.add, A.mult, after=[a7, k_s1])
         send(R("lrk")[:, 0:12], R("rk")[:, 0:12], "gotr%d" % t, t, [a9])
         gotr = ("gotr%d" % t, nin[t])
 
-        h = kind[t]
-
-        def scores():
-            pp = mm("pp", "curp%d" % h, 0, cl, 0, C, [gott, a6, keep["c%d" % h], keep["s%d" % h]])
-            return act(T.sp[:], T.pp[:, 0:C], F.Copy, [pp])
-
+        pp = mm("pp", "curp%d" % h, 0, cl, 0, C, [gott, keep["c%d" % h], keep["s%d" % h]])
         if t == 0:
-            k_val += [act(T.val0[:, place:place + LENS[i]], T.crow[:, 0:LENS[i]], F.Identity, scale=4096.0, bias=4.0 * i)
-                      for i, place in singles]
-            k_val += fill(T.val0, FILL0, FILL1 - FILL0, 4.0 * C)
-            keep["s0"] = pick_scales("curp0", "clu0", 128, 8, lrp, [gotu[0], k_lrp])
-            k_orow = act(T.orow[:], T.crow[:, 0:C], F.Identity, scale=4.0, bias=rcol)
-            k_dd = act(T.dcol[:, 4:8], T.dcol[:, 0:4], F.Identity, [k_dc], bias=-DROP)
-            k_low = fill(T.ss, C, 8, LOW)
-            k_o4 = act(T.ocol[:, 1:2], ccol, F.Identity, scale=-DROP, bias=3 * DROP)
+            k_o4 = act(col(5), ccol, F.Identity, scale=-DROP, bias=3 * DROP)
             k_d4 = [act(T.d4[:, b:C:4], T.crow[:, 0:C // 4], F.Identity, [k_dd], scale=0.0, bias=T.dcol[:, 4 + b:5 + b])
                     for b in range(4)]
-        else:
-            c5 = scores()
-        c1 = vcp(T.ss[:, 0:C].indirect(R("rk")[:, 0:12]), T.sc[:], [a9])
+            k_o4 = [act(col(6 + n), rcol, F.Identity, [k_o4], scale=w, bias=col(5)) for n, w in enumerate((0.25, 1024.0, 1.0))]
+            t1 = vhold(T.xs[:, 0:224], T.d16[:], T.val0[:, 64:NP], [k_val, k_d16])
+            k_b = act(col(9), col(0), F.Identity, scale=-1.0)
+            k_pre = [act(T.pre2[:, 4:18], T.bas[:, 4:18], F.Copy, [k_bas]),
+                     act(T.bas[:, 24:33], T.c16[:, 8:17], F.Identity, scale=-1.0, bias=LIFT),
+                     act(T.pre2[:, 0:4], T.bas[:, 0:4], F.Identity, [k_b], bias=col(9))]
+        c5 = act(T.sp[:], T.pp[:, 0:C], F.Copy, [pp])
         if t == 0:
-            t1 = vhold(T.hold[:], T.d16[:], T.val0[:], k_val)
-            keep["c0"] = pick_codes("curp0", "clu0", 128, 8, lrp, [gotu[0], k_lrp])
-            c5 = scores()
-            t2 = vts(T.tint[:, 0:18], T.hold[:, 15:NP:16], T.ocol[:, 0:1], None, A.subtract, after=[t1])
-            k_lpj = vts(T.lpj[:, 0:18], T.hold[:, 15:NP:16], T.ocol[:, 0:1], 1.0 / 4096.0, A.subtract, A.mult)
-            t3 = vts(T.tand[:, 0:18], T.tint[:, 0:18], 2, 1023, A.logical_shift_right, A.bitwise_and, after=[t2])
-            k_lpi = vcp(T.lpi[:, 0:18], T.tand[:, 0:18], [t3])
-        c4 = act(T.spi[:], T.ss[:, 0:C + 8].indirect(T.lpi[:, 0:18]), F.Copy, [c1, k_lpi] + k_low)
-        c0 = vcp(T.so[:, 0:C].indirect(R("rk")[:, 0:12]), T.orow[:], [k_orow])
-        pd = [mm("pw%d" % b, "ce", 128 * b, cl, 0, C, qe) for b in range(4)]
-        c7 = [act(T.dd[:, b:4 * C:4], T["pw%d" % b][:, 0:C], F.Copy, [pd[b]], scale=0.5) for b in range(4)]
+            z2 = [zeros(2), zeros(1)]
+        c0 = vcp(T.so[:, 0:C].indirect(R("rk")[:, 0:12]), T.crow[:], [a9])
         if t == 0:
+            t2 = vts(T.tint[:, 0:14], T.xs[:, 15:224:16], col(4), None, A.subtract, after=[t1, k_o16])
+            k_lpj = vts(T.lpj[:, 0:14], T.xs[:, 15:224:16], col(4), 1.0 / 4096.0, A.subtract, A.mult)
+        c1 = vcount(T.hh[:, 0:K], T.so[:, 0:K], T.pats[:], LIFT, [c0, k_pats])
+        c2 = vhold(T.h4[:, 0:K], T.d4[:, 0:K], T.so[:, 0:K], k_d4)
+        if t == 0:
+            t3 = vts(T.tand[:, 0:14], T.tint[:, 0:14], 2, 1023, A.logical_shift_right, A.bitwise_and, after=[t2])
+        c1 = vts(T.rkp[:, 20:24], T.hh[:, 15:K:16], col(1), None, A.add, after=[c1])
+        if t == 0:
+            k_lpi = vcp(T.lpi[:, 0:14], T.tand[:, 0:14], [t3])
+            qe.append(unpack(3))
+        c1 = act(T.ss[:, 0:K], T.sc[:, 0:C].indirect(T.rkp[:, 20:24]), F.Copy, [c1])
+        pd = [mm("pw%d" % b, "ce", 128 * b, cl, 0, C, [qe[b]] + read) for b in range(4)]
+        c7 = [act(T.dd[:, 0:4 * C:4], T.pw0[:, 0:C], F.Copy, [pd[0]], scale=0.5)]
+        c8 = act(T.spi[:, 0:K], T.off16[:, 0:K], F.Identity, [c1], bias=T.ss[:, 0:1])
+        c4 = act(T.spi[:, 64:NP], T.ss[:].indirect(T.lpi[:, 0:14]), F.Copy, [c1, k_lpi] + k_acc)
+        c7 += [act(T.dd[:, b:4 * C:4], T["pw%d" % b][:, 0:C], F.Copy, [pd[b]], scale=0.5) for b in range(1, 4)]
+        if t == 0:
+            z2.append(zeros(3))
             need("sync", gotr)
             done("ldw", Y.dma_start(T.cwq[:].bitcast(dt.uint8), T.wc[:]), 16)
             ldw = done("ldw", Y.dma_start(T.cws[:], T.ws[:]), 16)
             ldv = done("ldv", Y.dma_start(T.vb[:], T.v[:]), 16)
-            k_c3 = act(T.ocol[:, 3:4], qcol, F.Identity, bias=T.ocol[:, 0:1])
-            k_c2 = act(T.ocol[:, 2:3], rcol, F.Identity, scale=1025.0)
-            k_pre = [act(T.pre[:, 12:16], T.crow[:, 0:64:16], F.Identity, bias=qcol),
-                     act(T.bas[:, 12:21], T.crow[:, 128:257:16], F.Identity, bias=T.ocol[:, 0:1]),
-                     act(T.pre[:, 16:30], T.crow[:, 64:NP:16], F.Identity, [k_c3], bias=T.ocol[:, 3:4])]
 
         d0 = vcp(T.es[:, 0:C].indirect(R("lrk")[:, 0:12]), T.sp[:], [gotr, c5])
-        c2 = vhold(T.h4[:, 0:K], T.d4[:, 0:K], T.so[:, 0:K], [c0] + k_d4)
-        d1 = [vtt(T.vv[:, 16 * a:16 * b], T.es[:, 0:C].indirect(T.lpj[:, a:b]), T.spi[:, 16 * a:16 * b], A.add, [d0, c4, k_lpj])
-              for a, b in ((0, 8), (8, 18))]
-        d2 = [vtt(T.sm[:, a:a + 128], T.vv[:, a:a + 128], T.m16[:, a:a + 128], A.mult, [d1[a // 128]]) for a in (0, 128)]
-        d3 = [vsum(T.hold[:, 0:128], T.nm16[:, 0:128], T.sm[:, 0:128], [d2[0]])]
-        c3 = vts(R("ol")[:, 0:16], T.h4[:, 3:K:4], T.ocol[:, 1:2], None, A.add, after=[c2, k_o4])
-        d3.append(vsum(T.hold[:, 128:256], T.nm16[:, 128:256], T.sm[:, 128:256], [d2[1]]))
+        c3 = vts(R("ol")[:, 0:16], T.h4[:, 3:K:4], col(6), 4.0, A.add, A.mult, after=[c2] + k_o4)
         send(R("lol")[:, 0:16], R("ol")[:, 0:16], "goto%d" % t, t, [c3])
         goto = ("goto%d" % t, nin[t])
         lo, hi = 16 * 7, 16 * 16
+        d2 = vtt(T.sm[:, 0:K], T.es[:, 0:K], T.spi[:, 0:K], A.add, [d0, c8])
+        d1 = vtt(T.vv[:, 64:NP], T.es[:, 0:C].indirect(T.lpj[:, 0:14]), T.spi[:, 64:NP], A.add, [c4, k_lpj])
+        d3 = vhold(T.hold[:, 0:K], T.new16[:, 0:K], T.sm[:, 0:K], [d2])
+        turn2 = [int(s[1]) for s in ORDER2 if str(s)[0] == "q"]
 
-        def between2(k):
-            if k == 5:
-                got["eq"] = vtt(T.eq[:, 0:hi - lo], T.vv[:, lo:hi], T.hold[:, lo:hi], A.is_equal, [d3[1]])
-            if k == 7:
-                got["cor"] = vsum(T.cor[:, 0:hi - lo], T.nm16[:, lo:hi], T.eq[:, 0:hi - lo], [got["eq"]])
-            if k == 9:
-                got["pre"] = vtt(T.pre[:, 19:28], T.bas[:, 12:21], T.cor[:, 15:hi - lo:16], A.subtract, [got["cor"]] + k_pre)
-
-        def tile2(n, toks, turn):
+        def tile2(n, got):
             skip = 0 if t == 0 or n == 3 else FROM2[4 * n] - BASE2[n]
             w = NP - BASE2[n] - skip
             o = MOFF2[n] + 4 * skip
-            q = vq("cmb", o // 4, w, T.mb[:, o:o + 4 * w], toks + z2)
+            q = vq("cmb", o // 4, w, T.mb[:, o:o + 4 * w], [got[j] for j in range(4 * n, 4 * n + 4)] + z2)
             if n < 3:
-                got["x"] = mm("pa", "cg", 0, "cmb", MOFF2[n] // 4, 128, [q], n == turn[0], n == turn[-2])
-            got["y"] = mm("pb", "cg", 0, "cmb", MOFF2[n] // 4 + 160 - BASE2[n], 128, [q], n == turn[0], n == turn[-1])
+                got["pa"] = mm("pa", "cg", 0, "cmb", MOFF2[n] // 4, 128, [q], n == turn2[0], n == turn2[-2])
+            return mm("pb", "cg", 0, "cmb", MOFF2[n] // 4 + 160 - BASE2[n], 128, [q], n == turn2[0], n == turn2[-1])
 
-        sums = compare(T.vv, NP, lambda k: T.hold[:, 16 * k + 15:16 * k + 16], FROM2, SUM2, BASE2, MOFF2, T.mb, 12,
-                       ON_SCALAR2, [d3[0], d1[1]] + z2, between2, tile2, TILES2)
-        d6 = vhold(T.hh[:, 64:192], T.d16[:, 0:128], T.pa[:, 0:128], [got["x"]])
-        d9 = vtt(T.cnt[:, 12:30], T.pre[:, 12:30], T.acc[:, 12:30], A.add, [got["pre"], sums])
-        d8 = vhold(T.hh[:, 192:NP], T.d16[:, 0:96], T.pb[:, 32:128], [got["y"]])
-        d10 = vtt(T.cnt[:, 16:30], T.cnt[:, 16:30], T.hh[:, 79:NP:16], A.subtract, [d6, d8, d9])
-        if t == 0:
-            k_valr = act(T.valr[:], T.val0[:], F.Identity, [k_c2], bias=T.ocol[:, 2:3])
-        d11 = vcp(T.rkp[:, 0:18], T.cnt[:, 12:30], [d10])
-        c6 = act(T.aa[:], state[:, 0:4 * C].indirect(R("ol")[:, 0:16]), F.Copy, [c3], scale=0.5)
-        e0 = act(T.ee[:], T.dd[:, 0:4 * C].indirect(R("lol")[:, 0:16]), F.Copy, [goto, c7[-1]])
-        if t == 0:
-            keep["s1"] = pick_scales("curp1", "clu1", 128, 8, lrp, [gotu[1]])
-        if t == ROUNDS - 1:
-            act(T.nrow[:, 0:FILL1], T.crow[:, 0:FILL1], F.Copy)
-            k_nrow = act(T.nrow[:, FILL1:NP], T.crow[:, FILL0:NP - 8], F.Copy)
-
-        e1 = vcp(T.xs[:, 0:NP].indirect(T.rkp[:, 0:18]), T.valr[:], [d11, k_valr])
+        put = lambda a, b, after: vcp(T.xs[:, 0:NP].indirect(T.rkp[:, a:b]), T.val0[:, 16 * a:16 * b], after)
+        got = counting(ORDER2, T.vv, NP, lambda k: T.hold[:, 16 * k + 15:16 * k + 16],
+                       lambda k, got: [d1, d3] if k < 4 else [got["hold"]] + z2, FROM2, SUM2, slot2, T.acc2, {
+            "mask": lambda got: vtt(T.sm[:, K:hi], T.vv[:, K:hi], T.off16[:, 0:hi - K], A.add, [d1]),
+            "hold": lambda got: vhold(T.hold[:, K:hi], T.new16[:, 0:hi - K], T.sm[:, K:hi], [got["mask"]]),
+            "eq": lambda got: vtt(T.eq[:, 0:hi - lo], T.vv[:, lo:hi], T.hold[:, lo:hi], A.is_equal, [got["hold"]]),
+            "cor": lambda got: vcount(T.cor[:, 0:hi - lo], T.off16[:, 0:hi - lo], T.eq[:, 0:hi - lo], 0.0, [got["eq"]]),
+            "pre": lambda got: vtt(T.pre2[:, 7:16], T.bas[:, 24:33], T.cor[:, 15:hi - lo:16], A.add, [got["cor"]] + k_pre),
+            "q0": lambda got: tile2(0, got), "q1": lambda got: tile2(1, got), "q2": lambda got: tile2(2, got),
+            "q3": lambda got: tile2(3, got),
+            "x0": lambda got: vtt(T.hh[:, 15:64:16], T.pre2[:, 0:4], T.acc2[:, 0:4], A.subtract, k_pre + sums(got, 0, 4)),
+            "x1": lambda got: vtt(T.pat[:, 79:192:16], T.pre2[:, 4:12], T.acc2[:, 4:12], A.subtract, [got["pre"]] + sums(got, 4, 12)),
+            "x2": lambda got: vtt(T.pat[:, 207:NP:16], T.pre2[:, 12:18], T.acc2[:, 12:18], A.subtract, [got["pre"]] + sums(got, 12, 16)),
+            "s1": lambda got: vcount(T.hh[:, 64:192], T.pa[:, 0:128], T.pat[:, 64:192], LIFT, [got["pa"], got["x1"]]),
+            "s2": lambda got: vcount(T.hh[:, 192:NP], T.pb[:, 32:128], T.pat[:, 192:NP], LIFT, [got["q3"], got["x2"]]),
+            "n1": lambda got: vts(T.rkp[:, 0:12], T.hh[:, 15:192:16], col(1), -1.0, A.add, A.mult, after=[got["x0"], got["s1"]]),
+            "n2": lambda got: vts(T.rkp[:, 12:18], T.hh[:, 207:NP:16], col(1), -1.0, A.add, A.mult, after=[got["s2"]]),
+            "put1": lambda got: put(0, 12, [got["n1"], k_row0]),
+            "put2": lambda got: put(12, 18, [got["n2"], got["put1"]])})
+        e1 = got["put2"]
         if t == 0:
             keep["c1"] = pick_codes("curp1", "clu1", 128, 8, lrp, [gotu[1]])
         if t == 1:
             qv = vq("cv", 0, 128, T.vb[:], [ldv])
-        e2 = vhold(T.h4[:], T.d4[:], T.xs[:, 0:C], [e1])
-        e4 = vts(T.tint[:], T.h4[:, 3:C:4], T.ocol[:, 1:2], None, A.add, after=[e2])
-        e3 = vts(T.offe[:], T.h4[:, 3:C:4], T.ocol[:, 1:2], 1.0 / 1024.0, A.add, A.mult)
-        e5 = vts(T.tand[:], T.tint[:], 1023, None, A.bitwise_and, after=[e4])
-        e6 = vcp(T.offa[:], T.tand[:], [e5])
+        c6 = act(T.aa[:], state[:, 0:4 * C].indirect(R("ol")[:, 0:16]), F.Copy, [c3], scale=0.5)
+        e0 = act(T.ee[:], T.dd[:, 0:4 * C].indirect(R("lol")[:, 0:16]), F.Copy, [goto, c7[-1]])
+        if t == 0:
+            keep["s1"] = pick_scales("curp1", "clu1", 128, 8, lrp, [gotu[1]])
+
+        def numbers(a, b):
+            if t == ROUNDS - 1:
+                keep["n"] = vcp(T.nout[:, 0:NP].indirect(T.rkp[:, a:b]), T.nrow[:, 16 * a:16 * b], [keep.get("n", k_nrow)])
+
+        e2 = vhold(T.hi[:], T.d4[:], T.xs[:, 0:C], [e1])
+        numbers(0, 4)
+        e3 = vts(T.offe[:], T.hi[:, 3:C:4], col(7), 1.0 / 1024.0, A.add, A.mult, after=[e2])
+        e5 = vts(T.tand[:], T.hi[:, 3:C:4], 1023, None, A.bitwise_and)
+        arrivals = lambda a, b: (T.eg[:, 16 * a:16 * b], T.ee[:, 0:4 * K].indirect(T.offe[:, a:b]))
+        f0 = vcp(*arrivals(*ZRUNS[0]), [e3, e0])
+        e6 = vts(T.offa[:], T.tand[:], rcol, None, A.add, after=[e5])
         zs = []
-        for a, b in ((0, 8), (8, 20), (20, 32), (32, 48)):
-            f0 = act(T.eg[:, 16 * a:16 * b], T.ee[:, 0:4 * K].indirect(T.offe[:, a:b]), F.Copy, [e3, e0])
+        for a, b in ZRUNS:
+            if zs:
+                f0 = act(*arrivals(a, b), F.Copy, [e3, e0])
             zs.append(vtt(T.zz[:, 16 * a:16 * b], T.aa[:, 0:4 * K].indirect(T.offa[:, a:b]), T.eg[:, 16 * a:16 * b], A.add,
                           [e6, f0, c6]))
-            if b == 32:
-                qz = vq("cz", 0, 128, T.zz[:, 0:512], zs)
-                pw = [mm("pw%d" % n, "cw", 128 * n, "cz", 0, 128, [qz, ldw]) for n in range(4)]
+            if a == 0:
+                qz = vq("cz", 0, 128, T.zz[:, 256:768], zs[:-1])
+                pw = {n: mm("pw%d" % n, "cw", 128 * n, "cz", 0, 128, [qz, ldw]) for n in (0, 2, 1, 3)}
 
-        qz = vq("cz", 128, 128, T.zz[:, 256:768], zs)
+        numbers(4, 8)
+        qz = vq("cz", 128, 128, T.zz[:, 0:512], zs)
+        numbers(8, 12)
         banks = ["pa", "pb", "pp", "py"]
-        pw += [mm(banks[n], "cw", 128 * n, "cz", 128, 128, [qz]) for n in range(4)]
+        pw2 = [mm(banks[n], "cw", 128 * n, "cz", 128, 128, [qz]) for n in range(4)]
         nxt = "ct%d" % (t + 1)
-        ts = []
-        for b in range(4):
-            r0 = act(T.rr[:, C * b:C * b + 128], T["pw%d" % b][:, 0:128], F.Relu, [pw[b]], scale=0.03125)
-            ts.append(vtt(T.tt[:, b:512:4], T.rr[:, C * b:C * b + 128], T.zz[:, b:512:4], A.add, [r0]))
-        for b in range(4):
-            r0 = act(T.rr[:, C * b + 128:C * b + C], T[banks[b]][:, 64:128], F.Relu, [pw[4 + b]], scale=0.03125)
-            ts.append(vtt(T.tt[:, 512 + b:768:4], T.rr[:, C * b + 128:C * b + C], T.zz[:, 512 + b:768:4], A.add, [r0]))
-            if b == 0 and t < ROUNDS - 1:
-                early = first_scores(nxt, [vq(nxt, 0, 128, T.tt[:, 0:512], ts[:4])])
+        r0 = {b: act(T.rr[:, 256 + b:768:4], T["pw%d" % b][:, 0:128], F.Relu, [pw[b]], scale=0.03125) for b in pw}
+        r1 = [act(T.rr[:, b:256:4], T[banks[b]][:, 0:64], F.Relu, [pw2[b]], scale=0.03125) for b in range(4)]
+        add = lambda a, b, s, after: vtt(T.tt[:, a:b:s], T.rr[:, a:b:s], T.zz[:, a:b:s], A.add, after)
+        ts = [add(256, 768, 4, [r0[0]]), add(258, 768, 4, [r0[2]]), add(257, 768, 2, [r0[1], r0[3]]), add(0, 256, 4, r1[:1])]
+        qt = vq(nxt, C, 128, T.tt[:, 256:768], ts[:3])
+        if t < ROUNDS - 1:
+            early = first_scores(nxt, C, [qt])
+            send_state(t + 1, C, 64, 128, [qt])
+        else:
+            early = [mm("pw0", "cv", 0, nxt, C, 128, [qt, qv])]
+        ts += [add(2, 256, 4, r1[:3]), add(1, 256, 2, r1)]
         state = T.tt
         if t < ROUNDS - 1:
-            cp0 = act(T.sc[:, 0:128], T.pw1[:, 0:128], F.Copy, [early[1]])
+            cp0 = act(T.sc[:, 64:C], T.pw1[:, 0:128], F.Copy, [early[1]])
             a0 = first_mask(early)
-            qt = vq(nxt, 64, 128, T.tt[:, 256:768], ts + [early[1]])
-        else:
-            qt = vq(nxt, 0, C, T.tt[:], ts)
+        numbers(12, 14)
+        w = 128 if t < ROUNDS - 1 else C
+        qt = vq(nxt, 0, w, T.tt[:, 0:4 * w], ts)
+        numbers(14, 18)
 
     ct = "ct%d" % ROUNDS
-    py = mm("pw0", "cv", 0, ct, 0, C, [qt, qv])
-    n0 = vcp(T.nout[:, 0:NP].indirect(T.rkp[:, 0:18]), T.nrow[:], [k_nrow])
+    py = mm("pw1", "cv", 0, ct, 0, 128, [qt])
+    yc = act(T.ysb[:, 64:C], T.pw0[:, 0:128], F.Copy, early)
+    need("sync", yc)
+    done("stored", Y.dma_start(T.y[:, 64:C], T.ysb[:, 64:C]), 16)
     need("sync", qt)
-    done("stored", Y.dma_start(T.oc[:], T[ct + "q"][:].bitcast(dt.uint8)), 16)
+    done("stored", Y.dma_start(T.oc[:], T[ct + "q"][:, 0:C].bitcast(dt.uint8)), 16)
     for k in range(4):
         done("stored", Y.dma_start(T.osc[4 * k:4 * k + 4, :], T[ct + "s"][32 * k:32 * k + 4, 0:C]), 16)
-    yc = act(T.ysb[:], T.pw0[:, 0:C], F.Copy, [py])
+    yc = act(T.ysb[:, 0:64], T.pw1[:, 0:64], F.Copy, [py])
     need("act", yc)
-    done("stored", S.dma_start(T.y[:], T.ysb[:]), 16)
-    need("sync", n0)
+    done("stored", S.dma_start(T.y[:, 0:64], T.ysb[:, 0:64]), 16)
+    need("sync", keep["n"])
     done("stored", Y.dma_start(T.ol[:], T.nout[0:128:16, 0:C]), 16)
     need("pool", ("sent", count["sent"]), ("pool", count["pool"]))
     need("sync", ("act", count["act"]), ("pe", count["pe"]), ("stored", count["stored"]))

@@ -4,9 +4,7 @@ from concourse.mybir import dt, AluOpType, ActivationFunctionType, AxisListType
 C, K, ROUNDS = 192, 64, 3
 STEP = [1, 2, 1]
 LENS = [K // (i + 1) for i in range(K)]
-NP = 288
-FILL0, FILL1 = 248, 256
-LOW = -2.0 ** 83
+PAIRS, NP = sum(LENS), 288
 HIGH = 2.0 ** 90
 RESET = 2.0 ** 96
 DROP = float(2 ** 19)
@@ -19,10 +17,12 @@ FROM2 = [64] * 4 + [96] * 2 + [112] + [16 * k for k in range(7, 16)]
 SUM2 = FROM2[:7] + [16 * k + 16 for k in range(7, 16)]
 BASE2 = [64, 64, 64, 160]
 MOFF2 = [0, 4 * 224, 4 * 448, 4 * 672]
-ORDER1 = [5, "copy", 6, "mask", 7, 10, "in1", "hold", "a0", 9, 8, 4, "b0", "in2", 3, 1, 2, "q12", "r4", "cor", "r10", "q0", "pre",
-          "x", "s1", "s0"]
-ORDER2 = ["a0", "a1", "b0", "mask", "b1", 2, "hold", 3, 10, 9, 4, 5, 7, 6, "eq", "q1", 11, 8, "q0", 14, "cor", "q2",
-          15, 13, "pre", 12, "x0", "x1", "q3", "s1", "x2", "n1", "s2", "put1", "n2", "put2"]
+ORDER0 = ["copy", "mask", 6, 5, 10, "hold", "a0", 8, 4, "in1", "b0", 3, 9, 7, 1, "in2", 2, "q12", "q0", "cor", "r10", "pre", "r2",
+          "s1", "x", "s0"]
+ORDER1 = ["copy", 10, 6, "mask", 5, "in1", "hold", 8, "a0", 7, "b0", 4, 9, 3, "in2", 1, 2, "q12", "q0", "cor", "r8", "r2", "pre",
+          "r10", "s1", "x", "s0"]
+ORDER2 = ["a0", "fall", "a1", "mask", "b0", 3, 4, "hold", "b1", 2, 6, 10, 7, 5, "eq", "q1", 8, 9, 11, "q0", "cor", "q2",
+          15, 13, 12, 14, "pre", "q3", "x1", "s1", "r13", "n1", "x2", "s2", "put1", "n2", "num", "put2"]
 
 ZRUNS = [(16, 22), (22, 36), (36, 48), (0, 8), (8, 16)]
 
@@ -43,14 +43,14 @@ for _n, _w, _k in [
         ("xb", 4 * C, BF), ("ub", 512, BF), ("vb", 512, BF),
         ("pbit", 8, I32), ("pcol", 8, F32), ("crow", C, F32), ("cm16", NP, BF), ("c16", 24, F32), ("dcol", 8, F32),
         ("off16", 224, BF), ("new16", C, BF), ("d16", 224, BF), ("d4", C, BF), ("ocol", 16, F32),
-        ("pat", NP, F32), ("pats", K, F32), ("nrow", NP, F32), ("val0", NP, F32),
-        ("lrep", 16, U16), ("lrp", 16, U16), ("lcmp", 16, U16), ("lpi", 16, U16), ("lpj", 16, U16),
-        ("tint", 48, I32), ("tand", 48, I32), ("gidx", 128, BF), ("gtile", 512, BF), ("etile", 520, BF),
+        ("pat", 128, F32), ("hp", NP, F32), ("cnt", 24, F32), ("nrow", NP, F32), ("val0", NP, F32),
+        ("own16", K, BF), ("lrep", 32, U16), ("lcmp", 16, U16), ("lpi", 16, U16), ("lpj", 16, U16),
+        ("tand", 48, I32), ("gidx", 128, BF), ("gtile", 512, BF), ("etile", 520, BF),
         ("sc", C, F32), ("sp", C, F32), ("sm", NP, F32), ("hold", NP, F32), ("eq", C, BF), ("cor", C, BF),
         ("ma", 4 * 448, BF), ("mb", 4 * 800, BF), ("junk", 16 * 224, BF), ("sg", 4 * 224, BF), ("hh", NP, F32),
         ("acc1", 16, F32), ("acc2", 24, F32), ("bas", 40, F32), ("pre1", 16, F32), ("pre2", 24, F32), ("rkp", 32, U16),
-        ("ss", K + 8, F32), ("so", C, F32), ("es", C, F32), ("spi", NP, F32), ("vv", NP, F32), ("xs", NP, F32),
-        ("h4", K, F32), ("hi", C, I32), ("offa", 48, U16), ("offe", 48, U16), ("nout", NP, F32), ("ysb", C, F32),
+        ("ss", K, F32), ("so", C, F32), ("es", C, F32), ("spi", NP, F32), ("vv", NP, F32), ("xs", NP, F32),
+        ("h4", K, F32), ("hi", 224, I32), ("offa", 48, U16), ("offe", 48, U16), ("nout", NP, F32), ("ysb", C, F32),
         ("eg", 4 * C, BF), ("rr", 4 * C, F32)]:
     _sb(_n, _w, _k)
 for _n, _w in [("u", 128), ("urep", 128), ("ucmp", 32), ("lu0", 32), ("lu1", 32), ("urp0", 128), ("urp1", 128),
@@ -68,7 +68,7 @@ for _t in range(ROUNDS):
 for _n in ["pa", "pb", "pp", "py", "pw0", "pw1", "pw2", "pw3"]:
     SCRATCH[_n] = ("psum", [128, 512], F32)
 
-SEMAPHORES = (["vec", "act", "pe", "pool", "sent", "ldx", "ldu", "ldw", "ldv", "stored", "gotu0", "gotu1"]
+SEMAPHORES = (["vec", "act", "pe", "pool", "sent", "ldx", "ldy", "ldu", "ldw", "ldv", "stored", "gotu0", "gotu1"]
               + ["%s%d" % (n, t) for n in ("gott", "gotr", "goto") for t in range(ROUNDS)])
 
 
@@ -119,6 +119,10 @@ def rank_program(g, core, T, topo):
         need("vec", *after)
         return done("vec", V.tensor_tensor_scan(out, d0, d1, 0.0, A.add, A.min))
 
+    def vfall(a, b, after=()):
+        need("vec", *after)
+        return done("vec", V.tensor_tensor_scan(T.hold[:, a:b], T.own16[:, 0:b - a], T.vv[:, a:b], 0.0, A.min, A.max))
+
     def vcount(out, d0, d1, start, after=()):
         need("vec", *after)
         return done("vec", V.tensor_tensor_scan(out, d0, d1, start, A.min, A.add))
@@ -144,6 +148,9 @@ def rank_program(g, core, T, topo):
 
     def pick_scales(dst, src, n, m, off, after=()):
         return act(T[dst + "s"][:, 0:n], T[src + "s"][:, 0:m].indirect(off), F.Copy, after)
+
+    def first_scores(ct, at, after):
+        return mm("pw0", "curep", 0, ct, at, 128, after), mm("pw1", "curep", 0, ct, at, 128)
 
     peer = [T.cores[rank ^ s] for s in STEP]
     kind = [0, 1, 0]
@@ -175,7 +182,8 @@ def rank_program(g, core, T, topo):
         return ("gotu%d" % h, nin[h])
 
     ldu = done("ldu", Y.dma_start(T.ub[:], T.u[:]), 16)
-    ldx = done("ldx", S.dma_start(T.xb[:], T.x[:]), 16)
+    ldx = done("ldx", S.dma_start(T.xb[:, 256:768], T.x[:, 256:768]), 16)
+    ldy = done("ldy", Y.dma_start(T.xb[:, 0:256], T.x[:, 0:256]), 16)
 
     k_p = done("pool", g.iota(T.pbit[:, 3:4], [[0, 1]], 0, 1))
     k_cm16 = iota(T.cm16[:], [[0, NP // 16], [1, 16]], 0, 0)
@@ -186,17 +194,15 @@ def rank_program(g, core, T, topo):
     runs, place, i = [], 0, 0
     while i < K:
         n = LENS.count(LENS[i])
-        if place == FILL0:
-            runs.append((FILL0, FILL1, [[0, FILL1 - FILL0]], 4 * K))
-            place = FILL1
         runs.append((place, place + n * LENS[i], [[4, n], [4096, LENS[i]]], 4 * i))
         place += n * LENS[i]
         i += n
+    runs.append((PAIRS, NP, [[0, NP - PAIRS]], 0))
 
     def pair_rows(n):
         return [iota(T.val0[:, a:b], pattern, base, 0) for a, b, pattern, base in [runs.pop() for _ in range(n)]][-1]
 
-    pair_rows(6)
+    pair_rows(3)
 
     pint = T.pbit[:, 3:4]
     z1 = [vset(T.ma[:, MOFF1[n]:MOFF1[n] + 4 * (FROM1[4 * n + 2] - BASE1[n])], 0.0) for n in range(3)]
@@ -206,35 +212,36 @@ def rank_program(g, core, T, topo):
     k_et0 = vset(T.etile[:], 0.0)
     k_col = vcp(T.pcol[:, 0:4], T.pbit[:, 0:4], bits)
     qcol, rcol, ccol, ncol = [T.pcol[:, n:n + 1] for n in range(4)]
-    lrep, lrp, lcmp = T.lrep[:, 0:8], T.lrp[:, 0:8], T.lcmp[:, 0:2]
+    lrep, lrp, lcmp = T.lrep[:, 0:8], T.lrep[:, 16:24], T.lcmp[:, 0:2]
     col = lambda n: T.ocol[:, n:n + 1]
-    k_acc = [vset(T.acc1[:], 0.0), vset(T.acc2[:], 0.0), vset(T.ss[:, K:K + 8], LOW)]
+    k_acc = [vset(T.acc1[:], 0.0), vset(T.acc2[:], 0.0)]
     k_lrep = vts(lrep, T.cm16[:, 0:8], 16.0, None, A.mult, after=[k_cm16])
     k_off = vts(T.off16[:], T.cm16[:, 0:224], qcol, HIGH, A.not_equal, A.mult, after=[k_col])
     k_new = vts(T.new16[:], T.cm16[:, 0:C], 0.0, RESET, A.is_equal, A.mult)
     k_lcmp = vts(lcmp, T.pcol[:, 0:2], 7.0, 16.0, A.min, A.mult)
-    k_lrp = vcp(lrp, T.cm16[:, 0:8])
-    k_dc = vts(T.dcol[:, 0:4], T.cm16[:, 0:4], ccol, 5 * DROP, A.is_equal, A.mult)
-    k_et = vts(T.etile[:, 3:512:4], T.crow[:, 0:128], ncol, None, A.is_equal, after=[k_et0, k_crow])
-    unpack = lambda b: vq("ce", 128 * b, 128, T.etile[:, 3 - b:515 - b], [k_et])
-    qe = [unpack(0)]
 
     k_s0 = act(col(0), qcol, F.Square, [k_col], scale=-32.0, bias=480.0)
     k_s2 = act(col(2), qcol, F.Identity, scale=SLOPE, bias=-SLOPE / 2)
-    k_s3 = act(col(3), qcol, F.Identity, scale=-1.0, bias=LIFT)
     k_o16 = act(col(4), qcol, F.Identity, scale=DROP, bias=-15 * DROP)
     k_s1 = act(col(1), col(0), F.Identity, [k_s0], bias=-LIFT)
-    k_pat = act(T.pat[:], T.cm16[:], F.Identity, [k_s2, k_cm16], scale=-SLOPE, bias=col(2))
-    k_d16 = act(T.d16[:], T.off16[:], F.Identity, [k_off], scale=-17 * DROP / HIGH, bias=16 * DROP)
+    k_pat = act(T.pat[:], T.cm16[:, 0:128], F.Identity, [k_s2, k_cm16], scale=-SLOPE, bias=col(2))
 
     qu = vq("cu", 0, 128, T.ub[:], [ldu])
-    k_gt = vts(T.gtile[:, 0:512:4], T.gidx[:], qcol, ncol, A.add, A.is_equal, after=[k_gi])
+    first = vq("ct0", C, 128, T.xb[:, 256:768], [ldx])
+    k_et = vts(T.etile[:, 3:512:4], T.crow[:, 0:128], ncol, None, A.is_equal, after=[k_et0, k_crow])
+    unpack = lambda b: vq("ce", 128 * b, 128, T.etile[:, 3 - b:515 - b], [k_et])
     ur_c = pick_codes("curep", "cu", 128, 128, lrep, [qu, k_lrep])
     ur_s = pick_scales("curep", "cu", 128, 128, lrep, [qu, k_lrep])
-    qt = vq("ct0", 0, C, T.xb[:], [ldx])
+    early = first_scores("ct0", C, [first, ur_c, ur_s])
+    k_gt = vts(T.gtile[:, 0:512:4], T.gidx[:], qcol, ncol, A.add, A.is_equal, after=[k_gi])
     uc_c = pick_codes("cucmp", "cu", 32, 128, lcmp, [k_lcmp])
     uc_s = pick_scales("cucmp", "cu", 32, 128, lcmp, [k_lcmp])
-    qe.append(unpack(1))
+    gotu = [send_u(kind[0], [uc_c, uc_s])]
+    qt = vq("ct0", 0, C, T.xb[:], [ldy])
+    k_lrp = vcp(lrp, T.cm16[:, 0:8])
+    k_dc = vts(T.dcol[:, 0:4], T.cm16[:, 0:4], ccol, 5 * DROP, A.is_equal, A.mult)
+    qe = [unpack(0)]
+    k_s3 = act(col(3), col(1), F.Identity, [k_s1], scale=-1.0, bias=qcol)
     k_gt = [act(T.gtile[:, b:512:4], T.gtile[:, 0:512:4], F.Copy, [k_gt]) for b in range(1, 4)]
 
     def counting(order, row, n, own, ready, frm, summ, slot, acc, named):
@@ -270,11 +277,9 @@ def rank_program(g, core, T, topo):
         return T.mb[:, o + 4 * a:o + 4 * b - 3:4]
 
     def zeros(n):
-        w = 4 * (FROM2[4 * n + 3] - BASE2[n])
-        return act(T.mb[:, MOFF2[n]:MOFF2[n] + w], T.etile[:, 0:w], F.Identity, [k_et], scale=0.0)
-
-    def first_scores(ct, at, after):
-        return mm("pw0", "curep", 0, ct, at, 128, after), mm("pw1", "curep", 0, ct, at, 128)
+        a = 4 * 800 if n == 4 else MOFF2[n]
+        w = 0 if n == 4 else 4 * (FROM2[4 * n + 3] - BASE2[n])
+        return act(T.mb[:, a - 32:a + w], T.etile[:, 0:w + 32], F.Identity, [k_et], scale=0.0)
 
     def first_mask(early):
         return vtt(T.sm[:, 64:C], T.pw0[:, 0:128], T.off16[:, 0:128], A.add, [early[0], k_off])
@@ -284,30 +289,22 @@ def rank_program(g, core, T, topo):
     for t in range(ROUNDS):
         R = lambda n: T["%s%d" % (n, t)]
         ct, cl = "ct%d" % t, "cl%d" % t
-        if t == 0:
-            gotu = [send_u(kind[0], [uc_c, uc_s])]
         send_state(t, 0, 0, 64 if t else C, [qt])
         gott = ("gott%d" % t, (4 if t else 2) * nin[t])
         if t == 0:
-            gotu.append(send_u(kind[1], []))
             k_val = pair_rows(len(runs) - 1)
-            k_row0 = pair_rows(1)
         if t == 1:
-            iota(T.nrow[:, 0:FILL1], [[1, FILL1]], 0, 0)
-            k_nrow = iota(T.nrow[:, FILL1:NP], [[1, NP - FILL1]], FILL0, 0)
+            k_nrow = iota(T.nrow[:], [[1, NP]], 0, 0)
 
-        if t == 0:
-            early = first_scores(ct, 64, [qt, ur_c, ur_s])
         sb = mm("pw2", "curep", 0, ct, 0, 128, [qt])
         sb2 = mm("pw3", "curep", 0, ct, 0, 128)
         if t == 0:
             cp0 = act(T.sc[:, 64:C], T.pw1[:, 0:128], F.Copy, [early[1]])
             a0 = first_mask(early)
-            qe.append(unpack(2))
-            k_bas = act(T.bas[:, 0:18], T.c16[:, 0:18], F.Identity, [k_s3, k_c16], scale=-1.0, bias=col(3))
-            k_pats = act(T.pats[:], T.cm16[:, 0:K], F.Identity, scale=-SLOPE, bias=col(2))
-            k_dd = act(T.dcol[:, 4:8], T.dcol[:, 0:4], F.Identity, [k_dc], bias=-DROP)
-            k_pats = act(T.pats[:, 15:K:16], T.c16[:, 0:4], F.Identity, [k_pats], scale=0.0, bias=LIFT)
+            qe.append(unpack(1))
+            k_pat = act(T.pat[:, 15:128:16], T.c16[:, 0:8], F.Identity, [k_pat, k_c16], scale=0.0, bias=LIFT)
+            k_bas = act(T.bas[:, 0:18], T.c16[:, 0:18], F.Identity, [k_s3], bias=col(3))
+            k_d16 = act(T.d16[:], T.off16[:], F.Identity, [k_off], scale=-17 * DROP / HIGH, bias=16 * DROP)
         a1 = vhold(T.hold[:, 64:C], T.new16[:, 0:128], T.sm[:, 64:C], [a0, k_new])
         if t == 0:
             qg = vq("cg", 0, 128, T.gtile[:], k_gt)
@@ -322,7 +319,7 @@ def rank_program(g, core, T, topo):
             got["pa"] = mm("pa", "cg", 0, "cma", 64, 128, [q], False, True)
             got["py"] = mm("py", "cg", 0, "cma", 0, 128)
 
-        got = counting(ORDER1, T.sc, C, lambda k: T.hold[:, 16 * k + 15:16 * k + 16],
+        got = counting(ORDER1 if t else ORDER0, T.sc, C, lambda k: T.hold[:, 16 * k + 15:16 * k + 16],
                        lambda k, got: [a1, cp0] + z1 + ([got["hold"]] if k < 4 else []) + ([got["copy"]] if k < 3 else []),
                        FROM1, FROM1, slot1, T.acc1, {
             "copy": lambda got: act(T.sc[:, 0:64], T.pw3[:, 0:64], F.Copy, [sb2]),
@@ -331,51 +328,56 @@ def rank_program(g, core, T, topo):
             "in1": lambda got: vtt(slot1(-1, 64, C), T.pw0[:, 0:128], T.hold[:, 64:C], A.is_gt, [a1]),
             "in2": lambda got: vtt(slot1(-1, 0, 64), T.pw2[:, 0:64], T.hold[:, 0:64], A.is_gt, [got["hold"]]),
             "cor": lambda got: vcount(T.cor[:], T.off16[:, 0:C], slot1(-1, 0, C), 0.0, [got["in1"], got["in2"]]),
-            "pre": lambda got: vtt(T.pre1[:, 0:12], T.bas[:, 0:12], T.cor[:, 15:C:16], A.subtract, [got["cor"], k_bas]),
+            "pre": lambda got: vtt(T.pre1[:, 0:12], T.bas[:, 0:12], T.cor[:, 15:C:16], A.add, [got["cor"], k_bas]),
             "q0": tile0, "q12": tiles12,
-            "x": lambda got: vtt(T.pat[:, 15:C:16], T.pre1[:, 0:12], T.acc1[:, 0:12], A.subtract, [got["pre"], k_pat] + sums(got, 0, 11)),
-            "s0": lambda got: vcount(T.hh[:, 0:64], T.py[:, 0:64], T.pat[:, 0:64], LIFT, [got["py"], got["x"]]),
-            "s1": lambda got: vcount(T.hh[:, 64:C], T.pa[:, 0:128], T.pat[:, 64:C], LIFT, [got["pa"], got["x"]])})
-        a7 = max(got["s0"], got["s1"])
+            "x": lambda got: vtt(T.cnt[:, 0:12], T.pre1[:, 0:12], T.acc1[:, 0:12], A.add, [got["pre"]] + sums(got, 0, 11)),
+            "s0": lambda got: vcount(T.hh[:, 0:64], T.py[:, 0:64], T.pat[:, 0:64], LIFT, [got["py"], k_pat]),
+            "s1": lambda got: vcount(T.hh[:, 64:C], T.pa[:, 0:128], T.pat[:], LIFT, [got["pa"], k_pat])})
+        a7 = max(got["s0"], got["s1"], got["x"])
         read = [got["in1"], got["in2"], got["copy"]]
         h = kind[t]
         if t == 0:
+            k_dd = act(T.dcol[:, 4:8], T.dcol[:, 0:4], F.Identity, [k_dc], bias=-DROP)
+            k_b = act(col(9), col(1), F.Identity, scale=-1.0)
             keep["s0"] = pick_scales("curp0", "clu0", 128, 8, lrp, [gotu[0], k_lrp])
             keep["c0"] = pick_codes("curp0", "clu0", 128, 8, lrp, [gotu[0], k_lrp])
-        a9 = vts(R("rk")[:, 0:12], T.hh[:, 15:C:16], col(1), -1.0, A.add, A.mult, after=[a7, k_s1])
+        a9 = vtt(R("rk")[:, 0:12], T.cnt[:, 0:12], T.hh[:, 15:C:16], A.subtract, [a7])
         send(R("lrk")[:, 0:12], R("rk")[:, 0:12], "gotr%d" % t, t, [a9])
         gotr = ("gotr%d" % t, nin[t])
+        if t == 0:
+            gotu.append(send_u(kind[1], []))
+            k_row0 = pair_rows(1)
 
         pp = mm("pp", "curp%d" % h, 0, cl, 0, C, [gott, keep["c%d" % h], keep["s%d" % h]])
         if t == 0:
             k_o4 = act(col(5), ccol, F.Identity, scale=-DROP, bias=3 * DROP)
             k_d4 = [act(T.d4[:, b:C:4], T.crow[:, 0:C // 4], F.Identity, [k_dd], scale=0.0, bias=T.dcol[:, 4 + b:5 + b])
                     for b in range(4)]
-            k_o4 = [act(col(6 + n), rcol, F.Identity, [k_o4], scale=w, bias=col(5)) for n, w in enumerate((0.25, 1024.0, 1.0))]
-            t1 = vhold(T.xs[:, 0:224], T.d16[:], T.val0[:, 64:NP], [k_val, k_d16])
-            k_b = act(col(9), col(0), F.Identity, scale=-1.0)
+            k_o4 = [act(col(6 + n), rcol, F.Identity, [k_o4], scale=w, bias=col(5)) for n, w in enumerate((0.25, 1024.0))]
+            t1 = vhold(T.hi[:], T.d16[:], T.val0[:, 64:NP], [k_val, k_d16])
+            k_own = act(T.own16[:], T.off16[:, 0:K], F.Identity, scale=2.0, bias=-HIGH)
             k_pre = [act(T.pre2[:, 4:18], T.bas[:, 4:18], F.Copy, [k_bas]),
-                     act(T.bas[:, 24:33], T.c16[:, 8:17], F.Identity, scale=-1.0, bias=LIFT),
-                     act(T.pre2[:, 0:4], T.bas[:, 0:4], F.Identity, [k_b], bias=col(9))]
+                     act(T.bas[:, 24:33], T.c16[:, 8:17], F.Identity, [k_b], bias=col(9)),
+                     act(T.pre2[:, 0:4], T.c16[:, 0:4], F.Identity, bias=qcol),
+                     act(T.hp[:, 15:64:16], T.c16[:, 0:4], F.Identity, scale=0.0)]
+            z2 = [zeros(1), zeros(4)]
         c5 = act(T.sp[:], T.pp[:, 0:C], F.Copy, [pp])
         if t == 0:
-            z2 = [zeros(2), zeros(1)]
+            z2.append(zeros(2))
         c0 = vcp(T.so[:, 0:C].indirect(R("rk")[:, 0:12]), T.crow[:], [a9])
         if t == 0:
-            t2 = vts(T.tint[:, 0:14], T.xs[:, 15:224:16], col(4), None, A.subtract, after=[t1, k_o16])
-            k_lpj = vts(T.lpj[:, 0:14], T.xs[:, 15:224:16], col(4), 1.0 / 4096.0, A.subtract, A.mult)
-        c1 = vcount(T.hh[:, 0:K], T.so[:, 0:K], T.pats[:], LIFT, [c0, k_pats])
+            t3 = vts(T.tand[:, 0:14], T.hi[:, 15:224:16], 2, 1023, A.logical_shift_right, A.bitwise_and, after=[t1])
+            k_lpj = vts(T.lpj[:, 0:14], T.hi[:, 15:224:16], col(4), 1.0 / 4096.0, A.subtract, A.mult, after=[k_o16])
+        c1 = vcount(T.hh[:, 0:K], T.so[:, 0:K], T.pat[:, 0:K], LIFT, [c0])
         c2 = vhold(T.h4[:, 0:K], T.d4[:, 0:K], T.so[:, 0:K], k_d4)
         if t == 0:
-            t3 = vts(T.tand[:, 0:14], T.tint[:, 0:14], 2, 1023, A.logical_shift_right, A.bitwise_and, after=[t2])
+            k_lpi = vcp(T.lpi[:, 0:14], T.tand[:, 0:14], [t3])
         c1 = vts(T.rkp[:, 20:24], T.hh[:, 15:K:16], col(1), None, A.add, after=[c1])
         if t == 0:
-            k_lpi = vcp(T.lpi[:, 0:14], T.tand[:, 0:14], [t3])
-            qe.append(unpack(3))
+            qe += [unpack(2), unpack(3)]
         c1 = act(T.ss[:, 0:K], T.sc[:, 0:C].indirect(T.rkp[:, 20:24]), F.Copy, [c1])
         pd = [mm("pw%d" % b, "ce", 128 * b, cl, 0, C, [qe[b]] + read) for b in range(4)]
         c7 = [act(T.dd[:, 0:4 * C:4], T.pw0[:, 0:C], F.Copy, [pd[0]], scale=0.5)]
-        c8 = act(T.spi[:, 0:K], T.off16[:, 0:K], F.Identity, [c1], bias=T.ss[:, 0:1])
         c4 = act(T.spi[:, 64:NP], T.ss[:].indirect(T.lpi[:, 0:14]), F.Copy, [c1, k_lpi] + k_acc)
         c7 += [act(T.dd[:, b:4 * C:4], T["pw%d" % b][:, 0:C], F.Copy, [pd[b]], scale=0.5) for b in range(1, 4)]
         if t == 0:
@@ -390,40 +392,46 @@ def rank_program(g, core, T, topo):
         send(R("lol")[:, 0:16], R("ol")[:, 0:16], "goto%d" % t, t, [c3])
         goto = ("goto%d" % t, nin[t])
         lo, hi = 16 * 7, 16 * 16
-        d2 = vtt(T.sm[:, 0:K], T.es[:, 0:K], T.spi[:, 0:K], A.add, [d0, c8])
+        d2 = vts(T.vv[:, 0:K], T.es[:, 0:K], T.ss[:, 0:1], None, A.add, after=[d0, c1])
         d1 = vtt(T.vv[:, 64:NP], T.es[:, 0:C].indirect(T.lpj[:, 0:14]), T.spi[:, 64:NP], A.add, [c4, k_lpj])
-        d3 = vhold(T.hold[:, 0:K], T.new16[:, 0:K], T.sm[:, 0:K], [d2])
+        d3 = vfall(0, K, [d2, k_own])
         turn2 = [int(s[1]) for s in ORDER2 if str(s)[0] == "q"]
 
         def tile2(n, got):
             skip = 0 if t == 0 or n == 3 else FROM2[4 * n] - BASE2[n]
-            w = NP - BASE2[n] - skip
+            w = (NP if t == 0 or n == 3 else PAIRS) - BASE2[n] - skip
             o = MOFF2[n] + 4 * skip
             q = vq("cmb", o // 4, w, T.mb[:, o:o + 4 * w], [got[j] for j in range(4 * n, 4 * n + 4)] + z2)
             if n < 3:
                 got["pa"] = mm("pa", "cg", 0, "cmb", MOFF2[n] // 4, 128, [q], n == turn2[0], n == turn2[-2])
             return mm("pb", "cg", 0, "cmb", MOFF2[n] // 4 + 160 - BASE2[n], 128, [q], n == turn2[0], n == turn2[-1])
 
+        def numbers(a, b):
+            if t == ROUNDS - 1:
+                keep["n"] = vcp(T.nout[:, 0:NP].indirect(T.rkp[:, a:b]), T.nrow[:, 16 * a:16 * b], [keep.get("n", k_nrow)])
+
         put = lambda a, b, after: vcp(T.xs[:, 0:NP].indirect(T.rkp[:, a:b]), T.val0[:, 16 * a:16 * b], after)
-        got = counting(ORDER2, T.vv, NP, lambda k: T.hold[:, 16 * k + 15:16 * k + 16],
-                       lambda k, got: [d1, d3] if k < 4 else [got["hold"]] + z2, FROM2, SUM2, slot2, T.acc2, {
-            "mask": lambda got: vtt(T.sm[:, K:hi], T.vv[:, K:hi], T.off16[:, 0:hi - K], A.add, [d1]),
-            "hold": lambda got: vhold(T.hold[:, K:hi], T.new16[:, 0:hi - K], T.sm[:, K:hi], [got["mask"]]),
+        got = counting(ORDER2, T.vv, PAIRS, lambda k: T.hold[:, 16 * k + 15:16 * k + 16],
+                       lambda k, got: [d1, d3] if k < 4 else [got["fall" if k < 7 else "hold"]] + z2, FROM2, SUM2, slot2, T.acc2, {
+            "fall": lambda got: vfall(K, lo, [d1]),
+            "mask": lambda got: vtt(T.sm[:, lo:hi], T.vv[:, lo:hi], T.off16[:, 0:hi - lo], A.add, [d1]),
+            "hold": lambda got: vhold(T.hold[:, lo:hi], T.new16[:, 0:hi - lo], T.sm[:, lo:hi], [got["mask"]]),
             "eq": lambda got: vtt(T.eq[:, 0:hi - lo], T.vv[:, lo:hi], T.hold[:, lo:hi], A.is_equal, [got["hold"]]),
             "cor": lambda got: vcount(T.cor[:, 0:hi - lo], T.off16[:, 0:hi - lo], T.eq[:, 0:hi - lo], 0.0, [got["eq"]]),
-            "pre": lambda got: vtt(T.pre2[:, 7:16], T.bas[:, 24:33], T.cor[:, 15:hi - lo:16], A.add, [got["cor"]] + k_pre),
+            "pre": lambda got: vtt(T.pre2[:, 7:16], T.bas[:, 24:33], T.cor[:, 15:hi - lo:16], A.subtract, [got["cor"]] + k_pre),
             "q0": lambda got: tile2(0, got), "q1": lambda got: tile2(1, got), "q2": lambda got: tile2(2, got),
             "q3": lambda got: tile2(3, got),
-            "x0": lambda got: vtt(T.hh[:, 15:64:16], T.pre2[:, 0:4], T.acc2[:, 0:4], A.subtract, k_pre + sums(got, 0, 4)),
-            "x1": lambda got: vtt(T.pat[:, 79:192:16], T.pre2[:, 4:12], T.acc2[:, 4:12], A.subtract, [got["pre"]] + sums(got, 4, 12)),
-            "x2": lambda got: vtt(T.pat[:, 207:NP:16], T.pre2[:, 12:18], T.acc2[:, 12:18], A.subtract, [got["pre"]] + sums(got, 12, 16)),
-            "s1": lambda got: vcount(T.hh[:, 64:192], T.pa[:, 0:128], T.pat[:, 64:192], LIFT, [got["pa"], got["x1"]]),
-            "s2": lambda got: vcount(T.hh[:, 192:NP], T.pb[:, 32:128], T.pat[:, 192:NP], LIFT, [got["q3"], got["x2"]]),
-            "n1": lambda got: vts(T.rkp[:, 0:12], T.hh[:, 15:192:16], col(1), -1.0, A.add, A.mult, after=[got["x0"], got["s1"]]),
-            "n2": lambda got: vts(T.rkp[:, 12:18], T.hh[:, 207:NP:16], col(1), -1.0, A.add, A.mult, after=[got["s2"]]),
+            "x1": lambda got: vtt(T.cnt[:, 0:12], T.pre2[:, 0:12], T.acc2[:, 0:12], A.add, [got["pre"]] + sums(got, 0, 12)),
+            "x2": lambda got: vtt(T.cnt[:, 12:18], T.pre2[:, 12:18], T.acc2[:, 12:18], A.add, [got["pre"]] + sums(got, 12, 16)),
+            "s1": lambda got: vcount(T.hp[:, 64:192], T.pa[:, 0:128], T.pat[:], LIFT, [got["pa"]]),
+            "s2": lambda got: vcount(T.hp[:, 192:NP], T.pb[:, 32:128], T.pat[:, 0:96], LIFT, [got["q3"]]),
+            "n1": lambda got: vtt(T.rkp[:, 0:12], T.cnt[:, 0:12], T.hp[:, 15:192:16], A.subtract, [got["x1"], got["s1"]]),
+            "n2": lambda got: vtt(T.rkp[:, 12:18], T.cnt[:, 12:18], T.hp[:, 207:NP:16], A.subtract, [got["x2"], got["s2"]]),
             "put1": lambda got: put(0, 12, [got["n1"], k_row0]),
+            "num": lambda got: numbers(0, 2),
             "put2": lambda got: put(12, 18, [got["n2"], got["put1"]])})
         e1 = got["put2"]
+        numbers(2, 4)
         if t == 0:
             keep["c1"] = pick_codes("curp1", "clu1", 128, 8, lrp, [gotu[1]])
         if t == 1:
@@ -433,17 +441,14 @@ def rank_program(g, core, T, topo):
         if t == 0:
             keep["s1"] = pick_scales("curp1", "clu1", 128, 8, lrp, [gotu[1]])
 
-        def numbers(a, b):
-            if t == ROUNDS - 1:
-                keep["n"] = vcp(T.nout[:, 0:NP].indirect(T.rkp[:, a:b]), T.nrow[:, 16 * a:16 * b], [keep.get("n", k_nrow)])
-
-        e2 = vhold(T.hi[:], T.d4[:], T.xs[:, 0:C], [e1])
-        numbers(0, 4)
+        e2 = vhold(T.hi[:, 0:C], T.d4[:], T.xs[:, 0:C], [e1])
+        numbers(4, 6)
         e3 = vts(T.offe[:], T.hi[:, 3:C:4], col(7), 1.0 / 1024.0, A.add, A.mult, after=[e2])
         e5 = vts(T.tand[:], T.hi[:, 3:C:4], 1023, None, A.bitwise_and)
         arrivals = lambda a, b: (T.eg[:, 16 * a:16 * b], T.ee[:, 0:4 * K].indirect(T.offe[:, a:b]))
         f0 = vcp(*arrivals(*ZRUNS[0]), [e3, e0])
         e6 = vts(T.offa[:], T.tand[:], rcol, None, A.add, after=[e5])
+        numbers(6, 8)
         zs = []
         for a, b in ZRUNS:
             if zs:
@@ -454,9 +459,9 @@ def rank_program(g, core, T, topo):
                 qz = vq("cz", 0, 128, T.zz[:, 256:768], zs[:-1])
                 pw = {n: mm("pw%d" % n, "cw", 128 * n, "cz", 0, 128, [qz, ldw]) for n in (0, 2, 1, 3)}
 
-        numbers(4, 8)
+        numbers(8, 10)
         qz = vq("cz", 128, 128, T.zz[:, 0:512], zs)
-        numbers(8, 12)
+        numbers(10, 14)
         banks = ["pa", "pb", "pp", "py"]
         pw2 = [mm(banks[n], "cw", 128 * n, "cz", 128, 128, [qz]) for n in range(4)]
         nxt = "ct%d" % (t + 1)
@@ -464,35 +469,40 @@ def rank_program(g, core, T, topo):
         r1 = [act(T.rr[:, b:256:4], T[banks[b]][:, 0:64], F.Relu, [pw2[b]], scale=0.03125) for b in range(4)]
         add = lambda a, b, s, after: vtt(T.tt[:, a:b:s], T.rr[:, a:b:s], T.zz[:, a:b:s], A.add, after)
         ts = [add(256, 768, 4, [r0[0]]), add(258, 768, 4, [r0[2]]), add(257, 768, 2, [r0[1], r0[3]]), add(0, 256, 4, r1[:1])]
-        qt = vq(nxt, C, 128, T.tt[:, 256:768], ts[:3])
-        if t < ROUNDS - 1:
-            early = first_scores(nxt, C, [qt])
-            send_state(t + 1, C, 64, 128, [qt])
-        else:
-            early = [mm("pw0", "cv", 0, nxt, C, 128, [qt, qv])]
-        ts += [add(2, 256, 4, r1[:3]), add(1, 256, 2, r1)]
+        rest = lambda: [add(2, 256, 4, r1[:3]), add(1, 256, 2, r1)]
         state = T.tt
         if t < ROUNDS - 1:
+            first = vq(nxt, C, 128, T.tt[:, 256:768], ts[:3])
+            early = first_scores(nxt, C, [first])
+            send_state(t + 1, C, 64, 128, [first])
+            ts += rest()
             cp0 = act(T.sc[:, 64:C], T.pw1[:, 0:128], F.Copy, [early[1]])
             a0 = first_mask(early)
-        numbers(12, 14)
-        w = 128 if t < ROUNDS - 1 else C
-        qt = vq(nxt, 0, w, T.tt[:, 0:4 * w], ts)
+        else:
+            ts += rest()
+            first = vq(nxt, C, 128, T.tt[:, 256:768], ts[:3])
+            early = [mm("pw0", "cv", 0, nxt, C, 128, [first, qv])]
+        qt = vq(nxt, 0, 128, T.tt[:, 0:512], ts)
         numbers(14, 18)
 
     ct = "ct%d" % ROUNDS
+
+    def store(q, out, in_, after):
+        need(q, after)
+        done("stored", queue[q].dma_start(out, in_), 16)
+
+    def store_state(a, b, n, after):
+        store("sync", T.oc[:, 4 * b:4 * (b + n)], T[ct + "q"][:, a:a + n].bitcast(dt.uint8), after)
+        for k in range(4):
+            store("sync", T.osc[4 * k:4 * k + 4, b:b + n], T[ct + "s"][32 * k:32 * k + 4, a:a + n], after)
+
     py = mm("pw1", "cv", 0, ct, 0, 128, [qt])
-    yc = act(T.ysb[:, 64:C], T.pw0[:, 0:128], F.Copy, early)
-    need("sync", yc)
-    done("stored", Y.dma_start(T.y[:, 64:C], T.ysb[:, 64:C]), 16)
-    need("sync", qt)
-    done("stored", Y.dma_start(T.oc[:], T[ct + "q"][:, 0:C].bitcast(dt.uint8)), 16)
-    for k in range(4):
-        done("stored", Y.dma_start(T.osc[4 * k:4 * k + 4, :], T[ct + "s"][32 * k:32 * k + 4, 0:C]), 16)
-    yc = act(T.ysb[:, 0:64], T.pw1[:, 0:64], F.Copy, [py])
-    need("act", yc)
-    done("stored", S.dma_start(T.y[:, 0:64], T.ysb[:, 0:64]), 16)
-    need("sync", keep["n"])
-    done("stored", Y.dma_start(T.ol[:], T.nout[0:128:16, 0:C]), 16)
+    store_state(C, 64, 128, first)
+    ya = act(T.ysb[:, 64:C], T.pw0[:, 0:128], F.Copy, early)
+    yb = act(T.ysb[:, 0:64], T.pw1[:, 0:64], F.Copy, [py])
+    store("act", T.y[:, 64:C], T.ysb[:, 64:C], ya)
+    store("act", T.y[:, 0:64], T.ysb[:, 0:64], yb)
+    store_state(0, 0, 64, qt)
+    store("sync", T.ol[:], T.nout[0:128:16, 0:C], keep["n"])
     need("pool", ("sent", count["sent"]), ("pool", count["pool"]))
     need("sync", ("act", count["act"]), ("pe", count["pe"]), ("stored", count["stored"]))

from concourse.bass import DstId, RemoteDMATransfer
from concourse.mybir import dt, AluOpType, ActivationFunctionType, AxisListType

C, K, ROUNDS = 192, 64, 3
STEP = [1, 2, 1]
LENS = [K // (i + 1) for i in range(K)]
PAIRS, NP = sum(LENS), 288
HIGH = 2.0 ** 90
RESET = 2.0 ** 96
DROP = float(2 ** 19)
SLOPE, LIFT = 2048.0, float(2 ** 18)

FROM1 = [16 * k + 16 for k in range(11)]
BASE1 = [0, 64, 64]
MOFF1 = [0, 4 * 320, 4 * 192]
FROM2 = [64] * 4 + [96] * 2 + [112] + [16 * k for k in range(7, 16)]
SUM2 = FROM2[:7] + [16 * k + 16 for k in range(7, 16)]
BASE2 = [64, 64, 64, 160]
MOFF2 = [0, 4 * 224, 4 * 448, 4 * 672]
ORDER0 = ["copy", "mask", 6, 5, 10, "hold", "a0", 8, 4, "in1", "b0", 3, 9, 7, 1, "in2", 2, "q12", "q0", "cor", "r10", "pre", "r2",
          "s1", "x", "s0"]
ORDER1 = ["copy", 10, 6, "mask", 5, "in1", "hold", 8, "a0", 7, "b0", 4, 9, 3, "in2", 1, 2, "q12", "q0", "cor", "r8", "r2", "pre",
          "r10", "s1", "x", "s0"]
ORDER2 = ["a0", "fall", "a1", "mask", "b0", 3, 4, "hold", "b1", 2, 6, 10, 7, 5, "eq", "q1", 8, 9, 11, "q0", "cor", "q2",
          15, 13, 12, 14, "pre", "q3", "x1", "s1", "r13", "n1", "x2", "s2", "put1", "n2", "num", "put2"]

ZRUNS = [(16, 22), (22, 36), (36, 48), (0, 8), (8, 16)]

Q4, U8, BF, F32, I32, U16 = "float8_e4m3fn_x4", "uint8", "bfloat16", "float32", "int32", "uint16"
SCRATCH = {}


def _sb(name, n, kind):
    SCRATCH[name] = ("sbuf", [128, n], kind)


def _mx(name, n):
    _sb(name + "q", n, Q4)
    _sb(name + "s", n, U8)


for _n, _w, _k in [
        ("xb", 4 * C, BF), ("ub", 512, BF), ("vb", 512, BF),
        ("pbit", 8, I32), ("pcol", 8, F32), ("crow", C, F32), ("cm16", NP, BF), ("c16", 24, F32), ("dcol", 8, F32),
        ("off16", 224, BF), ("new16", C, BF), ("d16", 224, BF), ("d4", C, BF), ("ocol", 16, F32),
        ("pat", 128, F32), ("hp", NP, F32), ("cnt", 24, F32), ("nrow", NP, F32), ("val0", NP, F32),
        ("own16", K, BF), ("lrep", 32, U16), ("lcmp", 16, U16), ("lpi", 16, U16), ("lpj", 16, U16),
        ("tand", 48, I32), ("gidx", 128, BF), ("gtile", 512, BF), ("etile", 520, BF),
        ("sc", C, F32), ("sp", C, F32), ("sm", NP, F32), ("hold", NP, F32), ("eq", C, BF), ("cor", C, BF),
        ("ma", 4 * 448, BF), ("mb", 4 * 800, BF), ("junk", 16 * 224, BF), ("sg", 4 * 224, BF), ("hh", NP, F32),
        ("acc1", 16, F32), ("acc2", 24, F32), ("bas", 40, F32), ("pre1", 16, F32), ("pre2", 24, F32), ("rkp", 32, U16),
        ("ss", K, F32), ("so", C, F32), ("es", C, F32), ("spi", NP, F32), ("vv", NP, F32), ("xs", NP, F32),
        ("h4", K, F32), ("hi", 224, I32), ("offa", 48, U16), ("offe", 48, U16), ("nout", NP, F32), ("ysb", C, F32),
        ("eg", 4 * C, BF), ("rr", 4 * C, F32)]:
    _sb(_n, _w, _k)
for _n, _w in [("u", 128), ("urep", 128), ("ucmp", 32), ("lu0", 32), ("lu1", 32), ("urp0", 128), ("urp1", 128),
               ("v", 128), ("w", 512), ("e", 512), ("g", 128), ("ma", 448), ("mb", 800)]:
    _mx("c" + _n, _w)
for _t in range(ROUNDS + 1):
    _mx("ct%d" % _t, C + 128)
_mx("cz", 256)
for _n, _w, _k in [("zz", 4 * C, BF), ("dd", 4 * C, BF), ("aa", 4 * K, BF), ("ee", 4 * K, BF), ("tt", 4 * C, BF)]:
    _sb(_n, _w, _k)
for _t in range(ROUNDS):
    _mx("cl%d" % _t, C)
    for _n, _w, _k in [("rk", 16, U16), ("lrk", 16, U16), ("ol", 16, U16), ("lol", 16, U16)]:
        _sb("%s%d" % (_n, _t), _w, _k)
for _n in ["pa", "pb", "pp", "py", "pw0", "pw1", "pw2", "pw3"]:
    SCRATCH[_n] = ("psum", [128, 512], F32)

SEMAPHORES = (["vec", "act", "pe", "pool", "sent", "ldx", "ldy", "ldu", "ldw", "ldv", "stored", "gotu0", "gotu1"]
              + ["%s%d" % (n, t) for n in ("gott", "gotr", "goto") for t in range(ROUNDS)])


def rank_program(g, core, T, topo):
    rank = T.rank_of(core)
    if rank is None:
        return
    A, F = AluOpType, ActivationFunctionType
    V, S, P, Y = g.vector, g.scalar, g.tensor, g.sync
    queue = {"vec": V, "act": S, "pe": P, "pool": g, "sync": Y}
    count = {}
    seen = {q: {} for q in queue}

    def need(q, *toks):
        for sem, val in toks:
            if seen[q].get(sem, 0) < val:
                queue[q].wait_ge(T.sem[sem], val)
                seen[q][sem] = val

    def done(sem, inst, n=1):
        inst.then_inc(T.sem[sem], n)
        count[sem] = count.get(sem, 0) + n
        return (sem, count[sem])

    def vts(out, in0, s1, s2, op0, op1=None, after=()):
        need("vec", *after)
        if op1 is None:
            return done("vec", V.tensor_scalar(out, in0, s1, None, op0))
        return done("vec", V.tensor_scalar(out, in0, s1, s2, op0, op1))

    def vtt(out, in0, in1, op, after=()):
        need("vec", *after)
        return done("vec", V.tensor_tensor(out, in0, in1, op))

    def vcp(out, in_, after=()):
        need("vec", *after)
        return done("vec", V.tensor_copy(out, in_))

    def vset(out, value, after=()):
        need("vec", *after)
        return done("vec", V.memset(out, value))

    def vred(out, in_, after=()):
        need("vec", *after)
        return done("vec", V.tensor_reduce(out, in_, AxisListType.X, A.add))

    def vhold(out, d0, d1, after=()):
        need("vec", *after)
        return done("vec", V.tensor_tensor_scan(out, d0, d1, 0.0, A.add, A.min))

    def vfall(a, b, after=()):
        need("vec", *after)
        return done("vec", V.tensor_tensor_scan(T.hold[:, a:b], T.own16[:, 0:b - a], T.vv[:, a:b], 0.0, A.min, A.max))

    def vcount(out, d0, d1, start, after=()):
        need("vec", *after)
        return done("vec", V.tensor_tensor_scan(out, d0, d1, start, A.min, A.add))

    def vq(name, a, n, in_, after=()):
        need("vec", *after)
        return done("vec", V.quantize_mx(T[name + "q"][:, a:a + n], T[name + "s"][:, a:a + n], in_))

    def act(out, in_, func, after=(), **kw):
        need("act", *after)
        return done("act", S.activation(out, in_, func, **kw))

    def mm(out, lhs, a, rhs, b, n, after=(), start=True, stop=True):
        need("pe", *after)
        return done("pe", P.matmul_mx(T[out][:, 0:n], T[lhs + "q"][:, a:a + 128], T[lhs + "s"][:, a:a + 128],
                                      T[rhs + "q"][:, b:b + n], T[rhs + "s"][:, b:b + n], start, stop))

    def iota(out, pattern, base, cm):
        return done("pool", g.iota(out, pattern, base, cm, allow_small_or_imprecise_dtypes=True))

    def pick_codes(dst, src, n, m, off, after=()):
        return vcp(T[dst + "q"][:, 0:n].bitcast(dt.uint32), T[src + "q"][:, 0:m].bitcast(dt.uint32).indirect(off), after)

    def pick_scales(dst, src, n, m, off, after=()):
        return act(T[dst + "s"][:, 0:n], T[src + "s"][:, 0:m].indirect(off), F.Copy, after)

    def first_scores(ct, at, after):
        return mm("pw0", "curep", 0, ct, at, 128, after), mm("pw1", "curep", 0, ct, at, 128)

    peer = [T.cores[rank ^ s] for s in STEP]
    kind = [0, 1, 0]
    nen = [len(topo.engines(core, c)) for c in peer]
    nin = [len(topo.engines(c, core)) for c in peer]

    def send(out, in_, sem, t, after):
        need("pool", *after)
        rid, pid = topo.addr(peer[t])[0:2]
        g.remote_dma(out, in_, T.sem[sem], T.sem["sent"], pid, rid, topo.mask(core, peer[t]))
        count["sent"] = count.get("sent", 0) + nen[t]

    def send_state(t, a, b, n, after):
        src, dst = "ct%d" % t, "cl%d" % t
        send(T[dst + "q"][:, b:b + n].bitcast(dt.uint8), T[src + "q"][:, a:a + n].bitcast(dt.uint8), "gott%d" % t, t, after)
        send(T[dst + "s"][:, b:b + n], T[src + "s"][:, a:a + n], "gott%d" % t, t, after)

    def send_u(h, after):
        need("pool", *after)
        rid, pid = topo.addr(peer[h])[0:2]
        eng = topo.engines(core, peer[h])
        half = len(eng) // 2
        g.remote_dma_fused(
            [RemoteDMATransfer(dst_ids=[DstId(rid=rid, pnc=pid)], dma_engine_mask=sum(1 << x for x in e),
                               remote_sem=T.sem["gotu%d" % h], src=src, dst=dst)
             for src, dst, e in ((T.cucmpq[:, 0:8].bitcast(dt.uint8), T["clu%dq" % h][:, 0:8].bitcast(dt.uint8), eng[:half]),
                                 (T.cucmps[:], T["clu%ds" % h][:], eng[half:]))], local_sem=T.sem["sent"])
        count["sent"] = count.get("sent", 0) + len(eng)
        return ("gotu%d" % h, nin[h])

    ldu = done("ldu", Y.dma_start(T.ub[:], T.u[:]), 16)
    ldx = done("ldx", S.dma_start(T.xb[:, 256:768], T.x[:, 256:768]), 16)
    ldy = done("ldy", Y.dma_start(T.xb[:, 0:256], T.x[:, 0:256]), 16)

    k_p = done("pool", g.iota(T.pbit[:, 3:4], [[0, 1]], 0, 1))
    k_cm16 = iota(T.cm16[:], [[0, NP // 16], [1, 16]], 0, 0)
    k_crow = iota(T.crow[:], [[1, C]], 0, 0)
    k_gi = iota(T.gidx[:], [[16, 8], [0, 16]], 0, 0)
    k_c16 = iota(T.c16[:], [[16, 24]], 0, 0)

    runs, place, i = [], 0, 0
    while i < K:
        n = LENS.count(LENS[i])
        runs.append((place, place + n * LENS[i], [[4, n], [4096, LENS[i]]], 4 * i))
        place += n * LENS[i]
        i += n
    runs.append((PAIRS, NP, [[0, NP - PAIRS]], 0))

    def pair_rows(n):
        return [iota(T.val0[:, a:b], pattern, base, 0) for a, b, pattern, base in [runs.pop() for _ in range(n)]][-1]

    pair_rows(3)

    pint = T.pbit[:, 3:4]
    z1 = [vset(T.ma[:, MOFF1[n]:MOFF1[n] + 4 * (FROM1[4 * n + 2] - BASE1[n])], 0.0) for n in range(3)]
    bits = [vts(T.pbit[:, 0:1], pint, 15, None, A.bitwise_and, after=[k_p]),
            vts(T.pbit[:, 1:2], pint, 3, None, A.bitwise_and),
            vts(T.pbit[:, 2:3], pint, 2, 3, A.logical_shift_right, A.bitwise_and)]
    k_et0 = vset(T.etile[:], 0.0)
    k_col = vcp(T.pcol[:, 0:4], T.pbit[:, 0:4], bits)
    qcol, rcol, ccol, ncol = [T.pcol[:, n:n + 1] for n in range(4)]
    lrep, lrp, lcmp = T.lrep[:, 0:8], T.lrep[:, 16:24], T.lcmp[:, 0:2]
    col = lambda n: T.ocol[:, n:n + 1]
    k_acc = [vset(T.acc1[:], 0.0), vset(T.acc2[:], 0.0)]
    k_lrep = vts(lrep, T.cm16[:, 0:8], 16.0, None, A.mult, after=[k_cm16])
    k_off = vts(T.off16[:], T.cm16[:, 0:224], qcol, HIGH, A.not_equal, A.mult, after=[k_col])
    k_new = vts(T.new16[:], T.cm16[:, 0:C], 0.0, RESET, A.is_equal, A.mult)
    k_lcmp = vts(lcmp, T.pcol[:, 0:2], 7.0, 16.0, A.min, A.mult)

    k_s0 = act(col(0), qcol, F.Square, [k_col], scale=-32.0, bias=480.0)
    k_s2 = act(col(2), qcol, F.Identity, scale=SLOPE, bias=-SLOPE / 2)
    k_o16 = act(col(4), qcol, F.Identity, scale=DROP, bias=-15 * DROP)
    k_s1 = act(col(1), col(0), F.Identity, [k_s0], bias=-LIFT)
    k_pat = act(T.pat[:], T.cm16[:, 0:128], F.Identity, [k_s2, k_cm16], scale=-SLOPE, bias=col(2))

    qu = vq("cu", 0, 128, T.ub[:], [ldu])
    first = vq("ct0", C, 128, T.xb[:, 256:768], [ldx])
    k_et = vts(T.etile[:, 3:512:4], T.crow[:, 0:128], ncol, None, A.is_equal, after=[k_et0, k_crow])
    unpack = lambda b: vq("ce", 128 * b, 128, T.etile[:, 3 - b:515 - b], [k_et])
    ur_c = pick_codes("curep", "cu", 128, 128, lrep, [qu, k_lrep])
    ur_s = pick_scales("curep", "cu", 128, 128, lrep, [qu, k_lrep])
    early = first_scores("ct0", C, [first, ur_c, ur_s])
    k_gt = vts(T.gtile[:, 0:512:4], T.gidx[:], qcol, ncol, A.add, A.is_equal, after=[k_gi])
    uc_c = pick_codes("cucmp", "cu", 32, 128, lcmp, [k_lcmp])
    uc_s = pick_scales("cucmp", "cu", 32, 128, lcmp, [k_lcmp])
    gotu = [send_u(kind[0], [uc_c, uc_s])]
    qt = vq("ct0", 0, C, T.xb[:], [ldy])
    k_lrp = vcp(lrp, T.cm16[:, 0:8])
    k_dc = vts(T.dcol[:, 0:4], T.cm16[:, 0:4], ccol, 5 * DROP, A.is_equal, A.mult)
    qe = [unpack(0)]
    k_s3 = act(col(3), col(1), F.Identity, [k_s1], scale=-1.0, bias=qcol)
    k_gt = [act(T.gtile[:, b:512:4], T.gtile[:, 0:512:4], F.Copy, [k_gt]) for b in range(1, 4)]

    def counting(order, row, n, own, ready, frm, summ, slot, acc, named):
        got = {}
        for s in order:
            k = s if s in range(len(frm)) else int(s[1:]) if s[0] in "abr" and s[1:].isdigit() else None
            if k is None:
                got[s] = named[s](got)
            elif k == s:
                got[k] = vts(slot(k, frm[k], n), row[:, frm[k]:n], own(k), None, A.is_gt, after=ready(k, got))
                if "r%d" % k not in order:
                    got["r%d" % k] = act(T.junk[:, 224 * k:224 * k + n - summ[k]], slot(k, summ[k], n), F.Identity, [got[k]],
                                         accum_out=acc[:, k:k + 1])
            elif s[0] == "r":
                got[s] = vred(acc[:, k:k + 1], slot(k, summ[k], n), [got[k]] + k_acc)
            elif s[0] == "a":
                got[s] = act(T.sg[:, 224 * k:224 * k + n - frm[k]], row[:, frm[k]:n], F.Sign, ready(k, got), scale=-1.0, bias=own(k))
            else:
                got[k] = got["r%d" % k] = act(slot(k, frm[k], n), T.sg[:, 224 * k:224 * k + n - frm[k]], F.Relu, [got["a%d" % k]],
                                              scale=-1.0, accum_out=acc[:, k:k + 1])
        return got

    def sums(got, a, b):
        return [got["r%d" % k] for k in range(a, b)]

    def slot1(k, a, b):
        n = (k + 1) // 4
        o = MOFF1[n] + (k + 1) % 4 - 4 * BASE1[n]
        return T.ma[:, o + 4 * a:o + 4 * b - 3:4]

    def slot2(k, a, b):
        o = MOFF2[k // 4] + k % 4 - 4 * BASE2[k // 4]
        return T.mb[:, o + 4 * a:o + 4 * b - 3:4]

    def zeros(n):
        a = 4 * 800 if n == 4 else MOFF2[n]
        w = 0 if n == 4 else 4 * (FROM2[4 * n + 3] - BASE2[n])
        return act(T.mb[:, a - 32:a + w], T.etile[:, 0:w + 32], F.Identity, [k_et], scale=0.0)

    def first_mask(early):
        return vtt(T.sm[:, 64:C], T.pw0[:, 0:128], T.off16[:, 0:128], A.add, [early[0], k_off])

    state = T.xb
    keep = {}
    for t in range(ROUNDS):
        R = lambda n: T["%s%d" % (n, t)]
        ct, cl = "ct%d" % t, "cl%d" % t
        send_state(t, 0, 0, 64 if t else C, [qt])
        gott = ("gott%d" % t, (4 if t else 2) * nin[t])
        if t == 0:
            k_val = pair_rows(len(runs) - 1)
        if t == 1:
            k_nrow = iota(T.nrow[:], [[1, NP]], 0, 0)

        sb = mm("pw2", "curep", 0, ct, 0, 128, [qt])
        sb2 = mm("pw3", "curep", 0, ct, 0, 128)
        if t == 0:
            cp0 = act(T.sc[:, 64:C], T.pw1[:, 0:128], F.Copy, [early[1]])
            a0 = first_mask(early)
            qe.append(unpack(1))
            k_pat = act(T.pat[:, 15:128:16], T.c16[:, 0:8], F.Identity, [k_pat, k_c16], scale=0.0, bias=LIFT)
            k_bas = act(T.bas[:, 0:18], T.c16[:, 0:18], F.Identity, [k_s3], bias=col(3))
            k_d16 = act(T.d16[:], T.off16[:], F.Identity, [k_off], scale=-17 * DROP / HIGH, bias=16 * DROP)
        a1 = vhold(T.hold[:, 64:C], T.new16[:, 0:128], T.sm[:, 64:C], [a0, k_new])
        if t == 0:
            qg = vq("cg", 0, 128, T.gtile[:], k_gt)

        def tiles12(got):
            a = MOFF1[2] // 4 + (64 if t else 0)
            q = vq("cma", a, 448 - a, T.ma[:, 4 * a:4 * 448], [got[j] for j in range(3, 11)] + z1)
            return [mm("pa", "cg", 0, "cma", MOFF1[n] // 4, 128, [q, qg], n == 2, False) for n in (2, 1)]

        def tile0(got):
            q = vq("cma", 0, C, T.ma[:, 0:4 * C], [got[j] for j in (0, 1, 2, "in1", "in2")] + z1)
            got["pa"] = mm("pa", "cg", 0, "cma", 64, 128, [q], False, True)
            got["py"] = mm("py", "cg", 0, "cma", 0, 128)

        got = counting(ORDER1 if t else ORDER0, T.sc, C, lambda k: T.hold[:, 16 * k + 15:16 * k + 16],
                       lambda k, got: [a1, cp0] + z1 + ([got["hold"]] if k < 4 else []) + ([got["copy"]] if k < 3 else []),
                       FROM1, FROM1, slot1, T.acc1, {
            "copy": lambda got: act(T.sc[:, 0:64], T.pw3[:, 0:64], F.Copy, [sb2]),
            "mask": lambda got: vtt(T.sm[:, 0:64], T.pw2[:, 0:64], T.off16[:, 0:64], A.add, [sb]),
            "hold": lambda got: vhold(T.hold[:, 0:64], T.new16[:, 0:64], T.sm[:, 0:64], [got["mask"]]),
            "in1": lambda got: vtt(slot1(-1, 64, C), T.pw0[:, 0:128], T.hold[:, 64:C], A.is_gt, [a1]),
            "in2": lambda got: vtt(slot1(-1, 0, 64), T.pw2[:, 0:64], T.hold[:, 0:64], A.is_gt, [got["hold"]]),
            "cor": lambda got: vcount(T.cor[:], T.off16[:, 0:C], slot1(-1, 0, C), 0.0, [got["in1"], got["in2"]]),
            "pre": lambda got: vtt(T.pre1[:, 0:12], T.bas[:, 0:12], T.cor[:, 15:C:16], A.add, [got["cor"], k_bas]),
            "q0": tile0, "q12": tiles12,
            "x": lambda got: vtt(T.cnt[:, 0:12], T.pre1[:, 0:12], T.acc1[:, 0:12], A.add, [got["pre"]] + sums(got, 0, 11)),
            "s0": lambda got: vcount(T.hh[:, 0:64], T.py[:, 0:64], T.pat[:, 0:64], LIFT, [got["py"], k_pat]),
            "s1": lambda got: vcount(T.hh[:, 64:C], T.pa[:, 0:128], T.pat[:], LIFT, [got["pa"], k_pat])})
        a7 = max(got["s0"], got["s1"], got["x"])
        read = [got["in1"], got["in2"], got["copy"]]
        h = kind[t]
        if t == 0:
            k_dd = act(T.dcol[:, 4:8], T.dcol[:, 0:4], F.Identity, [k_dc], bias=-DROP)
            k_b = act(col(9), col(1), F.Identity, scale=-1.0)
            keep["s0"] = pick_scales("curp0", "clu0", 128, 8, lrp, [gotu[0], k_lrp])
            keep["c0"] = pick_codes("curp0", "clu0", 128, 8, lrp, [gotu[0], k_lrp])
        a9 = vtt(R("rk")[:, 0:12], T.cnt[:, 0:12], T.hh[:, 15:C:16], A.subtract, [a7])
        send(R("lrk")[:, 0:12], R("rk")[:, 0:12], "gotr%d" % t, t, [a9])
        gotr = ("gotr%d" % t, nin[t])
        if t == 0:
            gotu.append(send_u(kind[1], []))
            k_row0 = pair_rows(1)

        pp = mm("pp", "curp%d" % h, 0, cl, 0, C, [gott, keep["c%d" % h], keep["s%d" % h]])
        if t == 0:
            k_o4 = act(col(5), ccol, F.Identity, scale=-DROP, bias=3 * DROP)
            k_d4 = [act(T.d4[:, b:C:4], T.crow[:, 0:C // 4], F.Identity, [k_dd], scale=0.0, bias=T.dcol[:, 4 + b:5 + b])
                    for b in range(4)]
            k_o4 = [act(col(6 + n), rcol, F.Identity, [k_o4], scale=w, bias=col(5)) for n, w in enumerate((0.25, 1024.0))]
            t1 = vhold(T.hi[:], T.d16[:], T.val0[:, 64:NP], [k_val, k_d16])
            k_own = act(T.own16[:], T.off16[:, 0:K], F.Identity, scale=2.0, bias=-HIGH)
            k_pre = [act(T.pre2[:, 4:18], T.bas[:, 4:18], F.Copy, [k_bas]),
                     act(T.bas[:, 24:33], T.c16[:, 8:17], F.Identity, [k_b], bias=col(9)),
                     act(T.pre2[:, 0:4], T.c16[:, 0:4], F.Identity, bias=qcol),
                     act(T.hp[:, 15:64:16], T.c16[:, 0:4], F.Identity, scale=0.0)]
            z2 = [zeros(1), zeros(4)]
        c5 = act(T.sp[:], T.pp[:, 0:C], F.Copy, [pp])
        if t == 0:
            z2.append(zeros(2))
        c0 = vcp(T.so[:, 0:C].indirect(R("rk")[:, 0:12]), T.crow[:], [a9])
        if t == 0:
            t3 = vts(T.tand[:, 0:14], T.hi[:, 15:224:16], 2, 1023, A.logical_shift_right, A.bitwise_and, after=[t1])
            k_lpj = vts(T.lpj[:, 0:14], T.hi[:, 15:224:16], col(4), 1.0 / 4096.0, A.subtract, A.mult, after=[k_o16])
        c1 = vcount(T.hh[:, 0:K], T.so[:, 0:K], T.pat[:, 0:K], LIFT, [c0])
        c2 = vhold(T.h4[:, 0:K], T.d4[:, 0:K], T.so[:, 0:K], k_d4)
        if t == 0:
            k_lpi = vcp(T.lpi[:, 0:14], T.tand[:, 0:14], [t3])
        c1 = vts(T.rkp[:, 20:24], T.hh[:, 15:K:16], col(1), None, A.add, after=[c1])
        if t == 0:
            qe += [unpack(2), unpack(3)]
        c1 = act(T.ss[:, 0:K], T.sc[:, 0:C].indirect(T.rkp[:, 20:24]), F.Copy, [c1])
        pd = [mm("pw%d" % b, "ce", 128 * b, cl, 0, C, [qe[b]] + read) for b in range(4)]
        c7 = [act(T.dd[:, 0:4 * C:4], T.pw0[:, 0:C], F.Copy, [pd[0]], scale=0.5)]
        c4 = act(T.spi[:, 64:NP], T.ss[:].indirect(T.lpi[:, 0:14]), F.Copy, [c1, k_lpi] + k_acc)
        c7 += [act(T.dd[:, b:4 * C:4], T["pw%d" % b][:, 0:C], F.Copy, [pd[b]], scale=0.5) for b in range(1, 4)]
        if t == 0:
            z2.append(zeros(3))
            need("sync", gotr)
            done("ldw", Y.dma_start(T.cwq[:].bitcast(dt.uint8), T.wc[:]), 16)
            ldw = done("ldw", Y.dma_start(T.cws[:], T.ws[:]), 16)
            ldv = done("ldv", Y.dma_start(T.vb[:], T.v[:]), 16)

        d0 = vcp(T.es[:, 0:C].indirect(R("lrk")[:, 0:12]), T.sp[:], [gotr, c5])
        c3 = vts(R("ol")[:, 0:16], T.h4[:, 3:K:4], col(6), 4.0, A.add, A.mult, after=[c2] + k_o4)
        send(R("lol")[:, 0:16], R("ol")[:, 0:16], "goto%d" % t, t, [c3])
        goto = ("goto%d" % t, nin[t])
        lo, hi = 16 * 7, 16 * 16
        d2 = vts(T.vv[:, 0:K], T.es[:, 0:K], T.ss[:, 0:1], None, A.add, after=[d0, c1])
        d1 = vtt(T.vv[:, 64:NP], T.es[:, 0:C].indirect(T.lpj[:, 0:14]), T.spi[:, 64:NP], A.add, [c4, k_lpj])
        d3 = vfall(0, K, [d2, k_own])
        turn2 = [int(s[1]) for s in ORDER2 if str(s)[0] == "q"]

        def tile2(n, got):
            skip = 0 if t == 0 or n == 3 else FROM2[4 * n] - BASE2[n]
            w = (NP if t == 0 or n == 3 else PAIRS) - BASE2[n] - skip
            o = MOFF2[n] + 4 * skip
            q = vq("cmb", o // 4, w, T.mb[:, o:o + 4 * w], [got[j] for j in range(4 * n, 4 * n + 4)] + z2)
            if n < 3:
                got["pa"] = mm("pa", "cg", 0, "cmb", MOFF2[n] // 4, 128, [q], n == turn2[0], n == turn2[-2])
            return mm("pb", "cg", 0, "cmb", MOFF2[n] // 4 + 160 - BASE2[n], 128, [q], n == turn2[0], n == turn2[-1])

        def numbers(a, b):
            if t == ROUNDS - 1:
                keep["n"] = vcp(T.nout[:, 0:NP].indirect(T.rkp[:, a:b]), T.nrow[:, 16 * a:16 * b], [keep.get("n", k_nrow)])

        put = lambda a, b, after: vcp(T.xs[:, 0:NP].indirect(T.rkp[:, a:b]), T.val0[:, 16 * a:16 * b], after)
        got = counting(ORDER2, T.vv, PAIRS, lambda k: T.hold[:, 16 * k + 15:16 * k + 16],
                       lambda k, got: [d1, d3] if k < 4 else [got["fall" if k < 7 else "hold"]] + z2, FROM2, SUM2, slot2, T.acc2, {
            "fall": lambda got: vfall(K, lo, [d1]),
            "mask": lambda got: vtt(T.sm[:, lo:hi], T.vv[:, lo:hi], T.off16[:, 0:hi - lo], A.add, [d1]),
            "hold": lambda got: vhold(T.hold[:, lo:hi], T.new16[:, 0:hi - lo], T.sm[:, lo:hi], [got["mask"]]),
            "eq": lambda got: vtt(T.eq[:, 0:hi - lo], T.vv[:, lo:hi], T.hold[:, lo:hi], A.is_equal, [got["hold"]]),
            "cor": lambda got: vcount(T.cor[:, 0:hi - lo], T.off16[:, 0:hi - lo], T.eq[:, 0:hi - lo], 0.0, [got["eq"]]),
            "pre": lambda got: vtt(T.pre2[:, 7:16], T.bas[:, 24:33], T.cor[:, 15:hi - lo:16], A.subtract, [got["cor"]] + k_pre),
            "q0": lambda got: tile2(0, got), "q1": lambda got: tile2(1, got), "q2": lambda got: tile2(2, got),
            "q3": lambda got: tile2(3, got),
            "x1": lambda got: vtt(T.cnt[:, 0:12], T.pre2[:, 0:12], T.acc2[:, 0:12], A.add, [got["pre"]] + sums(got, 0, 12)),
            "x2": lambda got: vtt(T.cnt[:, 12:18], T.pre2[:, 12:18], T.acc2[:, 12:18], A.add, [got["pre"]] + sums(got, 12, 16)),
            "s1": lambda got: vcount(T.hp[:, 64:192], T.pa[:, 0:128], T.pat[:], LIFT, [got["pa"]]),
            "s2": lambda got: vcount(T.hp[:, 192:NP], T.pb[:, 32:128], T.pat[:, 0:96], LIFT, [got["q3"]]),
            "n1": lambda got: vtt(T.rkp[:, 0:12], T.cnt[:, 0:12], T.hp[:, 15:192:16], A.subtract, [got["x1"], got["s1"]]),
            "n2": lambda got: vtt(T.rkp[:, 12:18], T.cnt[:, 12:18], T.hp[:, 207:NP:16], A.subtract, [got["x2"], got["s2"]]),
            "put1": lambda got: put(0, 12, [got["n1"], k_row0]),
            "num": lambda got: numbers(0, 2),
            "put2": lambda got: put(12, 18, [got["n2"], got["put1"]])})
        e1 = got["put2"]
        numbers(2, 4)
        if t == 0:
            keep["c1"] = pick_codes("curp1", "clu1", 128, 8, lrp, [gotu[1]])
        if t == 1:
            qv = vq("cv", 0, 128, T.vb[:], [ldv])
        c6 = act(T.aa[:], state[:, 0:4 * C].indirect(R("ol")[:, 0:16]), F.Copy, [c3], scale=0.5)
        e0 = act(T.ee[:], T.dd[:, 0:4 * C].indirect(R("lol")[:, 0:16]), F.Copy, [goto, c7[-1]])
        if t == 0:
            keep["s1"] = pick_scales("curp1", "clu1", 128, 8, lrp, [gotu[1]])

        e2 = vhold(T.hi[:, 0:C], T.d4[:], T.xs[:, 0:C], [e1])
        numbers(4, 6)
        e3 = vts(T.offe[:], T.hi[:, 3:C:4], col(7), 1.0 / 1024.0, A.add, A.mult, after=[e2])
        e5 = vts(T.tand[:], T.hi[:, 3:C:4], 1023, None, A.bitwise_and)
        arrivals = lambda a, b: (T.eg[:, 16 * a:16 * b], T.ee[:, 0:4 * K].indirect(T.offe[:, a:b]))
        f0 = vcp(*arrivals(*ZRUNS[0]), [e3, e0])
        e6 = vts(T.offa[:], T.tand[:], rcol, None, A.add, after=[e5])
        numbers(6, 8)
        zs = []
        for a, b in ZRUNS:
            if zs:
                f0 = act(*arrivals(a, b), F.Copy, [e3, e0])
            zs.append(vtt(T.zz[:, 16 * a:16 * b], T.aa[:, 0:4 * K].indirect(T.offa[:, a:b]), T.eg[:, 16 * a:16 * b], A.add,
                          [e6, f0, c6]))
            if a == 0:
                qz = vq("cz", 0, 128, T.zz[:, 256:768], zs[:-1])
                pw = {n: mm("pw%d" % n, "cw", 128 * n, "cz", 0, 128, [qz, ldw]) for n in (0, 2, 1, 3)}

        numbers(8, 10)
        qz = vq("cz", 128, 128, T.zz[:, 0:512], zs)
        numbers(10, 14)
        banks = ["pa", "pb", "pp", "py"]
        pw2 = [mm(banks[n], "cw", 128 * n, "cz", 128, 128, [qz]) for n in range(4)]
        nxt = "ct%d" % (t + 1)
        r0 = {b: act(T.rr[:, 256 + b:768:4], T["pw%d" % b][:, 0:128], F.Relu, [pw[b]], scale=0.03125) for b in pw}
        r1 = [act(T.rr[:, b:256:4], T[banks[b]][:, 0:64], F.Relu, [pw2[b]], scale=0.03125) for b in range(4)]
        add = lambda a, b, s, after: vtt(T.tt[:, a:b:s], T.rr[:, a:b:s], T.zz[:, a:b:s], A.add, after)
        ts = [add(256, 768, 4, [r0[0]]), add(258, 768, 4, [r0[2]]), add(257, 768, 2, [r0[1], r0[3]]), add(0, 256, 4, r1[:1])]
        rest = lambda: [add(2, 256, 4, r1[:3]), add(1, 256, 2, r1)]
        state = T.tt
        if t < ROUNDS - 1:
            first = vq(nxt, C, 128, T.tt[:, 256:768], ts[:3])
            early = first_scores(nxt, C, [first])
            send_state(t + 1, C, 64, 128, [first])
            ts += rest()
            cp0 = act(T.sc[:, 64:C], T.pw1[:, 0:128], F.Copy, [early[1]])
            a0 = first_mask(early)
        else:
            ts += rest()
            first = vq(nxt, C, 128, T.tt[:, 256:768], ts[:3])
            early = [mm("pw0", "cv", 0, nxt, C, 128, [first, qv])]
        qt = vq(nxt, 0, 128, T.tt[:, 0:512], ts)
        numbers(14, 18)

    ct = "ct%d" % ROUNDS

    def store(q, out, in_, after):
        need(q, after)
        done("stored", queue[q].dma_start(out, in_), 16)

    def store_state(a, b, n, after):
        store("sync", T.oc[:, 4 * b:4 * (b + n)], T[ct + "q"][:, a:a + n].bitcast(dt.uint8), after)
        for k in range(4):
            store("sync", T.osc[4 * k:4 * k + 4, b:b + n], T[ct + "s"][32 * k:32 * k + 4, a:a + n], after)

    py = mm("pw1", "cv", 0, ct, 0, 128, [qt])
    store_state(C, 64, 128, first)
    ya = act(T.ysb[:, 64:C], T.pw0[:, 0:128], F.Copy, early)
    yb = act(T.ysb[:, 0:64], T.pw1[:, 0:64], F.Copy, [py])
    store("act", T.y[:, 64:C], T.ysb[:, 64:C], ya)
    store("act", T.y[:, 0:64], T.ysb[:, 0:64], yb)
    store_state(0, 0, 64, qt)
    store("sync", T.ol[:], T.nout[0:128:16, 0:C], keep["n"])
    need("pool", ("sent", count["sent"]), ("pool", count["pool"]))
    need("sync", ("act", count["act"]), ("pe", count["pe"]), ("stored", count["stored"]))
